import numpy as np
import ml_dtypes


def mxq(x, axis, fmt="e4m3"):
    dtype, down = {"e4m3": (ml_dtypes.float8_e4m3fn, 7), "e5m2": (ml_dtypes.float8_e5m2, 14)}[fmt]
    v = np.moveaxis(np.asarray(x, np.float32).astype(ml_dtypes.bfloat16).astype(np.float64), axis, -1)
    blocks = v.reshape(v.shape[:-1] + (-1, 32))
    amax = np.abs(blocks).max(-1, keepdims=True)
    byte = np.maximum(np.where(amax > 0, np.frexp(amax)[1] - 1 + 127, 0) - down, 1)
    scale = np.exp2(byte - 127.0)
    codes = (blocks / scale).astype(np.float32).astype(dtype).astype(np.float64)
    return np.moveaxis((codes * scale).reshape(v.shape), -1, axis)


WIDE = False


def mx_kscale(k):
    if not WIDE:
        return np.ones(k)
    levels = np.array([10, -10, 5, -5, 0])
    if k % 512:
        return np.exp2(np.random.permutation(np.resize(levels, k // 32))).repeat(32)
    a = np.empty((k // 512, 16))
    for p in range(k // 512):
        a[p, :8] = np.random.permutation(np.resize(levels, 8))
        for g in range(8):
            far = levels[np.abs(levels - a[p, g]) >= 10]
            a[p, g + 8] = far[np.random.randint(len(far))]
    return np.exp2(a.ravel()).repeat(32)


def f64(x):
    return np.asarray(x).astype(np.float64)


def striped(idx):
    return np.tile(idx.reshape(-1, 16).T, (8, 1)).astype(np.uint16)


def unstriped(offs):
    return offs[:16].T.reshape(-1).astype(np.int64)


E2M1 = np.array([0.0, 0.5, 1.0, 1.5, 2.0, 3.0, 4.0, 6.0, -0.0, -0.5, -1.0, -1.5, -2.0, -3.0, -4.0, -6.0])


def pack_weight(w, fmt):
    k, n = w.shape
    w = f64(np.asarray(w, np.float32).astype(ml_dtypes.bfloat16)).reshape(k // 32, 32, n)
    amax = np.abs(w).max(1)
    if fmt == "e4m3":
        byte = np.frexp(amax)[1] - 1 + 127 - 7
    else:
        mant, ex = np.frexp(amax / 6.0)
        byte = np.where(mant > 0.5, ex, ex - 1) + 127
    byte = np.clip(np.where(amax > 0, byte, 1), 1, 254)
    scaled = (w * np.exp2(127.0 - byte)[:, None, :]).reshape(k, n).astype(np.float32)
    by_word = np.ascontiguousarray(scaled.reshape(k // 512, 128, 4, n).transpose(0, 1, 3, 2))
    if fmt == "e4m3":
        words = by_word.astype(ml_dtypes.float8_e4m3fn).view(np.uint8)
    else:
        c = by_word.astype(ml_dtypes.float4_e2m1fn).view(np.uint8) & 0xF
        words = (c[..., 0::2] | (c[..., 1::2] << 4)).reshape(k // 512, 128, 2 * n)
    return np.ascontiguousarray(words), np.ascontiguousarray(byte.astype(np.uint8).reshape(k // 512, 16, n))


def unpack_weight(words, scales, fmt):
    g, _, n = scales.shape
    words = np.ascontiguousarray(words).reshape(g, 128, n, -1)
    if fmt == "e4m3":
        vals = words.view(ml_dtypes.float8_e4m3fn).astype(np.float64)
    else:
        nib = np.empty((g, 128, n, 4), np.uint8)
        nib[..., 0::2] = words & 0xF
        nib[..., 1::2] = words >> 4
        vals = E2M1[nib]
    vals = vals * np.repeat(np.exp2(scales.astype(np.float64) - 127.0), 8, axis=1)[..., None]
    return vals.transpose(0, 1, 3, 2).reshape(g * 512, n)


def gelu(v):
    return 0.5 * v * (1.0 + np.tanh(np.sqrt(2.0 / np.pi) * (v + 0.044715 * v**3)))


def striped8(idx):
    return np.concatenate([v.reshape(-1, 16).T for v in idx]).astype(np.uint16)


def unstriped8(offs):
    return np.stack([offs[16 * g:16 * g + 16].T.reshape(-1) for g in range(8)]).astype(np.int64)


def runs(v, idx8):
    k = np.arange(v.shape[0])
    return v[k[:, None], idx8[k % 512 // 64]]


def put_heads(h, wgs, idx8, t2):
    r = np.arange(h.shape[0])
    page = np.zeros((h.shape[0], t2))
    page[r[:, None], idx8[r % 512 // 64]] = wgs[r // 4 % 128] * h
    return page


K, T, S, H, N, T2 = 1024, 2048, 1024, 1024, 512, 2048

def setup_inputs():
    n = np.random.standard_normal
    s = mx_kscale(K)[:, None]
    u = mx_kscale(H)[:, None]
    tab_words, tab_scales = pack_weight(n((K, T)) * s, "e4m3")
    wa = (n((K, H)) * (0.6 / np.sqrt(K)) / s).astype(np.float32)
    wb_words, wb_scales = pack_weight(n((K, H)) * (0.6 / np.sqrt(K)) / s, "e2m1")
    gain = (np.random.uniform(0.8, 2.4, H) * u[:, 0]).astype(np.float32)
    wc_words, wc_scales = pack_weight(n((H, N)) / np.sqrt(H) / u, "e4m3")
    offs = striped8(np.stack([np.random.permutation(T)[:S] for _ in range(8)]))
    offs2 = striped8(np.stack([np.random.permutation(T2)[:S] for _ in range(8)]))
    wgo = np.repeat(np.random.uniform(0.5, 2.0, (8, S)), 16, axis=0).astype(np.float32)
    return {"tab_words": tab_words, "tab_scales": tab_scales, "offs": offs,
            "wa": wa, "wb_words": wb_words, "wb_scales": wb_scales, "gain": gain,
            "wc_words": wc_words, "wc_scales": wc_scales, "offs2": offs2, "wgo": wgo}

def reference(tab_words, tab_scales, offs, wa, wb_words, wb_scales, gain,
              wc_words, wc_scales, offs2, wgo):
    v = runs(unpack_weight(tab_words, tab_scales, "e4m3"), unstriped8(offs))
    a = np.exp(mxq(f64(wa), 0, "e4m3").T @ v)
    b = np.exp(unpack_weight(wb_words, wb_scales, "e2m1").T @ v)
    h = f64(gain)[:, None] * (a * b / (a + b))
    y = unpack_weight(wc_words, wc_scales, "e4m3").T @ mxq(h, 0, "e4m3")
    out = put_heads(y, f64(wgo), unstriped8(offs2), T2)
    return out

@@ -1,0 +1,299 @@
+from contextlib import ExitStack
+
+import concourse.mybir as mybir
+
+K, T, S, H, N, T2 = 1024, 2048, 1024, 1024, 512, 2048
+FLOPS = 2 * (2 * K * H * S + H * N * S)
+
+F32 = mybir.dt.float32
+BF16 = mybir.dt.bfloat16
+I32 = mybir.dt.int32
+U32 = mybir.dt.uint32
+U16 = mybir.dt.uint16
+U8 = mybir.dt.uint8
+FP8X4 = mybir.dt.float8_e4m3fn_x4
+FP4X4 = mybir.dt.float4_e2m1fn_x4
+ALU = mybir.AluOpType
+ACT = mybir.ActivationFunctionType
+
+P = 128
+PACK = 4
+PASS = P * PACK
+HALF = 512
+CHUNKS = ((0, 256), (256, 256), (512, 512))
+
+
+def tile_list_pen_biomass_cues_kernel(
+    tc, tab_words, tab_scales, offs, wa, wb_words, wb_scales, gain, wc_words, wc_scales, offs2, wgo, out
+):
+    nc = tc.nc
+    with ExitStack() as ctx:
+        lists = ctx.enter_context(tc.tile_pool(name="lists", bufs=1))
+        keep = ctx.enter_context(tc.tile_pool(name="keep", bufs=1))
+        ring = ctx.enter_context(tc.tile_pool(name="ring", bufs=2))
+        psum = ctx.enter_context(tc.psum_pool(name="psum", bufs=4))
+
+        def held(shape, dtype, name, tag=None):
+            return keep.tile(shape, dtype, name=name, tag=tag or name, align_bytes=64)
+
+        offs_sb = lists.tile([P, S // 16], U16, name="offs_sb")
+        offs2_sb = lists.tile([P, S // 16], U16, name="offs2_sb")
+        nc.sync.dma_start(offs_sb[:], offs)
+
+        tab_rows = held([P, T], U8, "tab_rows")
+        wb_rows = held([P, 2, H], U8, "wb_rows")
+        tab_plane = held([P, 2, S], U8, "tab_plane")
+        nc.vector.memset(tab_rows[:].bitcast(I32), 0)
+        nc.vector.memset(wb_rows[:].rearrange("p a c -> p (a c)").bitcast(I32), 0)
+        nc.vector.memset(tab_plane[:].rearrange("p a c -> p (a c)").bitcast(I32), 0)
+        for a in range(2):
+            nc.scalar.dma_start(tab_rows[a:P:8, :].bitcast(I32), tab_scales[a].bitcast(I32))
+        for d in range(4):
+            nc.scalar.dma_start(
+                wb_rows[32 * d : 32 * d + 4, :, :].bitcast(I32),
+                wb_scales[:, 4 * d : 4 * d + 4, :].rearrange("a q c -> q a c").bitcast(I32),
+            )
+
+        wb_raw = held([P, 2, 2 * H], U8, "wb_raw")
+        nc.sync.dma_start(wb_raw[:].bitcast(I32), wb_words.rearrange("a p c -> p a c").bitcast(I32))
+        tab_win = [held([P, T], I32, "tab_win%d" % a) for a in range(2)]
+        for a in range(2):
+            nc.sync.dma_start(tab_win[a][:], tab_words[a].rearrange("p t i -> p (t i)").bitcast(I32))
+        nc.sync.dma_start(offs2_sb[:], offs2)
+
+        picked_rows = held([P, S], U8, "picked_rows")
+        nc.vector.tensor_copy(picked_rows[:], tab_rows[:].indirect(offs_sb[:]))
+        for a in range(2):
+            for r in range(4):
+                nc.scalar.dma_start(
+                    tab_plane[r:P:32, a, :].bitcast(I32), picked_rows[8 * r + a : P : 32, :].bitcast(I32)
+                )
+
+        wb_codes = held([P, 2, 2 * H], U8, "wb_codes")
+        wb_plane = held([P, 2, H], U8, "wb_plane")
+        nc.vector.tensor_copy(
+            wb_codes[:].rearrange("p a c -> p (a c)").bitcast(U16).rearrange("p (g t m) -> p g m t", t=PACK, m=P),
+            wb_raw[:].rearrange("p a c -> p (a c)").bitcast(U16).rearrange("p (g m t) -> p g m t", t=PACK, m=P),
+        )
+        nc.vector.tensor_copy(
+            wb_plane[:].rearrange("p a (b t m) -> p (a b) m t", t=PACK, m=P),
+            wb_rows[:].rearrange("p a (b m t) -> p (a b) m t", t=PACK, m=P),
+        )
+
+        picked = {}
+        for h in range(2):
+            for a in range(2):
+                picked[a, h] = held([P, HALF], U32, "picked%d%d" % (a, h))
+                nc.vector.tensor_copy(
+                    picked[a, h][:], tab_win[a][:].bitcast(U32).indirect(offs_sb[:, 32 * h : 32 * h + 32])
+                )
+
+        wa_raw = {}
+        freed = ("wb_raw", "picked_rows", "tab_win0", "tab_win1")
+        wc_rows = held([P, 2, N], U8, "wc_rows", "wb_rows")
+        nc.vector.memset(wc_rows[:].rearrange("p a c -> p (a c)").bitcast(I32), 0)
+        for b in range(2):
+            for a in range(2):
+                wa_raw[a, b] = held([P, PACK, HALF], F32, "wa_raw%d%d" % (a, b), freed[2 * b + a])
+                nc.sync.dma_start(
+                    wa_raw[a, b][:],
+                    wa[PASS * a : PASS * (a + 1), PASS * b : PASS * (b + 1)].rearrange("(p i) c -> p i c", i=PACK),
+                )
+
+        def table_operand(a, h):
+            return dict(rhs=picked[a, h][:].bitcast(FP8X4), rhs_scale=tab_plane[:, a, HALF * h : HALF * (h + 1)])
+
+        def wb_passes(bank, b, t, h, stop):
+            c0 = PASS * b + P * t
+            for a in range(2):
+                nc.tensor.matmul_mx(
+                    out=bank[:],
+                    lhsT=wb_codes[:, a, 2 * c0 : 2 * (c0 + P)].bitcast(FP4X4),
+                    lhsT_scale=wb_plane[:, a, c0 : c0 + P],
+                    start=(a == 0),
+                    stop=(stop and a == 1),
+                    **table_operand(a, h),
+                )
+
+        wa_codes, wa_plane = {}, {}
+
+        def wa_passes(bank, b, t, h, start):
+            for a in range(2):
+                nc.tensor.matmul_mx(
+                    out=bank[:],
+                    lhsT=wa_codes[a, b][:, P * t : P * (t + 1)].bitcast(FP8X4),
+                    lhsT_scale=wa_plane[a, b][:, P * t : P * (t + 1)],
+                    start=(start and a == 0),
+                    stop=(a == 1),
+                    **table_operand(a, h),
+                )
+
+        direct = (1, 0)
+        exp_b, gate = {}, {}
+        for b, h in ((0, 0), (1, 0), (0, 1), (1, 1)):
+            for t in range(PACK):
+                bank = psum.tile([P, HALF], F32, name="bank_b")
+                wb_passes(bank, b, t, h, True)
+                exp_b[b, t, h] = held([P, HALF], F32, "exp_b%d%d%d" % (b, t, h))
+                gate[b, t, h] = held([P, HALF], F32, "gate%d%d%d" % (b, t, h))
+                nc.scalar.activation(exp_b[b, t, h][:], bank[:], ACT.Exp)
+                if (b, h) != direct:
+                    nc.scalar.copy(gate[b, t, h][:], bank[:])
+
+        def quantise_wa(a, b):
+            grouped = ring.tile([P, PACK, P, PACK], BF16, name="wa_grouped", align_bytes=64)
+            nc.vector.tensor_scalar(
+                out=grouped[:].rearrange("p t m i -> p m t i"),
+                in0=wa_raw[a, b][:].rearrange("p i (m t) -> p m t i", t=PACK),
+                scalar1=-1.0,
+                scalar2=None,
+                op0=ALU.mult,
+            )
+            wa_codes[a, b] = held([P, HALF], U32, "wa_codes%d%d" % (a, b))
+            wa_plane[a, b] = held([P, HALF], U8, "wa_plane%d%d" % (a, b))
+            nc.vector.quantize_mx(
+                out=wa_codes[a, b][:].bitcast(FP8X4),
+                scales=wa_plane[a, b][:],
+                in_=grouped[:].rearrange("p t m i -> p (t m i)"),
+            )
+
+        def difference(b, h):
+            for t in range(PACK):
+                bank = psum.tile([P, HALF], F32, name="bank_a")
+                wa_passes(bank, b, t, h, True)
+                nc.vector.tensor_tensor(gate[b, t, h][:], bank[:], gate[b, t, h][:], ALU.add)
+
+        for b in range(2):
+            for a in range(2):
+                quantise_wa(a, b)
+        wc_raw = held([P, 2, N], I32, "wc_raw", "wb_raw")
+        nc.sync.dma_start(wc_raw[:], wc_words.rearrange("a p c i -> p a (c i)").bitcast(I32))
+        for d in range(4):
+            nc.sync.dma_start(
+                wc_rows[32 * d : 32 * d + 4, :, :].bitcast(I32),
+                wc_scales[:, 4 * d : 4 * d + 4, :].rearrange("a q c -> q a c").bitcast(I32),
+            )
+        gain_sb = held([P, 2, PACK], F32, "gain_sb", "tab_win0")
+        nc.sync.dma_start(gain_sb[:], gain.rearrange("(b p t) -> p b t", b=2, t=PACK))
+        wgo_sb = held([P, S], F32, "wgo_sb", "picked_rows")
+        nc.sync.dma_start(wgo_sb[:], wgo)
+
+        difference(0, 0)
+        direct_bank = []
+        for t in range(PACK):
+            bank = psum.tile([P, HALF], F32, name="bank_b")
+            wb_passes(bank, direct[0], t, direct[1], False)
+            wa_passes(bank, direct[0], t, direct[1], False)
+            direct_bank.append(bank)
+
+        wc_codes = held([P, 2, N], I32, "wc_codes")
+        wc_plane = held([P, 2, N], U8, "wc_plane")
+        nc.vector.tensor_copy(
+            wc_codes[:].rearrange("p a (t m) -> p a m t", t=PACK),
+            wc_raw[:].rearrange("p a (m t) -> p a m t", t=PACK),
+        )
+        nc.vector.tensor_copy(
+            wc_plane[:].rearrange("p a (t m) -> p a m t", t=PACK),
+            wc_rows[:].rearrange("p a (m t) -> p a m t", t=PACK),
+        )
+        cells = [held([P, T2], F32, "cells%d" % i) for i in range(PACK)]
+        for i in range(PACK):
+            nc.vector.memset(cells[i][:], 0.0)
+
+        def products(c):
+            j0, width = CHUNKS[c]
+            h = j0 // HALF
+            cols = slice(j0 - HALF * h, j0 - HALF * h + width)
+            rows = []
+            for b in range(2):
+                h_rows = ring.tile([P, PACK, width], BF16, name="h_rows", bufs=3)
+                for t in range(PACK):
+                    source = direct_bank[t] if (b, h) == direct else gate[b, t, h]
+                    nc.scalar.activation(gate[b, t, h][:, cols], source[:, cols], ACT.Sigmoid, scale=-1.0)
+                    nc.vector.scalar_tensor_tensor(
+                        out=h_rows[:, t, :],
+                        in0=exp_b[b, t, h][:, cols],
+                        scalar=gain_sb[:, b, t : t + 1],
+                        in1=gate[b, t, h][:, cols],
+                        op0=ALU.mult,
+                        op1=ALU.mult,
+                    )
+                rows.append(h_rows)
+            return rows
+
+        def quantise_h(c, rows, copy):
+            width = CHUNKS[c][1]
+            operands = []
+            for b in range(2):
+                h_grouped = held([P, width, PACK], BF16, "h_grouped%d%d" % (c, b))
+                copy(
+                    h_grouped[:].rearrange("p (c i) t -> p c t i", i=4),
+                    rows[b][:].rearrange("p t (c i) -> p c t i", i=4),
+                )
+                codes = held([P, width], U32, "h_codes%d%d" % (c, b))
+                plane = held([P, width], U8, "h_plane%d%d" % (c, b))
+                nc.vector.quantize_mx(
+                    out=codes[:].bitcast(FP8X4), scales=plane[:], in_=h_grouped[:].rearrange("p c t -> p (c t)")
+                )
+                operands.append((codes, plane))
+            return operands
+
+        def mix(c, operands, tag):
+            width = CHUNKS[c][1]
+            per_bank = HALF // width
+            banks = []
+            for i0 in range(0, PACK, per_bank):
+                bank = psum.tile([P, per_bank, width], F32, name=tag)
+                for i in range(i0, i0 + per_bank):
+                    for b in range(2):
+                        nc.tensor.matmul_mx(
+                            out=bank[:, i - i0, :],
+                            lhsT=wc_codes[:, b, P * i : P * (i + 1)].bitcast(FP8X4),
+                            lhsT_scale=wc_plane[:, b, P * i : P * (i + 1)],
+                            rhs=operands[b][0][:].bitcast(FP8X4),
+                            rhs_scale=operands[b][1][:],
+                            start=(b == 0),
+                            stop=(b == 1),
+                        )
+                banks.append(bank)
+            return banks
+
+        y_sb = {}
+
+        def evacuate(c, k, bank, tag=None):
+            width = CHUNKS[c][1]
+            y_sb[c, k] = held([P, HALF // width, width], F32, "y_sb%d%d" % (c, k), tag)
+            nc.scalar.copy(y_sb[c, k][:], bank[:])
+
+        def scatter(c, k):
+            j0, width = CHUNKS[c]
+            per_bank = HALF // width
+            for u in range(per_bank):
+                nc.vector.tensor_tensor(
+                    cells[k * per_bank + u][:].indirect(offs2_sb[:, j0 // 16 : (j0 + width) // 16]),
+                    y_sb[c, k][:, u, :],
+                    wgo_sb[:, j0 : j0 + width],
+                    ALU.mult,
+                )
+
+        rows0 = products(0)
+        banks0 = mix(0, quantise_h(0, rows0, nc.vector.tensor_copy), "bank_a")
+        for k in range(2):
+            evacuate(0, k, banks0[k])
+        difference(0, 1)
+        difference(1, 1)
+        banks1 = mix(1, quantise_h(1, products(1), nc.scalar.copy), "bank_a")
+        rows2 = products(2)
+        evacuate(1, 0, banks1[0], "gate131")
+        operands2 = quantise_h(2, rows2, nc.scalar.copy)
+        evacuate(1, 1, banks1[1], "h_grouped21")
+        banks2 = mix(2, operands2, "bank_b")
+        for k in range(4):
+            evacuate(2, k, banks2[k], "exp_b0%d0" % k)
+        for c in range(3):
+            for k in range(4 * CHUNKS[c][1] // HALF):
+                scatter(c, k)
+
+        out_rows = out.rearrange("(p i) t -> i p t", i=PACK)
+        for i in range(PACK):
+            nc.sync.dma_start(out_rows[i], cells[i][:])

@@ -39,17 +39,22 @@ def tile_list_pen_biomass_cues_kernel(
         offs_sb = lists.tile([P, S // 16], U16, name="offs_sb")
         offs2_sb = lists.tile([P, S // 16], U16, name="offs2_sb")
         nc.sync.dma_start(offs_sb[:], offs)
+        nc.sync.dma_start(offs2_sb[:], offs2)
 
         tab_rows = held([P, T], U8, "tab_rows")
         wb_rows = held([P, 2, H], U8, "wb_rows")
         tab_plane = held([P, 2, S], U8, "tab_plane")
-        nc.vector.memset(tab_rows[:].bitcast(I32), 0)
+        warm_in = held([P, 2], F32, "warm_in", "tab_win0")
+        warm_out = held([P, 2], F32, "warm_out", "tab_win1")
+        nc.gpsimd.memset(warm_in[:], 0.0)
+        nc.scalar.activation(warm_out[:], warm_in[:], ACT.Exp)
+        nc.gpsimd.memset(tab_rows[:].bitcast(I32), 0)
         nc.vector.memset(wb_rows[:].rearrange("p a c -> p (a c)").bitcast(I32), 0)
         nc.vector.memset(tab_plane[:].rearrange("p a c -> p (a c)").bitcast(I32), 0)
         for a in range(2):
-            nc.scalar.dma_start(tab_rows[a:P:8, :].bitcast(I32), tab_scales[a].bitcast(I32))
+            nc.sync.dma_start(tab_rows[a:P:8, :].bitcast(I32), tab_scales[a].bitcast(I32))
         for d in range(4):
-            nc.scalar.dma_start(
+            nc.sync.dma_start(
                 wb_rows[32 * d : 32 * d + 4, :, :].bitcast(I32),
                 wb_scales[:, 4 * d : 4 * d + 4, :].rearrange("a q c -> q a c").bitcast(I32),
             )
@@ -59,7 +64,6 @@ def tile_list_pen_biomass_cues_kernel(
         tab_win = [held([P, T], I32, "tab_win%d" % a) for a in range(2)]
         for a in range(2):
             nc.sync.dma_start(tab_win[a][:], tab_words[a].rearrange("p t i -> p (t i)").bitcast(I32))
-        nc.sync.dma_start(offs2_sb[:], offs2)
 
         picked_rows = held([P, S], U8, "picked_rows")
         nc.vector.tensor_copy(picked_rows[:], tab_rows[:].indirect(offs_sb[:]))
@@ -91,7 +95,7 @@ def tile_list_pen_biomass_cues_kernel(
         wa_raw = {}
         freed = ("wb_raw", "picked_rows", "tab_win0", "tab_win1")
         wc_rows = held([P, 2, N], U8, "wc_rows", "wb_rows")
-        nc.vector.memset(wc_rows[:].rearrange("p a c -> p (a c)").bitcast(I32), 0)
+        nc.gpsimd.memset(wc_rows[:].rearrange("p a c -> p (a c)").bitcast(I32), 0)
         for b in range(2):
             for a in range(2):
                 wa_raw[a, b] = held([P, PACK, HALF], F32, "wa_raw%d%d" % (a, b), freed[2 * b + a])
@@ -105,26 +109,26 @@ def tile_list_pen_biomass_cues_kernel(
 
         def wb_passes(bank, b, t, h, stop):
             c0 = PASS * b + P * t
-            for a in range(2):
+            for a in (1, 0):
                 nc.tensor.matmul_mx(
                     out=bank[:],
                     lhsT=wb_codes[:, a, 2 * c0 : 2 * (c0 + P)].bitcast(FP4X4),
                     lhsT_scale=wb_plane[:, a, c0 : c0 + P],
-                    start=(a == 0),
-                    stop=(stop and a == 1),
+                    start=(a == 1),
+                    stop=(stop and a == 0),
                     **table_operand(a, h),
                 )
 
         wa_codes, wa_plane = {}, {}
 
         def wa_passes(bank, b, t, h, start):
-            for a in range(2):
+            for a in (1, 0):
                 nc.tensor.matmul_mx(
                     out=bank[:],
                     lhsT=wa_codes[a, b][:, P * t : P * (t + 1)].bitcast(FP8X4),
                     lhsT_scale=wa_plane[a, b][:, P * t : P * (t + 1)],
-                    start=(start and a == 0),
-                    stop=(a == 1),
+                    start=(start and a == 1),
+                    stop=(a == 0),
                     **table_operand(a, h),
                 )
 
@@ -141,7 +145,7 @@ def tile_list_pen_biomass_cues_kernel(
                     nc.scalar.copy(gate[b, t, h][:], bank[:])
 
         def quantise_wa(a, b):
-            grouped = ring.tile([P, PACK, P, PACK], BF16, name="wa_grouped", align_bytes=64)
+            grouped = held([P, PACK, P, PACK], BF16, "wa_grouped%d%d" % (a, b), "wa_grouped%d" % a)
             nc.vector.tensor_scalar(
                 out=grouped[:].rearrange("p t m i -> p m t i"),
                 in0=wa_raw[a, b][:].rearrange("p i (m t) -> p m t i", t=PACK),
@@ -196,9 +200,11 @@ def tile_list_pen_biomass_cues_kernel(
             wc_plane[:].rearrange("p a (t m) -> p a m t", t=PACK),
             wc_rows[:].rearrange("p a (m t) -> p a m t", t=PACK),
         )
-        cells = [held([P, T2], F32, "cells%d" % i) for i in range(PACK)]
+        cell_tags = (None, None, "tab_win1", "wa_grouped1")
+        cells = [held([P, T2], F32, "cells%d" % i, cell_tags[i]) for i in range(PACK)]
         for i in range(PACK):
-            nc.vector.memset(cells[i][:], 0.0)
+            for c0 in range(0, T2, HALF):
+                nc.gpsimd.memset(cells[i][:, c0 : c0 + HALF].bitcast(I32), 0)
 
         def products(c):
             j0, width = CHUNKS[c]

@@ -49,8 +49,8 @@ def tile_list_pen_biomass_cues_kernel(
         nc.gpsimd.memset(warm_in[:], 0.0)
         nc.scalar.activation(warm_out[:], warm_in[:], ACT.Exp)
         nc.gpsimd.memset(tab_rows[:].bitcast(I32), 0)
-        nc.vector.memset(wb_rows[:].rearrange("p a c -> p (a c)").bitcast(I32), 0)
-        nc.vector.memset(tab_plane[:].rearrange("p a c -> p (a c)").bitcast(I32), 0)
+        nc.gpsimd.memset(wb_rows[:].rearrange("p a c -> p (a c)").bitcast(I32), 0)
+        nc.gpsimd.memset(tab_plane[:, 1, :].bitcast(I32), 0)
         for a in range(2):
             nc.sync.dma_start(tab_rows[a:P:8, :].bitcast(I32), tab_scales[a].bitcast(I32))
         for d in range(4):
@@ -67,8 +67,9 @@ def tile_list_pen_biomass_cues_kernel(
 
         picked_rows = held([P, S], U8, "picked_rows")
         nc.vector.tensor_copy(picked_rows[:], tab_rows[:].indirect(offs_sb[:]))
-        for a in range(2):
-            for r in range(4):
+        nc.vector.tensor_copy(tab_plane[:, 0, :].bitcast(I32), picked_rows[:].bitcast(I32))
+        for a in (1, 0):
+            for r in range(1 - a, 4):
                 nc.scalar.dma_start(
                     tab_plane[r:P:32, a, :].bitcast(I32), picked_rows[8 * r + a : P : 32, :].bitcast(I32)
                 )
@@ -93,9 +94,7 @@ def tile_list_pen_biomass_cues_kernel(
                 )
 
         wa_raw = {}
-        freed = ("wb_raw", "picked_rows", "tab_win0", "tab_win1")
-        wc_rows = held([P, 2, N], U8, "wc_rows", "wb_rows")
-        nc.gpsimd.memset(wc_rows[:].rearrange("p a c -> p (a c)").bitcast(I32), 0)
+        freed = ("tab_rows", "wb_raw", "wb_rows", "picked_rows")
         for b in range(2):
             for a in range(2):
                 wa_raw[a, b] = held([P, PACK, HALF], F32, "wa_raw%d%d" % (a, b), freed[2 * b + a])
@@ -141,7 +140,9 @@ def tile_list_pen_biomass_cues_kernel(
                 exp_b[b, t, h] = held([P, HALF], F32, "exp_b%d%d%d" % (b, t, h))
                 gate[b, t, h] = held([P, HALF], F32, "gate%d%d%d" % (b, t, h))
                 nc.scalar.activation(exp_b[b, t, h][:], bank[:], ACT.Exp)
-                if (b, h) != direct:
+                if (b, h) == (1, 1) and t > 0:
+                    nc.vector.tensor_copy(gate[b, t, h][:], bank[:])
+                elif (b, h) != direct:
                     nc.scalar.copy(gate[b, t, h][:], bank[:])
 
         def quantise_wa(a, b):
@@ -170,16 +171,18 @@ def tile_list_pen_biomass_cues_kernel(
         for b in range(2):
             for a in range(2):
                 quantise_wa(a, b)
-        wc_raw = held([P, 2, N], I32, "wc_raw", "wb_raw")
+        wc_rows = held([P, 2, N], U8, "wc_rows", "tab_rows")
+        nc.gpsimd.memset(wc_rows[:].rearrange("p a c -> p (a c)").bitcast(I32), 0)
+        wc_raw = held([P, 2, N], I32, "wc_raw", "tab_win0")
         nc.sync.dma_start(wc_raw[:], wc_words.rearrange("a p c i -> p a (c i)").bitcast(I32))
         for d in range(4):
             nc.sync.dma_start(
                 wc_rows[32 * d : 32 * d + 4, :, :].bitcast(I32),
                 wc_scales[:, 4 * d : 4 * d + 4, :].rearrange("a q c -> q a c").bitcast(I32),
             )
-        gain_sb = held([P, 2, PACK], F32, "gain_sb", "tab_win0")
+        gain_sb = held([P, 2, PACK], F32, "gain_sb", "wb_raw")
         nc.sync.dma_start(gain_sb[:], gain.rearrange("(b p t) -> p b t", b=2, t=PACK))
-        wgo_sb = held([P, S], F32, "wgo_sb", "picked_rows")
+        wgo_sb = held([P, S], F32, "wgo_sb", "wb_rows")
         nc.sync.dma_start(wgo_sb[:], wgo)
 
         difference(0, 0)
@@ -200,8 +203,7 @@ def tile_list_pen_biomass_cues_kernel(
             wc_plane[:].rearrange("p a (t m) -> p a m t", t=PACK),
             wc_rows[:].rearrange("p a (m t) -> p a m t", t=PACK),
         )
-        cell_tags = (None, None, "tab_win1", "wa_grouped1")
-        cells = [held([P, T2], F32, "cells%d" % i, cell_tags[i]) for i in range(PACK)]
+        cells = [held([P, T2], F32, "cells%d" % i) for i in range(PACK)]
         for i in range(PACK):
             for c0 in range(0, T2, HALF):
                 nc.gpsimd.memset(cells[i][:, c0 : c0 + HALF].bitcast(I32), 0)
@@ -212,7 +214,7 @@ def tile_list_pen_biomass_cues_kernel(
             cols = slice(j0 - HALF * h, j0 - HALF * h + width)
             rows = []
             for b in range(2):
-                h_rows = ring.tile([P, PACK, width], BF16, name="h_rows", bufs=3)
+                h_rows = held([P, PACK, width], BF16, "h_rows%d%d" % (c, b))
                 for t in range(PACK):
                     source = direct_bank[t] if (b, h) == direct else gate[b, t, h]
                     nc.scalar.activation(gate[b, t, h][:, cols], source[:, cols], ACT.Sigmoid, scale=-1.0)
@@ -290,9 +292,9 @@ def tile_list_pen_biomass_cues_kernel(
         difference(1, 1)
         banks1 = mix(1, quantise_h(1, products(1), nc.scalar.copy), "bank_a")
         rows2 = products(2)
-        evacuate(1, 0, banks1[0], "gate131")
+        evacuate(1, 0, banks1[0], "gate121")
         operands2 = quantise_h(2, rows2, nc.scalar.copy)
-        evacuate(1, 1, banks1[1], "h_grouped21")
+        evacuate(1, 1, banks1[1], "h_rows21")
         banks2 = mix(2, operands2, "bank_b")
         for k in range(4):
             evacuate(2, k, banks2[k], "exp_b0%d0" % k)

@@ -20,7 +20,9 @@ P = 128
 PACK = 4
 PASS = P * PACK
 HALF = 512
-CHUNKS = ((0, 256), (256, 256), (512, 512))
+CHUNK = 256
+BANK = 2048
+SLOT = 8192
 
 
 def tile_list_pen_biomass_cues_kernel(
@@ -30,95 +32,115 @@ def tile_list_pen_biomass_cues_kernel(
     with ExitStack() as ctx:
         lists = ctx.enter_context(tc.tile_pool(name="lists", bufs=1))
         keep = ctx.enter_context(tc.tile_pool(name="keep", bufs=1))
-        ring = ctx.enter_context(tc.tile_pool(name="ring", bufs=2))
-        psum = ctx.enter_context(tc.psum_pool(name="psum", bufs=4))
+        shared = ctx.enter_context(tc.tile_pool(name="shared", bufs=1))
+        psum = ctx.enter_context(tc.psum_pool(name="psum", bufs=1))
 
-        def held(shape, dtype, name, tag=None):
-            return keep.tile(shape, dtype, name=name, tag=tag or name, align_bytes=64)
+        def held(shape, dtype, name):
+            return keep.tile(shape, dtype, name=name, align_bytes=64)
+
+        def placed(shape, dtype, name, slot, at=0):
+            return shared.tile(shape, dtype, name=name, align_bytes=64, offset=SLOT * slot + at)
+
+        def bank_tile(shape, name, bank):
+            return psum.tile(shape, F32, name=name, offset=BANK * bank)
 
         offs_sb = lists.tile([P, S // 16], U16, name="offs_sb")
         offs2_sb = lists.tile([P, S // 16], U16, name="offs2_sb")
         nc.sync.dma_start(offs_sb[:], offs)
-        nc.sync.dma_start(offs2_sb[:], offs2)
 
         tab_rows = held([P, T], U8, "tab_rows")
-        wb_rows = held([P, 2, H], U8, "wb_rows")
+        wb_rows = placed([P, 2, H], U8, "wb_rows", 2)
         tab_plane = held([P, 2, S], U8, "tab_plane")
-        warm_in = held([P, 2], F32, "warm_in", "tab_win0")
-        warm_out = held([P, 2], F32, "warm_out", "tab_win1")
-        nc.gpsimd.memset(warm_in[:], 0.0)
-        nc.scalar.activation(warm_out[:], warm_in[:], ACT.Exp)
-        nc.gpsimd.memset(tab_rows[:].bitcast(I32), 0)
-        nc.gpsimd.memset(wb_rows[:].rearrange("p a c -> p (a c)").bitcast(I32), 0)
-        nc.gpsimd.memset(tab_plane[:, 1, :].bitcast(I32), 0)
         for a in range(2):
-            nc.sync.dma_start(tab_rows[a:P:8, :].bitcast(I32), tab_scales[a].bitcast(I32))
-        for d in range(4):
             nc.sync.dma_start(
+                tab_rows[a:P:2, :].bitcast(I32),
+                tab_scales[a].bitcast(I32).unsqueeze(1).broadcast_to([16, 4, T // 4]),
+            )
+        nc.vector.memset(wb_rows[:].rearrange("p a c -> p (a c)").bitcast(I32), 0)
+        for d in range(4):
+            nc.scalar.dma_start(
                 wb_rows[32 * d : 32 * d + 4, :, :].bitcast(I32),
                 wb_scales[:, 4 * d : 4 * d + 4, :].rearrange("a q c -> q a c").bitcast(I32),
             )
 
-        wb_raw = held([P, 2, 2 * H], U8, "wb_raw")
-        nc.sync.dma_start(wb_raw[:].bitcast(I32), wb_words.rearrange("a p c -> p a c").bitcast(I32))
-        tab_win = [held([P, T], I32, "tab_win%d" % a) for a in range(2)]
-        for a in range(2):
+        tab_win = {}
+        wb_raw = placed([P, 2, 2 * H], U8, "wb_raw", 3)
+        wa_raw = {}
+
+        def load_table(a):
+            tab_win[a] = placed([P, T], I32, "tab_win%d" % a, a)
             nc.sync.dma_start(tab_win[a][:], tab_words[a].rearrange("p t i -> p (t i)").bitcast(I32))
 
-        picked_rows = held([P, S], U8, "picked_rows")
+        def load_wa(a, b):
+            wa_raw[a, b] = placed([P, PACK, HALF], F32, "wa_raw%d%d" % (a, b), 2 + 2 * b + a)
+            nc.sync.dma_start(
+                wa_raw[a, b][:],
+                wa[PASS * a : PASS * (a + 1), PASS * b : PASS * (b + 1)].rearrange("(p i) c -> p i c", i=PACK),
+            )
+
+        load_table(1)
+        nc.sync.dma_start(wb_raw[:].bitcast(I32), wb_words.rearrange("a p c -> p a c").bitcast(I32))
+        load_table(0)
+        nc.sync.dma_start(offs2_sb[:], offs2)
+
+        cells = [held([P, T2], F32, "cells%d" % i) for i in range(1)]
+        for i in range(1):
+            nc.vector.memset(cells[i][:].bitcast(I32), 0)
+
+        picked_rows = placed([P, S], U8, "picked_rows", 5, -512)
         nc.vector.tensor_copy(picked_rows[:], tab_rows[:].indirect(offs_sb[:]))
-        nc.vector.tensor_copy(tab_plane[:, 0, :].bitcast(I32), picked_rows[:].bitcast(I32))
+        picked = {}
+
+        def gather_words(a, h):
+            picked[a, h] = held([P, HALF], U32, "picked%d%d" % (a, h))
+            nc.vector.tensor_copy(
+                picked[a, h][:], tab_win[a][:].bitcast(U32).indirect(offs_sb[:, 32 * h : 32 * h + 32])
+            )
+
+        nc.vector.tensor_copy(
+            tab_plane[:].bitcast(I32), picked_rows[:].bitcast(I32).unsqueeze(1).broadcast_to([P, 2, S // 4])
+        )
         for a in (1, 0):
             for r in range(1 - a, 4):
                 nc.scalar.dma_start(
                     tab_plane[r:P:32, a, :].bitcast(I32), picked_rows[8 * r + a : P : 32, :].bitcast(I32)
                 )
 
+        gather_words(1, 0)
         wb_codes = held([P, 2, 2 * H], U8, "wb_codes")
         wb_plane = held([P, 2, H], U8, "wb_plane")
-        nc.vector.tensor_copy(
-            wb_codes[:].rearrange("p a c -> p (a c)").bitcast(U16).rearrange("p (g t m) -> p g m t", t=PACK, m=P),
-            wb_raw[:].rearrange("p a c -> p (a c)").bitcast(U16).rearrange("p (g m t) -> p g m t", t=PACK, m=P),
-        )
         nc.vector.tensor_copy(
             wb_plane[:].rearrange("p a (b t m) -> p (a b) m t", t=PACK, m=P),
             wb_rows[:].rearrange("p a (b m t) -> p (a b) m t", t=PACK, m=P),
         )
-
-        picked = {}
-        for h in range(2):
-            for a in range(2):
-                picked[a, h] = held([P, HALF], U32, "picked%d%d" % (a, h))
-                nc.vector.tensor_copy(
-                    picked[a, h][:], tab_win[a][:].bitcast(U32).indirect(offs_sb[:, 32 * h : 32 * h + 32])
-                )
-
-        wa_raw = {}
-        freed = ("tab_rows", "wb_raw", "wb_rows", "picked_rows")
-        for b in range(2):
-            for a in range(2):
-                wa_raw[a, b] = held([P, PACK, HALF], F32, "wa_raw%d%d" % (a, b), freed[2 * b + a])
-                nc.sync.dma_start(
-                    wa_raw[a, b][:],
-                    wa[PASS * a : PASS * (a + 1), PASS * b : PASS * (b + 1)].rearrange("(p i) c -> p i c", i=PACK),
-                )
+        nc.vector.tensor_copy(
+            wb_codes[:].rearrange("p a c -> p (a c)").bitcast(U16).rearrange("p (g t m) -> p g m t", t=PACK, m=P),
+            wb_raw[:].rearrange("p a c -> p (a c)").bitcast(U16).rearrange("p (g m t) -> p g m t", t=PACK, m=P),
+        )
+        gather_words(0, 0)
+        gather_words(1, 1)
+        gather_words(0, 1)
+        load_wa(0, 0)
+        load_wa(1, 0)
+        load_wa(0, 1)
+        load_wa(1, 1)
 
         def table_operand(a, h):
             return dict(rhs=picked[a, h][:].bitcast(FP8X4), rhs_scale=tab_plane[:, a, HALF * h : HALF * (h + 1)])
 
         def wb_passes(bank, b, t, h, stop):
             c0 = PASS * b + P * t
-            for a in (1, 0):
+            for a in range(2):
                 nc.tensor.matmul_mx(
                     out=bank[:],
                     lhsT=wb_codes[:, a, 2 * c0 : 2 * (c0 + P)].bitcast(FP4X4),
                     lhsT_scale=wb_plane[:, a, c0 : c0 + P],
-                    start=(a == 1),
-                    stop=(stop and a == 0),
+                    start=(a == 0),
+                    stop=(stop and a == 1),
                     **table_operand(a, h),
                 )
 
-        wa_codes, wa_plane = {}, {}
+        wa_grouped, wa_codes, wa_plane = {}, {}, {}
 
         def wa_passes(bank, b, t, h, start):
             for a in (1, 0):
@@ -131,176 +153,235 @@ def tile_list_pen_biomass_cues_kernel(
                     **table_operand(a, h),
                 )
 
-        direct = (1, 0)
-        exp_b, gate = {}, {}
-        for b, h in ((0, 0), (1, 0), (0, 1), (1, 1)):
-            for t in range(PACK):
-                bank = psum.tile([P, HALF], F32, name="bank_b")
-                wb_passes(bank, b, t, h, True)
-                exp_b[b, t, h] = held([P, HALF], F32, "exp_b%d%d%d" % (b, t, h))
-                gate[b, t, h] = held([P, HALF], F32, "gate%d%d%d" % (b, t, h))
-                nc.scalar.activation(exp_b[b, t, h][:], bank[:], ACT.Exp)
-                if (b, h) == (1, 1) and t > 0:
-                    nc.vector.tensor_copy(gate[b, t, h][:], bank[:])
-                elif (b, h) != direct:
-                    nc.scalar.copy(gate[b, t, h][:], bank[:])
+        def round_views(a, b):
+            if b == 1:
+                wa_grouped[a, b] = placed([P, PACK, P, PACK], BF16, "wa_grouped%d1" % a, 8 - 2 * a)
+            else:
+                wa_grouped[a, b] = held([P, PACK, P, PACK], BF16, "wa_grouped%d%d" % (a, b))
+            return (
+                wa_grouped[a, b][:].rearrange("p t m i -> p m t i"),
+                wa_raw[a, b][:].rearrange("p i (m t) -> p m t i", t=PACK),
+            )
+
+        def round_wa(a, b):
+            grouped, raw = round_views(a, b)
+            nc.vector.tensor_scalar(out=grouped, in0=raw, scalar1=-1.0, scalar2=None, op0=ALU.mult)
 
         def quantise_wa(a, b):
-            grouped = held([P, PACK, P, PACK], BF16, "wa_grouped%d%d" % (a, b), "wa_grouped%d" % a)
-            nc.vector.tensor_scalar(
-                out=grouped[:].rearrange("p t m i -> p m t i"),
-                in0=wa_raw[a, b][:].rearrange("p i (m t) -> p m t i", t=PACK),
-                scalar1=-1.0,
-                scalar2=None,
-                op0=ALU.mult,
-            )
             wa_codes[a, b] = held([P, HALF], U32, "wa_codes%d%d" % (a, b))
             wa_plane[a, b] = held([P, HALF], U8, "wa_plane%d%d" % (a, b))
             nc.vector.quantize_mx(
                 out=wa_codes[a, b][:].bitcast(FP8X4),
                 scales=wa_plane[a, b][:],
-                in_=grouped[:].rearrange("p t m i -> p (t m i)"),
+                in_=wa_grouped[a, b][:].rearrange("p t m i -> p (t m i)"),
             )
 
-        def difference(b, h):
-            for t in range(PACK):
-                bank = psum.tile([P, HALF], F32, name="bank_a")
-                wa_passes(bank, b, t, h, True)
-                nc.vector.tensor_tensor(gate[b, t, h][:], bank[:], gate[b, t, h][:], ALU.add)
+        exp_b, b_sb, gate = {}, {}, {}
 
-        for b in range(2):
-            for a in range(2):
-                quantise_wa(a, b)
-        wc_rows = held([P, 2, N], U8, "wc_rows", "tab_rows")
-        nc.gpsimd.memset(wc_rows[:].rearrange("p a c -> p (a c)").bitcast(I32), 0)
-        wc_raw = held([P, 2, N], I32, "wc_raw", "tab_win0")
+        def exponentials(b, h):
+            for t in range(PACK):
+                bank = bank_tile([P, HALF], "bank_b%d%d%d" % (b, t, h), t)
+                wb_passes(bank, b, t, h, True)
+                if (b, h) == (0, 1):
+                    exp_b[b, t, h] = placed([P, HALF], F32, "exp_b%d%d%d" % (b, t, h), 4, BANK * t)
+                    b_sb[b, t, h] = placed([P, HALF], F32, "b_sb%d%d%d" % (b, t, h), 3, BANK * t)
+                else:
+                    exp_b[b, t, h] = held([P, HALF], F32, "exp_b%d%d%d" % (b, t, h))
+                nc.scalar.activation(exp_b[b, t, h][:], bank[:], ACT.Exp)
+                if h == 0:
+                    if b == 0:
+                        b_sb[b, t, h] = placed([P, HALF], F32, "b_sb%d%d%d" % (b, t, h), 7, BANK * t)
+                    else:
+                        b_sb[b, t, h] = held([P, HALF], F32, "b_sb%d%d%d" % (b, t, h))
+                    gate[b, t, h] = b_sb[b, t, h]
+                if (b, h) != (1, 1):
+                    nc.scalar.copy(b_sb[b, t, h][:], bank[:])
+
+        def difference(b, h, first_bank):
+            for t in range(PACK):
+                bank = bank_tile([P, HALF], "bank_a%d%d%d" % (b, t, h), first_bank + t)
+                wa_passes(bank, b, t, h, True)
+                if h == 1:
+                    gate[b, t, h] = placed([P, HALF], F32, "gate%d%d%d" % (b, t, h), 7, BANK * t)
+                nc.vector.tensor_tensor(gate[b, t, h][:], bank[:], b_sb[b, t, h][:], ALU.add)
+
+        exponentials(0, 0)
+        exponentials(1, 0)
+        exponentials(1, 1)
+
+        round_wa(0, 0)
+        round_wa(1, 0)
+        quantise_wa(0, 0)
+        round_wa(0, 1)
+        quantise_wa(1, 0)
+        round_wa(1, 1)
+        quantise_wa(0, 1)
+        difference(0, 0, 4)
+        quantise_wa(1, 1)
+
+        wc_raw = placed([P, 2, N], I32, "wc_raw", 1)
+        wgo_sb = placed([P, S], F32, "wgo_sb", 1, 4096)
+        wc_rows = placed([P, N], U8, "wc_rows", 0)
+        gain_sb = placed([P, 2, PACK], F32, "gain_sb", 0, 1024)
+        nc.gpsimd.memset(wc_rows[:].bitcast(I32), 0)
         nc.sync.dma_start(wc_raw[:], wc_words.rearrange("a p c i -> p a (c i)").bitcast(I32))
         for d in range(4):
             nc.sync.dma_start(
-                wc_rows[32 * d : 32 * d + 4, :, :].bitcast(I32),
-                wc_scales[:, 4 * d : 4 * d + 4, :].rearrange("a q c -> q a c").bitcast(I32),
+                wc_rows[32 * d : 32 * d + 8, :].bitcast(I32), wc_scales[:, 4 * d : 4 * d + 4, :].bitcast(I32)
             )
-        gain_sb = held([P, 2, PACK], F32, "gain_sb", "wb_raw")
         nc.sync.dma_start(gain_sb[:], gain.rearrange("(b p t) -> p b t", b=2, t=PACK))
-        wgo_sb = held([P, S], F32, "wgo_sb", "wb_rows")
         nc.sync.dma_start(wgo_sb[:], wgo)
 
-        difference(0, 0)
-        direct_bank = []
-        for t in range(PACK):
-            bank = psum.tile([P, HALF], F32, name="bank_b")
-            wb_passes(bank, direct[0], t, direct[1], False)
-            wa_passes(bank, direct[0], t, direct[1], False)
-            direct_bank.append(bank)
+        cells.append(placed([P, T2], F32, "cells1", 8))
+        cells.append(placed([P, T2], F32, "cells2", 5))
+        cells.append(placed([P, T2], F32, "cells3", 6))
+        for i in range(1, PACK):
+            for c0 in range(0, T2, HALF):
+                nc.gpsimd.memset(cells[i][:, c0 : c0 + HALF].bitcast(I32), 0)
+
+        difference(1, 0, 4)
 
         wc_codes = held([P, 2, N], I32, "wc_codes")
-        wc_plane = held([P, 2, N], U8, "wc_plane")
+        wc_plane = held([P, N], U8, "wc_plane")
         nc.vector.tensor_copy(
             wc_codes[:].rearrange("p a (t m) -> p a m t", t=PACK),
             wc_raw[:].rearrange("p a (m t) -> p a m t", t=PACK),
         )
         nc.vector.tensor_copy(
-            wc_plane[:].rearrange("p a (t m) -> p a m t", t=PACK),
-            wc_rows[:].rearrange("p a (m t) -> p a m t", t=PACK),
+            wc_plane[:].rearrange("p (t m) -> p m t", t=PACK),
+            wc_rows[:].rearrange("p (m t) -> p m t", t=PACK),
         )
-        cells = [held([P, T2], F32, "cells%d" % i) for i in range(PACK)]
-        for i in range(PACK):
-            for c0 in range(0, T2, HALF):
-                nc.gpsimd.memset(cells[i][:, c0 : c0 + HALF].bitcast(I32), 0)
 
-        def products(c):
-            j0, width = CHUNKS[c]
-            h = j0 // HALF
-            cols = slice(j0 - HALF * h, j0 - HALF * h + width)
-            rows = []
-            for b in range(2):
-                h_rows = held([P, PACK, width], BF16, "h_rows%d%d" % (c, b))
-                for t in range(PACK):
-                    source = direct_bank[t] if (b, h) == direct else gate[b, t, h]
-                    nc.scalar.activation(gate[b, t, h][:, cols], source[:, cols], ACT.Sigmoid, scale=-1.0)
-                    nc.vector.scalar_tensor_tensor(
-                        out=h_rows[:, t, :],
-                        in0=exp_b[b, t, h][:, cols],
-                        scalar=gain_sb[:, b, t : t + 1],
-                        in1=gate[b, t, h][:, cols],
-                        op0=ALU.mult,
-                        op1=ALU.mult,
-                    )
-                rows.append(h_rows)
-            return rows
+        h_rows, operands, y_bank, y_sb = {}, {}, {}, {}
+        y_last = held([P, 2, HALF], F32, "y_last")
 
-        def quantise_h(c, rows, copy):
-            width = CHUNKS[c][1]
-            operands = []
-            for b in range(2):
-                h_grouped = held([P, width, PACK], BF16, "h_grouped%d%d" % (c, b))
-                copy(
-                    h_grouped[:].rearrange("p (c i) t -> p c t i", i=4),
-                    rows[b][:].rearrange("p t (c i) -> p c t i", i=4),
+        def columns(c):
+            return slice(CHUNK * (c % 2), CHUNK * (c % 2 + 1))
+
+        def sigmoids(c, b):
+            for t in range(PACK):
+                view = gate[b, t, c // 2][:, columns(c)]
+                nc.scalar.activation(view, view, ACT.Sigmoid, scale=-1.0)
+
+        def products(c, b):
+            if (c, b) == (3, 0):
+                h_rows[c, b] = placed([P, PACK, CHUNK], BF16, "h_rows30", 0, 2048)
+            else:
+                h_rows[c, b] = held([P, PACK, CHUNK], BF16, "h_rows%d%d" % (c, b))
+            for t in range(PACK):
+                nc.vector.scalar_tensor_tensor(
+                    out=h_rows[c, b][:, t, :],
+                    in0=exp_b[b, t, c // 2][:, columns(c)],
+                    scalar=gain_sb[:, b, t : t + 1],
+                    in1=gate[b, t, c // 2][:, columns(c)],
+                    op0=ALU.mult,
+                    op1=ALU.mult,
                 )
-                codes = held([P, width], U32, "h_codes%d%d" % (c, b))
-                plane = held([P, width], U8, "h_plane%d%d" % (c, b))
-                nc.vector.quantize_mx(
-                    out=codes[:].bitcast(FP8X4), scales=plane[:], in_=h_grouped[:].rearrange("p c t -> p (c t)")
-                )
-                operands.append((codes, plane))
-            return operands
 
-        def mix(c, operands, tag):
-            width = CHUNKS[c][1]
-            per_bank = HALF // width
-            banks = []
-            for i0 in range(0, PACK, per_bank):
-                bank = psum.tile([P, per_bank, width], F32, name=tag)
-                for i in range(i0, i0 + per_bank):
-                    for b in range(2):
+        def quantise_h(c, b):
+            h_grouped = held([P, CHUNK, PACK], BF16, "h_grouped%d%d" % (c, b))
+            nc.scalar.copy(
+                h_grouped[:].rearrange("p (c i) t -> p c t i", i=4),
+                h_rows[c, b][:].rearrange("p t (c i) -> p c t i", i=4),
+            )
+            codes = held([P, CHUNK], U32, "h_codes%d%d" % (c, b))
+            plane = held([P, CHUNK], U8, "h_plane%d%d" % (c, b))
+            nc.vector.quantize_mx(
+                out=codes[:].bitcast(FP8X4), scales=plane[:], in_=h_grouped[:].rearrange("p c t -> p (c t)")
+            )
+            operands[c, b] = (codes, plane)
+
+        def mix(c, order):
+            for k in range(2):
+                y_bank[c, k] = bank_tile([P, 2, CHUNK], "bank_y%d%d" % (c, k), (4, 0, 4, 6)[c] + k)
+                for u in range(2):
+                    i = 2 * k + u
+                    for b in order:
                         nc.tensor.matmul_mx(
-                            out=bank[:, i - i0, :],
+                            out=y_bank[c, k][:, u, :],
                             lhsT=wc_codes[:, b, P * i : P * (i + 1)].bitcast(FP8X4),
-                            lhsT_scale=wc_plane[:, b, P * i : P * (i + 1)],
-                            rhs=operands[b][0][:].bitcast(FP8X4),
-                            rhs_scale=operands[b][1][:],
-                            start=(b == 0),
-                            stop=(b == 1),
+                            lhsT_scale=wc_plane[4 * b : P, P * i : P * (i + 1)],
+                            rhs=operands[c, b][0][:].bitcast(FP8X4),
+                            rhs_scale=operands[c, b][1][:],
+                            start=(b == order[0]),
+                            stop=(b == order[1]),
                         )
-                banks.append(bank)
-            return banks
 
-        y_sb = {}
+        def evacuate(c, k):
+            if c >= 2 and k == 1:
+                nc.scalar.copy(y_last[:, :, columns(c)], y_bank[c, k][:])
+                return
+            y_sb[c, k] = held([P, 2, CHUNK], F32, "y_sb%d%d" % (c, k))
+            nc.scalar.copy(y_sb[c, k][:], y_bank[c, k][:])
 
-        def evacuate(c, k, bank, tag=None):
-            width = CHUNKS[c][1]
-            y_sb[c, k] = held([P, HALF // width, width], F32, "y_sb%d%d" % (c, k), tag)
-            nc.scalar.copy(y_sb[c, k][:], bank[:])
+        def late_scatter(u, slot, at):
+            y_late = placed([P, CHUNK], F32, "y_late%d" % u, slot, at)
+            nc.scalar.copy(y_late[:], y_bank[1, 1][:, u, :])
+            nc.vector.tensor_tensor(
+                cells[2 + u][:].indirect(offs2_sb[:, CHUNK // 16 : HALF // 16]), y_late[:], wgo_sb[:, CHUNK:HALF], ALU.mult
+            )
 
         def scatter(c, k):
-            j0, width = CHUNKS[c]
-            per_bank = HALF // width
-            for u in range(per_bank):
+            for u in range(2):
                 nc.vector.tensor_tensor(
-                    cells[k * per_bank + u][:].indirect(offs2_sb[:, j0 // 16 : (j0 + width) // 16]),
+                    cells[2 * k + u][:].indirect(offs2_sb[:, CHUNK * c // 16 : CHUNK * (c + 1) // 16]),
                     y_sb[c, k][:, u, :],
-                    wgo_sb[:, j0 : j0 + width],
+                    wgo_sb[:, CHUNK * c : CHUNK * (c + 1)],
                     ALU.mult,
                 )
 
-        rows0 = products(0)
-        banks0 = mix(0, quantise_h(0, rows0, nc.vector.tensor_copy), "bank_a")
-        for k in range(2):
-            evacuate(0, k, banks0[k])
-        difference(0, 1)
-        difference(1, 1)
-        banks1 = mix(1, quantise_h(1, products(1), nc.scalar.copy), "bank_a")
-        rows2 = products(2)
-        evacuate(1, 0, banks1[0], "gate121")
-        operands2 = quantise_h(2, rows2, nc.scalar.copy)
-        evacuate(1, 1, banks1[1], "h_rows21")
-        banks2 = mix(2, operands2, "bank_b")
-        for k in range(4):
-            evacuate(2, k, banks2[k], "exp_b0%d0" % k)
-        for c in range(3):
-            for k in range(4 * CHUNKS[c][1] // HALF):
-                scatter(c, k)
+        for b in range(2):
+            sigmoids(0, b)
+            products(0, b)
+        for b in range(2):
+            quantise_h(0, b)
+        mix(0, (1, 0))
+        for b in range(2):
+            sigmoids(1, b)
+            products(1, b)
+        evacuate(0, 0)
+        evacuate(0, 1)
+        for b in range(2):
+            quantise_h(1, b)
+
+        for t in range(PACK):
+            bank = bank_tile([P, HALF], "bank_d%d" % t, t)
+            wb_passes(bank, 1, t, 1, False)
+            wa_passes(bank, 1, t, 1, False)
+            gate[1, t, 1] = placed([P, HALF], F32, "gate1%d1" % t, 2, BANK * t)
+            nc.scalar.activation(gate[1, t, 1][:], bank[:], ACT.Sigmoid, scale=-1.0)
+
+        scatter(0, 0)
+        scatter(0, 1)
+        exponentials(0, 1)
+        for c in (2, 3):
+            products(c, 1)
+        difference(0, 1, 0)
+        mix(1, (1, 0))
+        evacuate(1, 0)
+        scatter(1, 0)
+        for c in (2, 3):
+            quantise_h(c, 1)
+        sigmoids(2, 0)
+        products(2, 0)
+        sigmoids(3, 0)
+        products(3, 0)
+        late_scatter(0, 4, BANK * 3)
+        quantise_h(2, 0)
+        mix(2, (0, 1))
+        quantise_h(3, 0)
+        late_scatter(1, 0, 2048)
+        evacuate(2, 0)
+        mix(3, (0, 1))
+        evacuate(3, 0)
+        evacuate(2, 1)
+        evacuate(3, 1)
+        for c in (2, 3):
+            scatter(c, 0)
+        for u in range(2):
+            nc.vector.tensor_tensor(
+                cells[2 + u][:].indirect(offs2_sb[:, HALF // 16 : S // 16]), y_last[:, u, :], wgo_sb[:, HALF:S], ALU.mult
+            )
 
         out_rows = out.rearrange("(p i) t -> i p t", i=PACK)
         for i in range(PACK):

@@ -23,6 +23,7 @@ HALF = 512
 CHUNK = 256
 BANK = 2048
 SLOT = 8192
+ON_VECTOR = ((0, 0), (0, 1), (2, 0), (3, 0))
 
 
 def tile_list_pen_biomass_cues_kernel(
@@ -47,24 +48,20 @@ def tile_list_pen_biomass_cues_kernel(
         offs_sb = lists.tile([P, S // 16], U16, name="offs_sb")
         offs2_sb = lists.tile([P, S // 16], U16, name="offs2_sb")
         nc.sync.dma_start(offs_sb[:], offs)
+        nc.sync.dma_start(offs2_sb[:], offs2)
 
-        tab_rows = held([P, T], U8, "tab_rows")
-        wb_rows = placed([P, 2, H], U8, "wb_rows", 2)
+        tab_rows = placed([P, T], U8, "tab_rows", 3, -1024)
+        wb_rows = placed([P, 2, H], U8, "wb_rows", 5, -1024)
         tab_plane = held([P, 2, S], U8, "tab_plane")
         for a in range(2):
             nc.sync.dma_start(
                 tab_rows[a:P:2, :].bitcast(I32),
                 tab_scales[a].bitcast(I32).unsqueeze(1).broadcast_to([16, 4, T // 4]),
             )
-        nc.vector.memset(wb_rows[:].rearrange("p a c -> p (a c)").bitcast(I32), 0)
-        for d in range(4):
-            nc.scalar.dma_start(
-                wb_rows[32 * d : 32 * d + 4, :, :].bitcast(I32),
-                wb_scales[:, 4 * d : 4 * d + 4, :].rearrange("a q c -> q a c").bitcast(I32),
-            )
+        nc.gpsimd.memset(wb_rows[:].rearrange("p a c -> p (a c)").bitcast(I32), 0)
 
         tab_win = {}
-        wb_raw = placed([P, 2, 2 * H], U8, "wb_raw", 3)
+        wb_raw = placed([P, 2, 2 * H], U8, "wb_raw", 9)
         wa_raw = {}
 
         def load_table(a):
@@ -79,45 +76,57 @@ def tile_list_pen_biomass_cues_kernel(
             )
 
         load_table(1)
-        nc.sync.dma_start(wb_raw[:].bitcast(I32), wb_words.rearrange("a p c -> p a c").bitcast(I32))
+        for d in range(4):
+            nc.sync.dma_start(
+                wb_rows[32 * d : 32 * d + 4, :, :].bitcast(I32),
+                wb_scales[:, 4 * d : 4 * d + 4, :].rearrange("a q c -> q a c").bitcast(I32),
+            )
         load_table(0)
-        nc.sync.dma_start(offs2_sb[:], offs2)
+        nc.sync.dma_start(wb_raw[:].bitcast(I32), wb_words.rearrange("a p c -> p a c").bitcast(I32))
 
+        nc.vector.memset(tab_plane[:, 1, :].bitcast(I32), 0)
         cells = [held([P, T2], F32, "cells%d" % i) for i in range(1)]
         for i in range(1):
             nc.vector.memset(cells[i][:].bitcast(I32), 0)
 
-        picked_rows = placed([P, S], U8, "picked_rows", 5, -512)
+        picked_rows = held([P, S], U8, "picked_rows")
         nc.vector.tensor_copy(picked_rows[:], tab_rows[:].indirect(offs_sb[:]))
         picked = {}
 
         def gather_words(a, h):
-            picked[a, h] = held([P, HALF], U32, "picked%d%d" % (a, h))
+            if h == 0:
+                picked[a, h] = held([P, HALF], U32, "picked%d%d" % (a, h))
+            else:
+                picked[a, h] = placed([P, HALF], U32, "picked%d%d" % (a, h), 9, BANK * a)
             nc.vector.tensor_copy(
                 picked[a, h][:], tab_win[a][:].bitcast(U32).indirect(offs_sb[:, 32 * h : 32 * h + 32])
             )
 
-        nc.vector.tensor_copy(
-            tab_plane[:].bitcast(I32), picked_rows[:].bitcast(I32).unsqueeze(1).broadcast_to([P, 2, S // 4])
-        )
+        nc.vector.tensor_copy(tab_plane[:, 0, :].bitcast(I32), picked_rows[:].bitcast(I32))
         for a in (1, 0):
             for r in range(1 - a, 4):
-                nc.scalar.dma_start(
+                nc.sync.dma_start(
                     tab_plane[r:P:32, a, :].bitcast(I32), picked_rows[8 * r + a : P : 32, :].bitcast(I32)
                 )
 
         gather_words(1, 0)
-        wb_codes = held([P, 2, 2 * H], U8, "wb_codes")
-        wb_plane = held([P, 2, H], U8, "wb_plane")
-        nc.vector.tensor_copy(
-            wb_plane[:].rearrange("p a (b t m) -> p (a b) m t", t=PACK, m=P),
-            wb_rows[:].rearrange("p a (b m t) -> p (a b) m t", t=PACK, m=P),
-        )
-        nc.vector.tensor_copy(
-            wb_codes[:].rearrange("p a c -> p (a c)").bitcast(U16).rearrange("p (g t m) -> p g m t", t=PACK, m=P),
-            wb_raw[:].rearrange("p a c -> p (a c)").bitcast(U16).rearrange("p (g m t) -> p g m t", t=PACK, m=P),
-        )
+        wb_codes = [held([P, 2, 2 * PASS], U8, "wb_codes%d" % b) for b in range(2)]
+        wb_plane = [held([P, 2, PASS], U8, "wb_plane%d" % b) for b in range(2)]
+
+        def deal_wb(b):
+            cols = slice(PASS * b, PASS * (b + 1))
+            nc.vector.tensor_copy(
+                wb_plane[b][:].rearrange("p a (t m) -> p a m t", t=PACK),
+                wb_rows[:, :, cols].rearrange("p a (m t) -> p a m t", t=PACK),
+            )
+            nc.vector.tensor_copy(
+                wb_codes[b][:].bitcast(U16).rearrange("p a (t m) -> p a m t", t=PACK),
+                wb_raw[:].bitcast(U16)[:, :, cols].rearrange("p a (m t) -> p a m t", t=PACK),
+            )
+
         gather_words(0, 0)
+        deal_wb(0)
+        deal_wb(1)
         gather_words(1, 1)
         gather_words(0, 1)
         load_wa(0, 0)
@@ -129,12 +138,12 @@ def tile_list_pen_biomass_cues_kernel(
             return dict(rhs=picked[a, h][:].bitcast(FP8X4), rhs_scale=tab_plane[:, a, HALF * h : HALF * (h + 1)])
 
         def wb_passes(bank, b, t, h, stop):
-            c0 = PASS * b + P * t
+            c0 = P * t
             for a in range(2):
                 nc.tensor.matmul_mx(
                     out=bank[:],
-                    lhsT=wb_codes[:, a, 2 * c0 : 2 * (c0 + P)].bitcast(FP4X4),
-                    lhsT_scale=wb_plane[:, a, c0 : c0 + P],
+                    lhsT=wb_codes[b][:, a, 2 * c0 : 2 * (c0 + P)].bitcast(FP4X4),
+                    lhsT_scale=wb_plane[b][:, a, c0 : c0 + P],
                     start=(a == 0),
                     stop=(stop and a == 1),
                     **table_operand(a, h),
@@ -278,12 +287,20 @@ def tile_list_pen_biomass_cues_kernel(
                     op1=ALU.mult,
                 )
 
-        def quantise_h(c, b):
-            h_grouped = held([P, CHUNK, PACK], BF16, "h_grouped%d%d" % (c, b))
-            nc.scalar.copy(
-                h_grouped[:].rearrange("p (c i) t -> p c t i", i=4),
+        h_groups = {}
+
+        def interleave(c, b):
+            h_groups[c, b] = held([P, CHUNK, PACK], BF16, "h_grouped%d%d" % (c, b))
+            copy = nc.vector.tensor_copy if (c, b) in ON_VECTOR else nc.scalar.copy
+            copy(
+                h_groups[c, b][:].rearrange("p (c i) t -> p c t i", i=4),
                 h_rows[c, b][:].rearrange("p t (c i) -> p c t i", i=4),
             )
+
+        def quantise_h(c, b):
+            if (c, b) not in h_groups:
+                interleave(c, b)
+            h_grouped = h_groups[c, b]
             codes = held([P, CHUNK], U32, "h_codes%d%d" % (c, b))
             plane = held([P, CHUNK], U8, "h_plane%d%d" % (c, b))
             nc.vector.quantize_mx(
@@ -334,6 +351,8 @@ def tile_list_pen_biomass_cues_kernel(
             sigmoids(0, b)
             products(0, b)
         for b in range(2):
+            interleave(0, b)
+        for b in range(2):
             quantise_h(0, b)
         mix(0, (1, 0))
         for b in range(2):
@@ -366,10 +385,12 @@ def tile_list_pen_biomass_cues_kernel(
         products(2, 0)
         sigmoids(3, 0)
         products(3, 0)
-        late_scatter(0, 4, BANK * 3)
+        interleave(2, 0)
+        interleave(3, 0)
         quantise_h(2, 0)
         mix(2, (0, 1))
         quantise_h(3, 0)
+        late_scatter(0, 4, BANK * 3)
         late_scatter(1, 0, 2048)
         evacuate(2, 0)
         mix(3, (0, 1))

@@ -23,7 +23,7 @@ HALF = 512
 CHUNK = 256
 BANK = 2048
 SLOT = 8192
-ON_VECTOR = ((0, 0), (0, 1), (2, 0), (3, 0))
+ON_VECTOR = ()
 
 
 def tile_list_pen_biomass_cues_kernel(
@@ -50,18 +50,19 @@ def tile_list_pen_biomass_cues_kernel(
         nc.sync.dma_start(offs_sb[:], offs)
         nc.sync.dma_start(offs2_sb[:], offs2)
 
-        tab_rows = placed([P, T], U8, "tab_rows", 3, -1024)
-        wb_rows = placed([P, 2, H], U8, "wb_rows", 5, -1024)
+        tab_rows = held([P, T], U8, "tab_rows")
+        wb_rows = placed([P, 2, H], U8, "wb_rows", 5)
         tab_plane = held([P, 2, S], U8, "tab_plane")
         for a in range(2):
-            nc.sync.dma_start(
-                tab_rows[a:P:2, :].bitcast(I32),
-                tab_scales[a].bitcast(I32).unsqueeze(1).broadcast_to([16, 4, T // 4]),
-            )
+            for e in range(2):
+                nc.sync.dma_start(
+                    tab_rows[2 * a + e : P : 4, :].bitcast(I32),
+                    tab_scales[a, e:16:2, :].bitcast(I32).unsqueeze(1).broadcast_to([8, 4, T // 4]),
+                )
         nc.gpsimd.memset(wb_rows[:].rearrange("p a c -> p (a c)").bitcast(I32), 0)
 
         tab_win = {}
-        wb_raw = placed([P, 2, 2 * H], U8, "wb_raw", 9)
+        wb_raw = [placed([P, 2, 2 * PASS], U8, "wb_raw0", 4, -1024), held([P, 2, 2 * PASS], U8, "wb_raw1")]
         wa_raw = {}
 
         def load_table(a):
@@ -81,15 +82,24 @@ def tile_list_pen_biomass_cues_kernel(
                 wb_rows[32 * d : 32 * d + 4, :, :].bitcast(I32),
                 wb_scales[:, 4 * d : 4 * d + 4, :].rearrange("a q c -> q a c").bitcast(I32),
             )
+
+        def load_wb(b):
+            nc.sync.dma_start(
+                wb_raw[b][:].bitcast(I32),
+                wb_words[:, :, 2 * PASS * b : 2 * PASS * (b + 1)].rearrange("a p c -> p a c").bitcast(I32),
+            )
+
+        load_wb(0)
+        load_wa(0, 0)
         load_table(0)
-        nc.sync.dma_start(wb_raw[:].bitcast(I32), wb_words.rearrange("a p c -> p a c").bitcast(I32))
+        load_wb(1)
 
         nc.vector.memset(tab_plane[:, 1, :].bitcast(I32), 0)
-        cells = [held([P, T2], F32, "cells%d" % i) for i in range(1)]
-        for i in range(1):
+        cells = [held([P, T2], F32, "cells%d" % i) for i in range(PACK)]
+        for i in range(PACK):
             nc.vector.memset(cells[i][:].bitcast(I32), 0)
 
-        picked_rows = held([P, S], U8, "picked_rows")
+        picked_rows = placed([P, S], U8, "picked_rows", 8, 1536)
         nc.vector.tensor_copy(picked_rows[:], tab_rows[:].indirect(offs_sb[:]))
         picked = {}
 
@@ -97,16 +107,17 @@ def tile_list_pen_biomass_cues_kernel(
             if h == 0:
                 picked[a, h] = held([P, HALF], U32, "picked%d%d" % (a, h))
             else:
-                picked[a, h] = placed([P, HALF], U32, "picked%d%d" % (a, h), 9, BANK * a)
+                picked[a, h] = placed([P, HALF], U32, "picked%d%d" % (a, h), 8, BANK * a)
             nc.vector.tensor_copy(
                 picked[a, h][:], tab_win[a][:].bitcast(U32).indirect(offs_sb[:, 32 * h : 32 * h + 32])
             )
 
         nc.vector.tensor_copy(tab_plane[:, 0, :].bitcast(I32), picked_rows[:].bitcast(I32))
         for a in (1, 0):
-            for r in range(1 - a, 4):
+            for r in range(2 - 2 * a, 4):
                 nc.sync.dma_start(
-                    tab_plane[r:P:32, a, :].bitcast(I32), picked_rows[8 * r + a : P : 32, :].bitcast(I32)
+                    tab_plane[r:P:32, a, :].bitcast(I32),
+                    picked_rows[16 * (r // 2) + 2 * a + r % 2 : P : 32, :].bitcast(I32),
                 )
 
         gather_words(1, 0)
@@ -116,20 +127,19 @@ def tile_list_pen_biomass_cues_kernel(
         def deal_wb(b):
             cols = slice(PASS * b, PASS * (b + 1))
             nc.vector.tensor_copy(
+                wb_codes[b][:].bitcast(U16).rearrange("p a (t m) -> p a m t", t=PACK),
+                wb_raw[b][:].bitcast(U16).rearrange("p a (m t) -> p a m t", t=PACK),
+            )
+            nc.vector.tensor_copy(
                 wb_plane[b][:].rearrange("p a (t m) -> p a m t", t=PACK),
                 wb_rows[:, :, cols].rearrange("p a (m t) -> p a m t", t=PACK),
             )
-            nc.vector.tensor_copy(
-                wb_codes[b][:].bitcast(U16).rearrange("p a (t m) -> p a m t", t=PACK),
-                wb_raw[:].bitcast(U16)[:, :, cols].rearrange("p a (m t) -> p a m t", t=PACK),
-            )
 
-        gather_words(0, 0)
         deal_wb(0)
+        gather_words(0, 0)
         deal_wb(1)
         gather_words(1, 1)
         gather_words(0, 1)
-        load_wa(0, 0)
         load_wa(1, 0)
         load_wa(0, 1)
         load_wa(1, 1)
@@ -164,7 +174,7 @@ def tile_list_pen_biomass_cues_kernel(
 
         def round_views(a, b):
             if b == 1:
-                wa_grouped[a, b] = placed([P, PACK, P, PACK], BF16, "wa_grouped%d1" % a, 8 - 2 * a)
+                wa_grouped[a, b] = placed([P, PACK, P, PACK], BF16, "wa_grouped%d1" % a, 6, 4096 * a)
             else:
                 wa_grouped[a, b] = held([P, PACK, P, PACK], BF16, "wa_grouped%d%d" % (a, b))
             return (
@@ -184,6 +194,9 @@ def tile_list_pen_biomass_cues_kernel(
                 scales=wa_plane[a, b][:],
                 in_=wa_grouped[a, b][:].rearrange("p t m i -> p (t m i)"),
             )
+
+        first_grouped, first_raw = round_views(0, 0)
+        nc.scalar.activation(first_grouped, first_raw, ACT.Copy, scale=-1.0)
 
         exp_b, b_sb, gate = {}, {}, {}
 
@@ -218,21 +231,20 @@ def tile_list_pen_biomass_cues_kernel(
         exponentials(1, 0)
         exponentials(1, 1)
 
-        round_wa(0, 0)
-        round_wa(1, 0)
         quantise_wa(0, 0)
+        round_wa(1, 0)
         round_wa(0, 1)
         quantise_wa(1, 0)
         round_wa(1, 1)
         quantise_wa(0, 1)
-        difference(0, 0, 4)
         quantise_wa(1, 1)
+        difference(0, 0, 4)
 
         wc_raw = placed([P, 2, N], I32, "wc_raw", 1)
         wgo_sb = placed([P, S], F32, "wgo_sb", 1, 4096)
         wc_rows = placed([P, N], U8, "wc_rows", 0)
         gain_sb = placed([P, 2, PACK], F32, "gain_sb", 0, 1024)
-        nc.gpsimd.memset(wc_rows[:].bitcast(I32), 0)
+        nc.vector.memset(wc_rows[:].bitcast(I32), 0)
         nc.sync.dma_start(wc_raw[:], wc_words.rearrange("a p c i -> p a (c i)").bitcast(I32))
         for d in range(4):
             nc.sync.dma_start(
@@ -240,13 +252,6 @@ def tile_list_pen_biomass_cues_kernel(
             )
         nc.sync.dma_start(gain_sb[:], gain.rearrange("(b p t) -> p b t", b=2, t=PACK))
         nc.sync.dma_start(wgo_sb[:], wgo)
-
-        cells.append(placed([P, T2], F32, "cells1", 8))
-        cells.append(placed([P, T2], F32, "cells2", 5))
-        cells.append(placed([P, T2], F32, "cells3", 6))
-        for i in range(1, PACK):
-            for c0 in range(0, T2, HALF):
-                nc.gpsimd.memset(cells[i][:, c0 : c0 + HALF].bitcast(I32), 0)
 
         difference(1, 0, 4)
 

@@ -21,9 +21,14 @@ PACK = 4
 PASS = P * PACK
 HALF = 512
 CHUNK = 256
+LIST = 16
 BANK = 2048
-SLOT = 8192
-ON_VECTOR = ()
+SLOT = 4 * BANK
+
+TABLE_0, TABLE_1, WA_00, WA_10, WA_01, WA_11, LATE_WORDS, FIRST_H = range(8)
+LOW_BANKS, HIGH_BANKS = 0, 4
+
+ON_VECTOR = ((0, 0), (0, 1), (2, 0), (3, 0))
 
 
 def tile_list_pen_biomass_cues_kernel(
@@ -33,44 +38,50 @@ def tile_list_pen_biomass_cues_kernel(
     with ExitStack() as ctx:
         lists = ctx.enter_context(tc.tile_pool(name="lists", bufs=1))
         keep = ctx.enter_context(tc.tile_pool(name="keep", bufs=1))
-        shared = ctx.enter_context(tc.tile_pool(name="shared", bufs=1))
+        reused = ctx.enter_context(tc.tile_pool(name="reused", bufs=1))
         psum = ctx.enter_context(tc.psum_pool(name="psum", bufs=1))
 
         def held(shape, dtype, name):
             return keep.tile(shape, dtype, name=name, align_bytes=64)
 
         def placed(shape, dtype, name, slot, at=0):
-            return shared.tile(shape, dtype, name=name, align_bytes=64, offset=SLOT * slot + at)
+            return reused.tile(shape, dtype, name=name, align_bytes=64, offset=SLOT * slot + at)
 
-        def bank_tile(shape, name, bank):
+        def in_bank(shape, name, bank):
             return psum.tile(shape, F32, name=name, offset=BANK * bank)
 
-        offs_sb = lists.tile([P, S // 16], U16, name="offs_sb")
-        offs2_sb = lists.tile([P, S // 16], U16, name="offs2_sb")
+        offs_sb = lists.tile([P, S // LIST], U16, name="offs_sb")
+        offs2_sb = lists.tile([P, S // LIST], U16, name="offs2_sb")
         nc.sync.dma_start(offs_sb[:], offs)
         nc.sync.dma_start(offs2_sb[:], offs2)
 
         tab_rows = held([P, T], U8, "tab_rows")
-        wb_rows = placed([P, 2, H], U8, "wb_rows", 5)
-        tab_plane = held([P, 2, S], U8, "tab_plane")
         for a in range(2):
             for e in range(2):
                 nc.sync.dma_start(
                     tab_rows[2 * a + e : P : 4, :].bitcast(I32),
                     tab_scales[a, e:16:2, :].bitcast(I32).unsqueeze(1).broadcast_to([8, 4, T // 4]),
                 )
+
+        wb_rows = placed([P, 2, H], U8, "wb_rows", WA_11)
+        tab_plane = held([P, 2, S], U8, "tab_plane")
         nc.gpsimd.memset(wb_rows[:].rearrange("p a c -> p (a c)").bitcast(I32), 0)
 
-        tab_win = {}
-        wb_raw = [placed([P, 2, 2 * PASS], U8, "wb_raw0", 4, -1024), held([P, 2, 2 * PASS], U8, "wb_raw1")]
-        wa_raw = {}
+        tab_win, wb_raw, wa_raw = {}, {}, {}
 
         def load_table(a):
-            tab_win[a] = placed([P, T], I32, "tab_win%d" % a, a)
+            tab_win[a] = placed([P, T], I32, "tab_win%d" % a, TABLE_0 + a)
             nc.sync.dma_start(tab_win[a][:], tab_words[a].rearrange("p t i -> p (t i)").bitcast(I32))
 
+        def load_wb(b, tile):
+            wb_raw[b] = tile
+            nc.sync.dma_start(
+                tile[:].bitcast(I32),
+                wb_words[:, :, 2 * PASS * b : 2 * PASS * (b + 1)].rearrange("a p c -> p a c").bitcast(I32),
+            )
+
         def load_wa(a, b):
-            wa_raw[a, b] = placed([P, PACK, HALF], F32, "wa_raw%d%d" % (a, b), 2 + 2 * b + a)
+            wa_raw[a, b] = placed([P, PACK, HALF], F32, "wa_raw%d%d" % (a, b), WA_00 + 2 * b + a)
             nc.sync.dma_start(
                 wa_raw[a, b][:],
                 wa[PASS * a : PASS * (a + 1), PASS * b : PASS * (b + 1)].rearrange("(p i) c -> p i c", i=PACK),
@@ -82,59 +93,51 @@ def tile_list_pen_biomass_cues_kernel(
                 wb_rows[32 * d : 32 * d + 4, :, :].bitcast(I32),
                 wb_scales[:, 4 * d : 4 * d + 4, :].rearrange("a q c -> q a c").bitcast(I32),
             )
-
-        def load_wb(b):
-            nc.sync.dma_start(
-                wb_raw[b][:].bitcast(I32),
-                wb_words[:, :, 2 * PASS * b : 2 * PASS * (b + 1)].rearrange("a p c -> p a c").bitcast(I32),
-            )
-
-        load_wb(0)
+        load_wb(0, placed([P, 2, 2 * PASS], U8, "wb_raw0", WA_01, -PASS * 2))
         load_wa(0, 0)
         load_table(0)
-        load_wb(1)
+        load_wb(1, held([P, 2, 2 * PASS], U8, "wb_raw1"))
 
         nc.vector.memset(tab_plane[:, 1, :].bitcast(I32), 0)
         cells = [held([P, T2], F32, "cells%d" % i) for i in range(PACK)]
         for i in range(PACK):
             nc.vector.memset(cells[i][:].bitcast(I32), 0)
 
-        picked_rows = placed([P, S], U8, "picked_rows", 8, 1536)
+        picked_rows = placed([P, S], U8, "picked_rows", LATE_WORDS, BANK - S // 2)
         nc.vector.tensor_copy(picked_rows[:], tab_rows[:].indirect(offs_sb[:]))
-        picked = {}
-
-        def gather_words(a, h):
-            if h == 0:
-                picked[a, h] = held([P, HALF], U32, "picked%d%d" % (a, h))
-            else:
-                picked[a, h] = placed([P, HALF], U32, "picked%d%d" % (a, h), 8, BANK * a)
-            nc.vector.tensor_copy(
-                picked[a, h][:], tab_win[a][:].bitcast(U32).indirect(offs_sb[:, 32 * h : 32 * h + 32])
-            )
-
         nc.vector.tensor_copy(tab_plane[:, 0, :].bitcast(I32), picked_rows[:].bitcast(I32))
         for a in (1, 0):
             for r in range(2 - 2 * a, 4):
                 nc.sync.dma_start(
                     tab_plane[r:P:32, a, :].bitcast(I32),
-                    picked_rows[16 * (r // 2) + 2 * a + r % 2 : P : 32, :].bitcast(I32),
+                    picked_rows[LIST * (r // 2) + 2 * a + r % 2 : P : 32, :].bitcast(I32),
                 )
 
-        gather_words(1, 0)
+        picked = {}
+
+        def gather_words(a, half):
+            name = "picked%d%d" % (a, half)
+            if half == 0:
+                picked[a, half] = held([P, HALF], U32, name)
+            else:
+                picked[a, half] = placed([P, HALF], U32, name, LATE_WORDS, BANK * a)
+            entries = offs_sb[:, HALF * half // LIST : HALF * (half + 1) // LIST]
+            nc.vector.tensor_copy(picked[a, half][:], tab_win[a][:].bitcast(U32).indirect(entries))
+
         wb_codes = [held([P, 2, 2 * PASS], U8, "wb_codes%d" % b) for b in range(2)]
         wb_plane = [held([P, 2, PASS], U8, "wb_plane%d" % b) for b in range(2)]
 
         def deal_wb(b):
-            cols = slice(PASS * b, PASS * (b + 1))
             nc.vector.tensor_copy(
                 wb_codes[b][:].bitcast(U16).rearrange("p a (t m) -> p a m t", t=PACK),
                 wb_raw[b][:].bitcast(U16).rearrange("p a (m t) -> p a m t", t=PACK),
             )
             nc.vector.tensor_copy(
                 wb_plane[b][:].rearrange("p a (t m) -> p a m t", t=PACK),
-                wb_rows[:, :, cols].rearrange("p a (m t) -> p a m t", t=PACK),
+                wb_rows[:, :, PASS * b : PASS * (b + 1)].rearrange("p a (m t) -> p a m t", t=PACK),
             )
 
+        gather_words(1, 0)
         deal_wb(0)
         gather_words(0, 0)
         deal_wb(1)
@@ -144,24 +147,25 @@ def tile_list_pen_biomass_cues_kernel(
         load_wa(0, 1)
         load_wa(1, 1)
 
-        def table_operand(a, h):
-            return dict(rhs=picked[a, h][:].bitcast(FP8X4), rhs_scale=tab_plane[:, a, HALF * h : HALF * (h + 1)])
+        def table_operand(a, half):
+            return dict(
+                rhs=picked[a, half][:].bitcast(FP8X4), rhs_scale=tab_plane[:, a, HALF * half : HALF * (half + 1)]
+            )
 
-        def wb_passes(bank, b, t, h, stop):
-            c0 = P * t
+        def wb_passes(bank, b, t, half, stop):
             for a in range(2):
                 nc.tensor.matmul_mx(
                     out=bank[:],
-                    lhsT=wb_codes[b][:, a, 2 * c0 : 2 * (c0 + P)].bitcast(FP4X4),
-                    lhsT_scale=wb_plane[b][:, a, c0 : c0 + P],
+                    lhsT=wb_codes[b][:, a, 2 * P * t : 2 * P * (t + 1)].bitcast(FP4X4),
+                    lhsT_scale=wb_plane[b][:, a, P * t : P * (t + 1)],
                     start=(a == 0),
                     stop=(stop and a == 1),
-                    **table_operand(a, h),
+                    **table_operand(a, half),
                 )
 
         wa_grouped, wa_codes, wa_plane = {}, {}, {}
 
-        def wa_passes(bank, b, t, h, start):
+        def wa_passes(bank, b, t, half, start):
             for a in (1, 0):
                 nc.tensor.matmul_mx(
                     out=bank[:],
@@ -169,21 +173,18 @@ def tile_list_pen_biomass_cues_kernel(
                     lhsT_scale=wa_plane[a, b][:, P * t : P * (t + 1)],
                     start=(start and a == 1),
                     stop=(a == 0),
-                    **table_operand(a, h),
+                    **table_operand(a, half),
                 )
 
-        def round_views(a, b):
-            if b == 1:
-                wa_grouped[a, b] = placed([P, PACK, P, PACK], BF16, "wa_grouped%d1" % a, 6, 4096 * a)
-            else:
-                wa_grouped[a, b] = held([P, PACK, P, PACK], BF16, "wa_grouped%d%d" % (a, b))
+        def rounding_views(a, b):
+            wa_grouped[a, b] = held([P, PACK, P, PACK], BF16, "wa_grouped%d%d" % (a, b))
             return (
                 wa_grouped[a, b][:].rearrange("p t m i -> p m t i"),
                 wa_raw[a, b][:].rearrange("p i (m t) -> p m t i", t=PACK),
             )
 
         def round_wa(a, b):
-            grouped, raw = round_views(a, b)
+            grouped, raw = rounding_views(a, b)
             nc.vector.tensor_scalar(out=grouped, in0=raw, scalar1=-1.0, scalar2=None, op0=ALU.mult)
 
         def quantise_wa(a, b):
@@ -195,37 +196,32 @@ def tile_list_pen_biomass_cues_kernel(
                 in_=wa_grouped[a, b][:].rearrange("p t m i -> p (t m i)"),
             )
 
-        first_grouped, first_raw = round_views(0, 0)
+        first_grouped, first_raw = rounding_views(0, 0)
         nc.scalar.activation(first_grouped, first_raw, ACT.Copy, scale=-1.0)
 
-        exp_b, b_sb, gate = {}, {}, {}
+        exp_b, gate = {}, {}
 
-        def exponentials(b, h):
+        def exponentials(b, half):
             for t in range(PACK):
-                bank = bank_tile([P, HALF], "bank_b%d%d%d" % (b, t, h), t)
-                wb_passes(bank, b, t, h, True)
-                if (b, h) == (0, 1):
-                    exp_b[b, t, h] = placed([P, HALF], F32, "exp_b%d%d%d" % (b, t, h), 4, BANK * t)
-                    b_sb[b, t, h] = placed([P, HALF], F32, "b_sb%d%d%d" % (b, t, h), 3, BANK * t)
+                name = "%d%d%d" % (b, t, half)
+                bank = in_bank([P, HALF], "bank_b" + name, LOW_BANKS + t)
+                wb_passes(bank, b, t, half, True)
+                if (b, half) == (0, 1):
+                    exp_b[b, t, half] = placed([P, HALF], F32, "exp_b" + name, WA_01, BANK * t)
+                    gate[b, t, half] = placed([P, HALF], F32, "gate" + name, WA_10, BANK * t)
                 else:
-                    exp_b[b, t, h] = held([P, HALF], F32, "exp_b%d%d%d" % (b, t, h))
-                nc.scalar.activation(exp_b[b, t, h][:], bank[:], ACT.Exp)
-                if h == 0:
-                    if b == 0:
-                        b_sb[b, t, h] = placed([P, HALF], F32, "b_sb%d%d%d" % (b, t, h), 7, BANK * t)
-                    else:
-                        b_sb[b, t, h] = held([P, HALF], F32, "b_sb%d%d%d" % (b, t, h))
-                    gate[b, t, h] = b_sb[b, t, h]
-                if (b, h) != (1, 1):
-                    nc.scalar.copy(b_sb[b, t, h][:], bank[:])
+                    exp_b[b, t, half] = held([P, HALF], F32, "exp_b" + name)
+                nc.scalar.activation(exp_b[b, t, half][:], bank[:], ACT.Exp)
+                if half == 0:
+                    gate[b, t, half] = held([P, HALF], F32, "gate" + name)
+                if (b, half) != (1, 1):
+                    nc.scalar.copy(gate[b, t, half][:], bank[:])
 
-        def difference(b, h, first_bank):
+        def difference(b, half):
             for t in range(PACK):
-                bank = bank_tile([P, HALF], "bank_a%d%d%d" % (b, t, h), first_bank + t)
-                wa_passes(bank, b, t, h, True)
-                if h == 1:
-                    gate[b, t, h] = placed([P, HALF], F32, "gate%d%d%d" % (b, t, h), 7, BANK * t)
-                nc.vector.tensor_tensor(gate[b, t, h][:], bank[:], b_sb[b, t, h][:], ALU.add)
+                bank = in_bank([P, HALF], "bank_a%d%d%d" % (b, t, half), HIGH_BANKS + t)
+                wa_passes(bank, b, t, half, True)
+                nc.vector.tensor_tensor(gate[b, t, half][:], bank[:], gate[b, t, half][:], ALU.add)
 
         exponentials(0, 0)
         exponentials(1, 0)
@@ -238,12 +234,12 @@ def tile_list_pen_biomass_cues_kernel(
         round_wa(1, 1)
         quantise_wa(0, 1)
         quantise_wa(1, 1)
-        difference(0, 0, 4)
+        difference(0, 0)
 
-        wc_raw = placed([P, 2, N], I32, "wc_raw", 1)
-        wgo_sb = placed([P, S], F32, "wgo_sb", 1, 4096)
-        wc_rows = placed([P, N], U8, "wc_rows", 0)
-        gain_sb = placed([P, 2, PACK], F32, "gain_sb", 0, 1024)
+        wc_raw = placed([P, 2, N], I32, "wc_raw", TABLE_1)
+        wgo_sb = placed([P, S], F32, "wgo_sb", TABLE_1, 2 * BANK)
+        wc_rows = placed([P, N], U8, "wc_rows", TABLE_0)
+        gain_sb = placed([P, 2, PACK], F32, "gain_sb", TABLE_0, BANK // 2)
         nc.vector.memset(wc_rows[:].bitcast(I32), 0)
         nc.sync.dma_start(wc_raw[:], wc_words.rearrange("a p c i -> p a (c i)").bitcast(I32))
         for d in range(4):
@@ -253,21 +249,22 @@ def tile_list_pen_biomass_cues_kernel(
         nc.sync.dma_start(gain_sb[:], gain.rearrange("(b p t) -> p b t", b=2, t=PACK))
         nc.sync.dma_start(wgo_sb[:], wgo)
 
-        difference(1, 0, 4)
+        difference(1, 0)
 
         wc_codes = held([P, 2, N], I32, "wc_codes")
         wc_plane = held([P, N], U8, "wc_plane")
         nc.vector.tensor_copy(
-            wc_codes[:].rearrange("p a (t m) -> p a m t", t=PACK),
-            wc_raw[:].rearrange("p a (m t) -> p a m t", t=PACK),
+            wc_codes[:].rearrange("p b (t m) -> p b m t", t=PACK),
+            wc_raw[:].rearrange("p b (m t) -> p b m t", t=PACK),
         )
         nc.vector.tensor_copy(
             wc_plane[:].rearrange("p (t m) -> p m t", t=PACK),
             wc_rows[:].rearrange("p (m t) -> p m t", t=PACK),
         )
 
-        h_rows, operands, y_bank, y_sb = {}, {}, {}, {}
+        h_rows, h_grouped, h_operand, y_bank, y_sb = {}, {}, {}, {}, {}
         y_last = held([P, 2, HALF], F32, "y_last")
+        last_rows_at = BANK
 
         def columns(c):
             return slice(CHUNK * (c % 2), CHUNK * (c % 2 + 1))
@@ -278,10 +275,13 @@ def tile_list_pen_biomass_cues_kernel(
                 nc.scalar.activation(view, view, ACT.Sigmoid, scale=-1.0)
 
         def products(c, b):
+            name = "h_rows%d%d" % (c, b)
             if (c, b) == (3, 0):
-                h_rows[c, b] = placed([P, PACK, CHUNK], BF16, "h_rows30", 0, 2048)
+                h_rows[c, b] = placed([P, PACK, CHUNK], BF16, name, TABLE_0, last_rows_at)
+            elif c == 1:
+                h_rows[c, b] = placed([P, PACK, CHUNK], BF16, name, FIRST_H, BANK * b)
             else:
-                h_rows[c, b] = held([P, PACK, CHUNK], BF16, "h_rows%d%d" % (c, b))
+                h_rows[c, b] = held([P, PACK, CHUNK], BF16, name)
             for t in range(PACK):
                 nc.vector.scalar_tensor_tensor(
                     out=h_rows[c, b][:, t, :],
@@ -292,30 +292,29 @@ def tile_list_pen_biomass_cues_kernel(
                     op1=ALU.mult,
                 )
 
-        h_groups = {}
-
         def interleave(c, b):
-            h_groups[c, b] = held([P, CHUNK, PACK], BF16, "h_grouped%d%d" % (c, b))
+            name = "h_grouped%d%d" % (c, b)
+            if c == 0:
+                h_grouped[c, b] = placed([P, CHUNK, PACK], BF16, name, FIRST_H, BANK * b)
+            else:
+                h_grouped[c, b] = held([P, CHUNK, PACK], BF16, name)
             copy = nc.vector.tensor_copy if (c, b) in ON_VECTOR else nc.scalar.copy
             copy(
-                h_groups[c, b][:].rearrange("p (c i) t -> p c t i", i=4),
-                h_rows[c, b][:].rearrange("p t (c i) -> p c t i", i=4),
+                h_grouped[c, b][:].rearrange("p (j e) t -> p j t e", e=4),
+                h_rows[c, b][:].rearrange("p t (j e) -> p j t e", e=4),
             )
 
         def quantise_h(c, b):
-            if (c, b) not in h_groups:
-                interleave(c, b)
-            h_grouped = h_groups[c, b]
             codes = held([P, CHUNK], U32, "h_codes%d%d" % (c, b))
             plane = held([P, CHUNK], U8, "h_plane%d%d" % (c, b))
             nc.vector.quantize_mx(
-                out=codes[:].bitcast(FP8X4), scales=plane[:], in_=h_grouped[:].rearrange("p c t -> p (c t)")
+                out=codes[:].bitcast(FP8X4), scales=plane[:], in_=h_grouped[c, b][:].rearrange("p j t -> p (j t)")
             )
-            operands[c, b] = (codes, plane)
+            h_operand[c, b] = (codes, plane)
 
-        def mix(c, order):
+        def mix(c, first_bank, order):
             for k in range(2):
-                y_bank[c, k] = bank_tile([P, 2, CHUNK], "bank_y%d%d" % (c, k), (4, 0, 4, 6)[c] + k)
+                y_bank[c, k] = in_bank([P, 2, CHUNK], "bank_y%d%d" % (c, k), first_bank + k)
                 for u in range(2):
                     i = 2 * k + u
                     for b in order:
@@ -323,34 +322,32 @@ def tile_list_pen_biomass_cues_kernel(
                             out=y_bank[c, k][:, u, :],
                             lhsT=wc_codes[:, b, P * i : P * (i + 1)].bitcast(FP8X4),
                             lhsT_scale=wc_plane[4 * b : P, P * i : P * (i + 1)],
-                            rhs=operands[c, b][0][:].bitcast(FP8X4),
-                            rhs_scale=operands[c, b][1][:],
+                            rhs=h_operand[c, b][0][:].bitcast(FP8X4),
+                            rhs_scale=h_operand[c, b][1][:],
                             start=(b == order[0]),
                             stop=(b == order[1]),
                         )
 
         def evacuate(c, k):
-            if c >= 2 and k == 1:
-                nc.scalar.copy(y_last[:, :, columns(c)], y_bank[c, k][:])
-                return
             y_sb[c, k] = held([P, 2, CHUNK], F32, "y_sb%d%d" % (c, k))
             nc.scalar.copy(y_sb[c, k][:], y_bank[c, k][:])
 
-        def late_scatter(u, slot, at):
-            y_late = placed([P, CHUNK], F32, "y_late%d" % u, slot, at)
-            nc.scalar.copy(y_late[:], y_bank[1, 1][:, u, :])
+        def put(i, values, first, count):
             nc.vector.tensor_tensor(
-                cells[2 + u][:].indirect(offs2_sb[:, CHUNK // 16 : HALF // 16]), y_late[:], wgo_sb[:, CHUNK:HALF], ALU.mult
+                cells[i][:].indirect(offs2_sb[:, first // LIST : (first + count) // LIST]),
+                values,
+                wgo_sb[:, first : first + count],
+                ALU.mult,
             )
 
         def scatter(c, k):
             for u in range(2):
-                nc.vector.tensor_tensor(
-                    cells[2 * k + u][:].indirect(offs2_sb[:, CHUNK * c // 16 : CHUNK * (c + 1) // 16]),
-                    y_sb[c, k][:, u, :],
-                    wgo_sb[:, CHUNK * c : CHUNK * (c + 1)],
-                    ALU.mult,
-                )
+                put(2 * k + u, y_sb[c, k][:, u, :], CHUNK * c, CHUNK)
+
+        def late_scatter(u, slot, at):
+            y_late = placed([P, CHUNK], F32, "y_late%d" % u, slot, at)
+            nc.scalar.copy(y_late[:], y_bank[1, 1][:, u, :])
+            put(2 + u, y_late[:], CHUNK, CHUNK)
 
         for b in range(2):
             sigmoids(0, b)
@@ -359,20 +356,21 @@ def tile_list_pen_biomass_cues_kernel(
             interleave(0, b)
         for b in range(2):
             quantise_h(0, b)
-        mix(0, (1, 0))
+        mix(0, HIGH_BANKS, (1, 0))
         for b in range(2):
             sigmoids(1, b)
             products(1, b)
         evacuate(0, 0)
         evacuate(0, 1)
         for b in range(2):
+            interleave(1, b)
             quantise_h(1, b)
 
         for t in range(PACK):
-            bank = bank_tile([P, HALF], "bank_d%d" % t, t)
+            bank = in_bank([P, HALF], "bank_sum%d" % t, LOW_BANKS + t)
             wb_passes(bank, 1, t, 1, False)
             wa_passes(bank, 1, t, 1, False)
-            gate[1, t, 1] = placed([P, HALF], F32, "gate1%d1" % t, 2, BANK * t)
+            gate[1, t, 1] = placed([P, HALF], F32, "gate1%d1" % t, WA_00, BANK * t)
             nc.scalar.activation(gate[1, t, 1][:], bank[:], ACT.Sigmoid, scale=-1.0)
 
         scatter(0, 0)
@@ -380,34 +378,34 @@ def tile_list_pen_biomass_cues_kernel(
         exponentials(0, 1)
         for c in (2, 3):
             products(c, 1)
-        difference(0, 1, 0)
-        mix(1, (1, 0))
+        difference(0, 1)
+        mix(1, LOW_BANKS, (1, 0))
         evacuate(1, 0)
         scatter(1, 0)
         for c in (2, 3):
+            interleave(c, 1)
             quantise_h(c, 1)
-        sigmoids(2, 0)
-        products(2, 0)
-        sigmoids(3, 0)
-        products(3, 0)
-        interleave(2, 0)
-        interleave(3, 0)
+        for c in (2, 3):
+            sigmoids(c, 0)
+            products(c, 0)
+        for c in (2, 3):
+            interleave(c, 0)
         quantise_h(2, 0)
-        mix(2, (0, 1))
+        mix(2, HIGH_BANKS, (0, 1))
         quantise_h(3, 0)
-        late_scatter(0, 4, BANK * 3)
-        late_scatter(1, 0, 2048)
+
+        late_scatter(0, WA_01, BANK * (PACK - 1))
+        late_scatter(1, TABLE_0, last_rows_at)
         evacuate(2, 0)
-        mix(3, (0, 1))
+        mix(3, HIGH_BANKS + 2, (0, 1))
         evacuate(3, 0)
-        evacuate(2, 1)
-        evacuate(3, 1)
+        for c in (2, 3):
+            nc.scalar.copy(y_last[:, :, columns(c)], y_bank[c, 1][:])
+
         for c in (2, 3):
             scatter(c, 0)
         for u in range(2):
-            nc.vector.tensor_tensor(
-                cells[2 + u][:].indirect(offs2_sb[:, HALF // 16 : S // 16]), y_last[:, u, :], wgo_sb[:, HALF:S], ALU.mult
-            )
+            put(2 + u, y_last[:, u, :], HALF, HALF)
 
         out_rows = out.rearrange("(p i) t -> i p t", i=PACK)
         for i in range(PACK):

@@ -28,7 +28,7 @@ SLOT = 4 * BANK
 TABLE_0, TABLE_1, WA_00, WA_10, WA_01, WA_11, LATE_WORDS, FIRST_H = range(8)
 LOW_BANKS, HIGH_BANKS = 0, 4
 
-ON_VECTOR = ((0, 0), (0, 1), (2, 0), (3, 0))
+ON_VECTOR = ((0, 1), (3, 0))
 
 
 def tile_list_pen_biomass_cues_kernel(
@@ -105,14 +105,6 @@ def tile_list_pen_biomass_cues_kernel(
 
         picked_rows = placed([P, S], U8, "picked_rows", LATE_WORDS, BANK - S // 2)
         nc.vector.tensor_copy(picked_rows[:], tab_rows[:].indirect(offs_sb[:]))
-        nc.vector.tensor_copy(tab_plane[:, 0, :].bitcast(I32), picked_rows[:].bitcast(I32))
-        for a in (1, 0):
-            for r in range(2 - 2 * a, 4):
-                nc.sync.dma_start(
-                    tab_plane[r:P:32, a, :].bitcast(I32),
-                    picked_rows[LIST * (r // 2) + 2 * a + r % 2 : P : 32, :].bitcast(I32),
-                )
-
         picked = {}
 
         def gather_words(a, half):
@@ -123,6 +115,15 @@ def tile_list_pen_biomass_cues_kernel(
                 picked[a, half] = placed([P, HALF], U32, name, LATE_WORDS, BANK * a)
             entries = offs_sb[:, HALF * half // LIST : HALF * (half + 1) // LIST]
             nc.vector.tensor_copy(picked[a, half][:], tab_win[a][:].bitcast(U32).indirect(entries))
+
+        gather_words(1, 0)
+        nc.vector.tensor_copy(tab_plane[:, 0, :].bitcast(I32), picked_rows[:].bitcast(I32))
+        for a in (1, 0):
+            for r in range(2 - 2 * a, 4):
+                nc.sync.dma_start(
+                    tab_plane[r:P:32, a, :].bitcast(I32),
+                    picked_rows[LIST * (r // 2) + 2 * a + r % 2 : P : 32, :].bitcast(I32),
+                )
 
         wb_codes = [held([P, 2, 2 * PASS], U8, "wb_codes%d" % b) for b in range(2)]
         wb_plane = [held([P, 2, PASS], U8, "wb_plane%d" % b) for b in range(2)]
@@ -137,7 +138,6 @@ def tile_list_pen_biomass_cues_kernel(
                 wb_rows[:, :, PASS * b : PASS * (b + 1)].rearrange("p a (m t) -> p a m t", t=PACK),
             )
 
-        gather_words(1, 0)
         deal_wb(0)
         gather_words(0, 0)
         deal_wb(1)

@@ -23,12 +23,14 @@ HALF = 512
 CHUNK = 256
 LIST = 16
 BANK = 2048
-SLOT = 4 * BANK
+KIB = 1024
 
-TABLE_0, TABLE_1, WA_00, WA_10, WA_01, WA_11, LATE_WORDS, FIRST_H = range(8)
+TABLE = (0, 8)
+WA = {(0, 0): 16, (1, 0): 26, (0, 1): 34, (1, 1): 42}
+LATE_WORDS = 50
+FIRST_SIGMOIDS = 54
+LAST_EXP, FIRST_GATE, LAST_ROWS = 70, 78, 86
 LOW_BANKS, HIGH_BANKS = 0, 4
-
-ON_VECTOR = ((0, 1), (3, 0))
 
 
 def tile_list_pen_biomass_cues_kernel(
@@ -44,8 +46,8 @@ def tile_list_pen_biomass_cues_kernel(
         def held(shape, dtype, name):
             return keep.tile(shape, dtype, name=name, align_bytes=64)
 
-        def placed(shape, dtype, name, slot, at=0):
-            return reused.tile(shape, dtype, name=name, align_bytes=64, offset=SLOT * slot + at)
+        def placed(shape, dtype, name, kib):
+            return reused.tile(shape, dtype, name=name, align_bytes=64, offset=int(KIB * kib))
 
         def in_bank(shape, name, bank):
             return psum.tile(shape, F32, name=name, offset=BANK * bank)
@@ -55,33 +57,29 @@ def tile_list_pen_biomass_cues_kernel(
         nc.sync.dma_start(offs_sb[:], offs)
         nc.sync.dma_start(offs2_sb[:], offs2)
 
-        tab_rows = held([P, T], U8, "tab_rows")
-        for a in range(2):
-            for e in range(2):
-                nc.sync.dma_start(
-                    tab_rows[2 * a + e : P : 4, :].bitcast(I32),
-                    tab_scales[a, e:16:2, :].bitcast(I32).unsqueeze(1).broadcast_to([8, 4, T // 4]),
-                )
+        tab_rows = placed([P, T], U8, "tab_rows", WA[0, 0] + 7)
+        for j in range(4):
+            nc.sync.dma_start(tab_rows[j:P:4, :].bitcast(I32), tab_scales.rearrange("a q t -> q a t").bitcast(I32))
 
-        wb_rows = placed([P, 2, H], U8, "wb_rows", WA_11)
+        wb_rows = placed([P, 2, H], U8, "wb_rows", WA[1, 1])
         tab_plane = held([P, 2, S], U8, "tab_plane")
         nc.gpsimd.memset(wb_rows[:].rearrange("p a c -> p (a c)").bitcast(I32), 0)
 
         tab_win, wb_raw, wa_raw = {}, {}, {}
 
         def load_table(a):
-            tab_win[a] = placed([P, T], I32, "tab_win%d" % a, TABLE_0 + a)
+            tab_win[a] = placed([P, T], I32, "tab_win%d" % a, TABLE[a])
             nc.sync.dma_start(tab_win[a][:], tab_words[a].rearrange("p t i -> p (t i)").bitcast(I32))
 
-        def load_wb(b, tile):
-            wb_raw[b] = tile
+        def load_wb(b, kib):
+            wb_raw[b] = placed([P, 2, 2 * PASS], U8, "wb_raw%d" % b, kib)
             nc.sync.dma_start(
-                tile[:].bitcast(I32),
+                wb_raw[b][:].bitcast(I32),
                 wb_words[:, :, 2 * PASS * b : 2 * PASS * (b + 1)].rearrange("a p c -> p a c").bitcast(I32),
             )
 
         def load_wa(a, b):
-            wa_raw[a, b] = placed([P, PACK, HALF], F32, "wa_raw%d%d" % (a, b), WA_00 + 2 * b + a)
+            wa_raw[a, b] = placed([P, PACK, HALF], F32, "wa_raw%d%d" % (a, b), WA[a, b])
             nc.sync.dma_start(
                 wa_raw[a, b][:],
                 wa[PASS * a : PASS * (a + 1), PASS * b : PASS * (b + 1)].rearrange("(p i) c -> p i c", i=PACK),
@@ -93,18 +91,25 @@ def tile_list_pen_biomass_cues_kernel(
                 wb_rows[32 * d : 32 * d + 4, :, :].bitcast(I32),
                 wb_scales[:, 4 * d : 4 * d + 4, :].rearrange("a q c -> q a c").bitcast(I32),
             )
-        load_wb(0, placed([P, 2, 2 * PASS], U8, "wb_raw0", WA_01, -PASS * 2))
-        load_wa(0, 0)
+        load_wb(0, WA[0, 1] - 1)
         load_table(0)
-        load_wb(1, held([P, 2, 2 * PASS], U8, "wb_raw1"))
 
-        nc.vector.memset(tab_plane[:, 1, :].bitcast(I32), 0)
-        cells = [held([P, T2], F32, "cells%d" % i) for i in range(PACK)]
-        for i in range(PACK):
+        nc.vector.memset(tab_plane[:].rearrange("p a s -> p (a s)").bitcast(I32), 0)
+        cells = {}
+        for i in range(2):
+            cells[i] = held([P, T2], F32, "cells%d" % i)
             nc.vector.memset(cells[i][:].bitcast(I32), 0)
 
-        picked_rows = placed([P, S], U8, "picked_rows", LATE_WORDS, BANK - S // 2)
+        picked_rows = placed([P, S], U8, "picked_rows", LATE_WORDS + 1.5)
         nc.vector.tensor_copy(picked_rows[:], tab_rows[:].indirect(offs_sb[:]))
+        for d in range(4):
+            nc.sync.dma_start(
+                tab_plane[32 * d : 32 * d + 4, :, :].bitcast(I32),
+                picked_rows[32 * d : 32 * (d + 1) : 4, :].bitcast(I32),
+            )
+        load_wb(1, WA[0, 0] + 8)
+        load_wa(0, 0)
+
         picked = {}
 
         def gather_words(a, half):
@@ -112,24 +117,15 @@ def tile_list_pen_biomass_cues_kernel(
             if half == 0:
                 picked[a, half] = held([P, HALF], U32, name)
             else:
-                picked[a, half] = placed([P, HALF], U32, name, LATE_WORDS, BANK * a)
+                picked[a, half] = placed([P, HALF], U32, name, LATE_WORDS + 2 * a)
             entries = offs_sb[:, HALF * half // LIST : HALF * (half + 1) // LIST]
             nc.vector.tensor_copy(picked[a, half][:], tab_win[a][:].bitcast(U32).indirect(entries))
 
-        gather_words(1, 0)
-        nc.vector.tensor_copy(tab_plane[:, 0, :].bitcast(I32), picked_rows[:].bitcast(I32))
-        for a in (1, 0):
-            for r in range(2 - 2 * a, 4):
-                nc.sync.dma_start(
-                    tab_plane[r:P:32, a, :].bitcast(I32),
-                    picked_rows[LIST * (r // 2) + 2 * a + r % 2 : P : 32, :].bitcast(I32),
-                )
-
-        wb_codes = [held([P, 2, 2 * PASS], U8, "wb_codes%d" % b) for b in range(2)]
-        wb_plane = [held([P, 2, PASS], U8, "wb_plane%d" % b) for b in range(2)]
+        wb_codes = [placed([P, 2, 2 * PASS], U8, "wb_codes0", FIRST_SIGMOIDS + 3), held([P, 2, 2 * PASS], U8, "wb_codes1")]
+        wb_plane = [placed([P, 2, PASS], U8, "wb_plane0", FIRST_SIGMOIDS + 11.5), held([P, 2, PASS], U8, "wb_plane1")]
 
         def deal_wb(b):
-            nc.vector.tensor_copy(
+            nc.scalar.copy(
                 wb_codes[b][:].bitcast(U16).rearrange("p a (t m) -> p a m t", t=PACK),
                 wb_raw[b][:].bitcast(U16).rearrange("p a (m t) -> p a m t", t=PACK),
             )
@@ -138,6 +134,7 @@ def tile_list_pen_biomass_cues_kernel(
                 wb_rows[:, :, PASS * b : PASS * (b + 1)].rearrange("p a (m t) -> p a m t", t=PACK),
             )
 
+        gather_words(1, 0)
         deal_wb(0)
         gather_words(0, 0)
         deal_wb(1)
@@ -176,16 +173,15 @@ def tile_list_pen_biomass_cues_kernel(
                     **table_operand(a, half),
                 )
 
-        def rounding_views(a, b):
-            wa_grouped[a, b] = held([P, PACK, P, PACK], BF16, "wa_grouped%d%d" % (a, b))
-            return (
-                wa_grouped[a, b][:].rearrange("p t m i -> p m t i"),
-                wa_raw[a, b][:].rearrange("p i (m t) -> p m t i", t=PACK),
-            )
-
         def round_wa(a, b):
-            grouped, raw = rounding_views(a, b)
-            nc.vector.tensor_scalar(out=grouped, in0=raw, scalar1=-1.0, scalar2=None, op0=ALU.mult)
+            wa_grouped[a, b] = held([P, PACK, P, PACK], BF16, "wa_grouped%d%d" % (a, b))
+            nc.vector.tensor_scalar(
+                out=wa_grouped[a, b][:].rearrange("p t m i -> p m t i"),
+                in0=wa_raw[a, b][:].rearrange("p i (m t) -> p m t i", t=PACK),
+                scalar1=-1.0,
+                scalar2=None,
+                op0=ALU.mult,
+            )
 
         def quantise_wa(a, b):
             wa_codes[a, b] = held([P, HALF], U32, "wa_codes%d%d" % (a, b))
@@ -196,60 +192,55 @@ def tile_list_pen_biomass_cues_kernel(
                 in_=wa_grouped[a, b][:].rearrange("p t m i -> p (t m i)"),
             )
 
-        first_grouped, first_raw = rounding_views(0, 0)
-        nc.scalar.activation(first_grouped, first_raw, ACT.Copy, scale=-1.0)
+        exp_b = {key: held([P, PACK, HALF], F32, "exp_b%d%d" % key) for key in ((0, 0), (1, 0), (0, 1))}
+        exp_b[1, 1] = placed([P, PACK, HALF], F32, "exp_b11", LAST_EXP)
+        gate = {(0, 0): placed([P, PACK, HALF], F32, "gate00", FIRST_GATE), (1, 0): held([P, PACK, HALF], F32, "gate10")}
+        b_bank = {}
 
-        exp_b, gate = {}, {}
+        b_order = [(0, t, 0) for t in range(PACK)]
+        for t in range(PACK):
+            b_order.extend([(1, t, 0), (1, t, 1)])
+        b_order.extend([(0, t, 1) for t in range(PACK)])
+        for n, (b, t, half) in enumerate(b_order):
+            b_bank[b, t, half] = in_bank([P, HALF], "bank_b%d%d%d" % (b, t, half), LOW_BANKS + n % 4)
+            wb_passes(b_bank[b, t, half], b, t, half, True)
+            nc.scalar.activation(exp_b[b, half][:, t, :], b_bank[b, t, half][:], ACT.Exp)
+            if half == 0:
+                nc.scalar.copy(gate[b, half][:, t, :], b_bank[b, t, half][:])
 
-        def exponentials(b, half):
+        def difference(b, half, first_bank):
             for t in range(PACK):
-                name = "%d%d%d" % (b, t, half)
-                bank = in_bank([P, HALF], "bank_b" + name, LOW_BANKS + t)
-                wb_passes(bank, b, t, half, True)
-                if (b, half) == (0, 1):
-                    exp_b[b, t, half] = placed([P, HALF], F32, "exp_b" + name, WA_01, BANK * t)
-                    gate[b, t, half] = placed([P, HALF], F32, "gate" + name, WA_10, BANK * t)
-                else:
-                    exp_b[b, t, half] = held([P, HALF], F32, "exp_b" + name)
-                nc.scalar.activation(exp_b[b, t, half][:], bank[:], ACT.Exp)
-                if half == 0:
-                    gate[b, t, half] = held([P, HALF], F32, "gate" + name)
-                if (b, half) != (1, 1):
-                    nc.scalar.copy(gate[b, t, half][:], bank[:])
-
-        def difference(b, half):
-            for t in range(PACK):
-                bank = in_bank([P, HALF], "bank_a%d%d%d" % (b, t, half), HIGH_BANKS + t)
+                bank = in_bank([P, HALF], "bank_a%d%d%d" % (b, t, half), first_bank + t)
                 wa_passes(bank, b, t, half, True)
-                nc.vector.tensor_tensor(gate[b, t, half][:], bank[:], gate[b, t, half][:], ALU.add)
+                nc.vector.tensor_tensor(gate[b, half][:, t, :], bank[:], gate[b, half][:, t, :], ALU.add)
 
-        exponentials(0, 0)
-        exponentials(1, 0)
-        exponentials(1, 1)
-
-        quantise_wa(0, 0)
+        round_wa(0, 0)
         round_wa(1, 0)
-        round_wa(0, 1)
+        quantise_wa(0, 0)
         quantise_wa(1, 0)
+        round_wa(0, 1)
         round_wa(1, 1)
         quantise_wa(0, 1)
         quantise_wa(1, 1)
-        difference(0, 0)
+        for a in (1, 0):
+            cells[2 + a] = placed([P, T2], F32, "cells%d" % (2 + a), TABLE[a])
+            nc.vector.memset(cells[2 + a][:].bitcast(I32), 0)
+        difference(0, 0, HIGH_BANKS)
 
-        wc_raw = placed([P, 2, N], I32, "wc_raw", TABLE_1)
-        wgo_sb = placed([P, S], F32, "wgo_sb", TABLE_1, 2 * BANK)
-        wc_rows = placed([P, N], U8, "wc_rows", TABLE_0)
-        gain_sb = placed([P, 2, PACK], F32, "gain_sb", TABLE_0, BANK // 2)
+        wc_raw = placed([P, 2, N], I32, "wc_raw", WA[0, 0])
+        wgo_sb = placed([P, S], F32, "wgo_sb", WA[0, 0] + 4)
+        wc_rows = placed([P, N], U8, "wc_rows", WA[1, 0])
+        gain_sb = placed([P, 2, PACK], F32, "gain_sb", WA[1, 0] + 1)
         nc.vector.memset(wc_rows[:].bitcast(I32), 0)
         nc.sync.dma_start(wc_raw[:], wc_words.rearrange("a p c i -> p a (c i)").bitcast(I32))
+        nc.sync.dma_start(gain_sb[:], gain.rearrange("(b p t) -> p b t", b=2, t=PACK))
         for d in range(4):
             nc.sync.dma_start(
                 wc_rows[32 * d : 32 * d + 8, :].bitcast(I32), wc_scales[:, 4 * d : 4 * d + 4, :].bitcast(I32)
             )
-        nc.sync.dma_start(gain_sb[:], gain.rearrange("(b p t) -> p b t", b=2, t=PACK))
         nc.sync.dma_start(wgo_sb[:], wgo)
 
-        difference(1, 0)
+        difference(1, 0, HIGH_BANKS)
 
         wc_codes = held([P, 2, N], I32, "wc_codes")
         wc_plane = held([P, N], U8, "wc_plane")
@@ -262,75 +253,59 @@ def tile_list_pen_biomass_cues_kernel(
             wc_rows[:].rearrange("p (m t) -> p m t", t=PACK),
         )
 
-        h_rows, h_grouped, h_operand, y_bank, y_sb = {}, {}, {}, {}, {}
-        y_last = held([P, 2, HALF], F32, "y_last")
-        last_rows_at = BANK
+        sigmoid, h_rows, h_grouped, h_operand = {}, {}, {}, {}
 
-        def columns(c):
-            return slice(CHUNK * (c % 2), CHUNK * (c % 2 + 1))
+        def within_half(first, count):
+            return slice(first % HALF, first % HALF + count)
 
-        def sigmoids(c, b):
-            for t in range(PACK):
-                view = gate[b, t, c // 2][:, columns(c)]
-                nc.scalar.activation(view, view, ACT.Sigmoid, scale=-1.0)
-
-        def products(c, b):
-            name = "h_rows%d%d" % (c, b)
-            if (c, b) == (3, 0):
-                h_rows[c, b] = placed([P, PACK, CHUNK], BF16, name, TABLE_0, last_rows_at)
-            elif c == 1:
-                h_rows[c, b] = placed([P, PACK, CHUNK], BF16, name, FIRST_H, BANK * b)
+        def products(first, count, b):
+            name = "h_rows%d_%d" % (first, b)
+            if (first, b) == (HALF, 0):
+                h_rows[first, b] = placed([P, PACK, count], BF16, name, LAST_ROWS)
             else:
-                h_rows[c, b] = held([P, PACK, CHUNK], BF16, name)
+                h_rows[first, b] = held([P, PACK, count], BF16, name)
             for t in range(PACK):
                 nc.vector.scalar_tensor_tensor(
-                    out=h_rows[c, b][:, t, :],
-                    in0=exp_b[b, t, c // 2][:, columns(c)],
+                    out=h_rows[first, b][:, t, :],
+                    in0=exp_b[b, first // HALF][:, t, within_half(first, count)],
                     scalar=gain_sb[:, b, t : t + 1],
-                    in1=gate[b, t, c // 2][:, columns(c)],
+                    in1=sigmoid[first, b][:, t, :],
                     op0=ALU.mult,
                     op1=ALU.mult,
                 )
 
-        def interleave(c, b):
-            name = "h_grouped%d%d" % (c, b)
-            if c == 0:
-                h_grouped[c, b] = placed([P, CHUNK, PACK], BF16, name, FIRST_H, BANK * b)
-            else:
-                h_grouped[c, b] = held([P, CHUNK, PACK], BF16, name)
-            copy = nc.vector.tensor_copy if (c, b) in ON_VECTOR else nc.scalar.copy
+        def interleave(first, count, b, copy):
+            h_grouped[first, b] = held([P, count, PACK], BF16, "h_grouped%d_%d" % (first, b))
             copy(
-                h_grouped[c, b][:].rearrange("p (j e) t -> p j t e", e=4),
-                h_rows[c, b][:].rearrange("p t (j e) -> p j t e", e=4),
+                h_grouped[first, b][:].rearrange("p (j e) t -> p j t e", e=4),
+                h_rows[first, b][:].rearrange("p t (j e) -> p j t e", e=4),
             )
 
-        def quantise_h(c, b):
-            codes = held([P, CHUNK], U32, "h_codes%d%d" % (c, b))
-            plane = held([P, CHUNK], U8, "h_plane%d%d" % (c, b))
+        def quantise_h(first, count, b):
+            codes = held([P, count], U32, "h_codes%d_%d" % (first, b))
+            plane = held([P, count], U8, "h_plane%d_%d" % (first, b))
             nc.vector.quantize_mx(
-                out=codes[:].bitcast(FP8X4), scales=plane[:], in_=h_grouped[c, b][:].rearrange("p j t -> p (j t)")
+                out=codes[:].bitcast(FP8X4), scales=plane[:], in_=h_grouped[first, b][:].rearrange("p j t -> p (j t)")
             )
-            h_operand[c, b] = (codes, plane)
+            h_operand[first, b] = (codes, plane)
 
-        def mix(c, first_bank, order):
-            for k in range(2):
-                y_bank[c, k] = in_bank([P, 2, CHUNK], "bank_y%d%d" % (c, k), first_bank + k)
-                for u in range(2):
-                    i = 2 * k + u
-                    for b in order:
-                        nc.tensor.matmul_mx(
-                            out=y_bank[c, k][:, u, :],
-                            lhsT=wc_codes[:, b, P * i : P * (i + 1)].bitcast(FP8X4),
-                            lhsT_scale=wc_plane[4 * b : P, P * i : P * (i + 1)],
-                            rhs=h_operand[c, b][0][:].bitcast(FP8X4),
-                            rhs_scale=h_operand[c, b][1][:],
-                            start=(b == order[0]),
-                            stop=(b == order[1]),
-                        )
+        def mix(first, i, view, order):
+            for b in order:
+                nc.tensor.matmul_mx(
+                    out=view,
+                    lhsT=wc_codes[:, b, P * i : P * (i + 1)].bitcast(FP8X4),
+                    lhsT_scale=wc_plane[4 * b : P, P * i : P * (i + 1)],
+                    rhs=h_operand[first, b][0][:].bitcast(FP8X4),
+                    rhs_scale=h_operand[first, b][1][:],
+                    start=(b == order[0]),
+                    stop=(b == order[1]),
+                )
 
-        def evacuate(c, k):
-            y_sb[c, k] = held([P, 2, CHUNK], F32, "y_sb%d%d" % (c, k))
-            nc.scalar.copy(y_sb[c, k][:], y_bank[c, k][:])
+        def mix_chunk(first, first_bank):
+            banks = [in_bank([P, 2, CHUNK], "bank_y%d_%d" % (first, k), first_bank + k) for k in range(2)]
+            for i in range(PACK):
+                mix(first, i, banks[i // 2][:, i % 2, :], (1, 0))
+            return banks
 
         def put(i, values, first, count):
             nc.vector.tensor_tensor(
@@ -340,73 +315,77 @@ def tile_list_pen_biomass_cues_kernel(
                 ALU.mult,
             )
 
-        def scatter(c, k):
-            for u in range(2):
-                put(2 * k + u, y_sb[c, k][:, u, :], CHUNK * c, CHUNK)
+        def evacuate(bank, tile):
+            nc.scalar.copy(tile[:], bank[:])
+            return tile
 
-        def late_scatter(u, slot, at):
-            y_late = placed([P, CHUNK], F32, "y_late%d" % u, slot, at)
-            nc.scalar.copy(y_late[:], y_bank[1, 1][:, u, :])
-            put(2 + u, y_late[:], CHUNK, CHUNK)
+        def first_sigmoids(c, b, steps):
+            sigmoid[CHUNK * c, b] = placed([P, PACK, CHUNK], F32, "sigmoid%d%d" % (c, b), FIRST_SIGMOIDS + 8 * c + 4 * b)
+            for t in range(0, PACK, steps):
+                nc.scalar.activation(
+                    sigmoid[CHUNK * c, b][:, t : t + steps, :],
+                    gate[b, 0][:, t : t + steps, CHUNK * c : CHUNK * (c + 1)],
+                    ACT.Sigmoid,
+                    scale=-1.0,
+                )
 
-        for b in range(2):
-            sigmoids(0, b)
-            products(0, b)
-        for b in range(2):
-            interleave(0, b)
-        for b in range(2):
-            quantise_h(0, b)
-        mix(0, HIGH_BANKS, (1, 0))
-        for b in range(2):
-            sigmoids(1, b)
-            products(1, b)
-        evacuate(0, 0)
-        evacuate(0, 1)
-        for b in range(2):
-            interleave(1, b)
-            quantise_h(1, b)
+        sum_bank = {}
 
+        def summed(t, bank):
+            sum_bank[t] = in_bank([P, HALF], "bank_sum%d" % t, bank)
+            wb_passes(sum_bank[t], 1, t, 1, False)
+            wa_passes(sum_bank[t], 1, t, 1, False)
+
+        for t in range(2):
+            summed(t, HIGH_BANKS + 2 + t)
+        for b in range(2):
+            first_sigmoids(0, b, 1)
+            products(0, CHUNK, b)
+        gate[0, 1] = placed([P, PACK, HALF], F32, "gate01", WA[0, 1])
         for t in range(PACK):
-            bank = in_bank([P, HALF], "bank_sum%d" % t, LOW_BANKS + t)
-            wb_passes(bank, 1, t, 1, False)
-            wa_passes(bank, 1, t, 1, False)
-            gate[1, t, 1] = placed([P, HALF], F32, "gate1%d1" % t, WA_00, BANK * t)
-            nc.scalar.activation(gate[1, t, 1][:], bank[:], ACT.Sigmoid, scale=-1.0)
+            nc.scalar.copy(gate[0, 1][:, t, :], b_bank[0, t, 1][:])
+        for b in range(2):
+            interleave(0, CHUNK, b, nc.vector.tensor_copy)
+        for b in range(2):
+            quantise_h(0, CHUNK, b)
+        banks = mix_chunk(0, HIGH_BANKS)
+        for b in range(2):
+            first_sigmoids(1, b, PACK)
+            products(CHUNK, CHUNK, b)
+        first_y = [evacuate(banks[k], held([P, 2, CHUNK], F32, "first_y%d" % k)) for k in range(2)]
+        difference(0, 1, LOW_BANKS)
+        for t in range(2, PACK):
+            summed(t, HIGH_BANKS + t - 2)
+        for b in range(2):
+            interleave(CHUNK, CHUNK, b, nc.scalar.copy)
+        for i in range(PACK):
+            put(i, first_y[i // 2][:, i % 2, :], 0, CHUNK)
+        for b in range(2):
+            quantise_h(CHUNK, CHUNK, b)
+        banks = mix_chunk(CHUNK, LOW_BANKS)
 
-        scatter(0, 0)
-        scatter(0, 1)
-        exponentials(0, 1)
-        for c in (2, 3):
-            products(c, 1)
-        difference(0, 1)
-        mix(1, LOW_BANKS, (1, 0))
-        evacuate(1, 0)
-        scatter(1, 0)
-        for c in (2, 3):
-            interleave(c, 1)
-            quantise_h(c, 1)
-        for c in (2, 3):
-            sigmoids(c, 0)
-            products(c, 0)
-        for c in (2, 3):
-            interleave(c, 0)
-        quantise_h(2, 0)
-        mix(2, HIGH_BANKS, (0, 1))
-        quantise_h(3, 0)
+        sigmoid[HALF, 1] = placed([P, PACK, HALF], F32, "sigmoid_sum", FIRST_GATE)
+        for t in range(PACK):
+            nc.scalar.activation(sigmoid[HALF, 1][:, t, :], sum_bank[t][:], ACT.Sigmoid, scale=-1.0)
+        sigmoid[HALF, 0] = gate[0, 1]
+        nc.scalar.activation(gate[0, 1][:], gate[0, 1][:], ACT.Sigmoid, scale=-1.0)
+        for b in (1, 0):
+            products(HALF, HALF, b)
 
-        late_scatter(0, WA_01, BANK * (PACK - 1))
-        late_scatter(1, TABLE_0, last_rows_at)
-        evacuate(2, 0)
-        mix(3, HIGH_BANKS + 2, (0, 1))
-        evacuate(3, 0)
-        for c in (2, 3):
-            nc.scalar.copy(y_last[:, :, columns(c)], y_bank[c, 1][:])
-
-        for c in (2, 3):
-            scatter(c, 0)
+        second_y = evacuate(banks[0], placed([P, 2, CHUNK], F32, "second_y0", LAST_EXP))
+        for b in (1, 0):
+            interleave(HALF, HALF, b, nc.scalar.copy)
         for u in range(2):
-            put(2 + u, y_last[:, u, :], HALF, HALF)
+            put(u, second_y[:, u, :], CHUNK, CHUNK)
+        for b in (1, 0):
+            quantise_h(HALF, HALF, b)
+        second_y = evacuate(banks[1], placed([P, 2, CHUNK], F32, "second_y1", LAST_ROWS))
+        for u in range(2):
+            put(2 + u, second_y[:, u, :], CHUNK, CHUNK)
 
         out_rows = out.rearrange("(p i) t -> i p t", i=PACK)
         for i in range(PACK):
+            bank = in_bank([P, HALF], "bank_last%d" % i, HIGH_BANKS + i)
+            mix(HALF, i, bank[:], (0, 1))
+            put(i, evacuate(bank, held([P, HALF], F32, "last_y%d" % i))[:], HALF, HALF)
             nc.sync.dma_start(out_rows[i], cells[i][:])

@@ -29,7 +29,7 @@ TABLE = (0, 8)
 WA = {(0, 0): 16, (1, 0): 26, (0, 1): 34, (1, 1): 42}
 LATE_WORDS = 50
 FIRST_SIGMOIDS = 54
-LAST_EXP, FIRST_GATE, LAST_ROWS = 70, 78, 86
+LAST_EXP, FIRST_GATE, LAST_ROWS, FIRST_EXP = 70, 78, 86, 90
 LOW_BANKS, HIGH_BANKS = 0, 4
 
 
@@ -192,9 +192,10 @@ def tile_list_pen_biomass_cues_kernel(
                 in_=wa_grouped[a, b][:].rearrange("p t m i -> p (t m i)"),
             )
 
-        exp_b = {key: held([P, PACK, HALF], F32, "exp_b%d%d" % key) for key in ((0, 0), (1, 0), (0, 1))}
+        exp_b = {(b, 0): placed([P, PACK, HALF], F32, "exp_b%d0" % b, FIRST_EXP + 8 * b) for b in range(2)}
+        exp_b[0, 1] = placed([P, PACK, HALF], F32, "exp_b01", TABLE[0])
         exp_b[1, 1] = placed([P, PACK, HALF], F32, "exp_b11", LAST_EXP)
-        gate = {(0, 0): placed([P, PACK, HALF], F32, "gate00", FIRST_GATE), (1, 0): held([P, PACK, HALF], F32, "gate10")}
+        gate = {(0, 0): placed([P, PACK, HALF], F32, "gate00", FIRST_GATE), (1, 0): placed([P, PACK, HALF], F32, "gate10", TABLE[1])}
         b_bank = {}
 
         b_order = [(0, t, 0) for t in range(PACK)]
@@ -222,9 +223,6 @@ def tile_list_pen_biomass_cues_kernel(
         round_wa(1, 1)
         quantise_wa(0, 1)
         quantise_wa(1, 1)
-        for a in (1, 0):
-            cells[2 + a] = placed([P, T2], F32, "cells%d" % (2 + a), TABLE[a])
-            nc.vector.memset(cells[2 + a][:].bitcast(I32), 0)
         difference(0, 0, HIGH_BANKS)
 
         wc_raw = placed([P, 2, N], I32, "wc_raw", WA[0, 0])
@@ -352,6 +350,8 @@ def tile_list_pen_biomass_cues_kernel(
         for b in range(2):
             first_sigmoids(1, b, PACK)
             products(CHUNK, CHUNK, b)
+            cells[2 + b] = placed([P, T2], F32, "cells%d" % (2 + b), FIRST_EXP + 8 * b)
+            nc.gpsimd.memset(cells[2 + b][:].bitcast(I32), 0)
         first_y = [evacuate(banks[k], held([P, 2, CHUNK], F32, "first_y%d" % k)) for k in range(2)]
         difference(0, 1, LOW_BANKS)
         for t in range(2, PACK):

@@ -29,8 +29,8 @@ TABLE = (0, 8)
 WA = {(0, 0): 16, (1, 0): 26, (0, 1): 34, (1, 1): 42}
 LATE_WORDS = 50
 FIRST_SIGMOIDS = 54
-LAST_EXP, FIRST_GATE, LAST_ROWS, FIRST_EXP = 70, 78, 86, 90
-LOW_BANKS, HIGH_BANKS = 0, 4
+FIRST_GATE, LAST_ROWS, FIRST_EXP, LAST_GROUPED = 70, 78, 82, 98
+HIGH_BANKS, LOW_BANKS = 0, 4
 
 
 def tile_list_pen_biomass_cues_kernel(
@@ -163,24 +163,29 @@ def tile_list_pen_biomass_cues_kernel(
         wa_grouped, wa_codes, wa_plane = {}, {}, {}
 
         def wa_passes(bank, b, t, half, start):
-            for a in (1, 0):
+            for a in range(2):
                 nc.tensor.matmul_mx(
                     out=bank[:],
                     lhsT=wa_codes[a, b][:, P * t : P * (t + 1)].bitcast(FP8X4),
                     lhsT_scale=wa_plane[a, b][:, P * t : P * (t + 1)],
-                    start=(start and a == 1),
-                    stop=(a == 0),
+                    start=(start and a == 0),
+                    stop=(a == 1),
                     **table_operand(a, half),
                 )
 
         def round_wa(a, b):
-            wa_grouped[a, b] = held([P, PACK, P, PACK], BF16, "wa_grouped%d%d" % (a, b))
-            nc.vector.tensor_scalar(
+            name = "wa_grouped%d%d" % (a, b)
+            if b == 0:
+                wa_grouped[a, b] = held([P, PACK, P, PACK], BF16, name)
+            else:
+                wa_grouped[a, b] = placed([P, PACK, P, PACK], BF16, name, LAST_GROUPED)
+            (nc.gpsimd if (a, b) == (1, 1) else nc.vector).tensor_scalar(
                 out=wa_grouped[a, b][:].rearrange("p t m i -> p m t i"),
                 in0=wa_raw[a, b][:].rearrange("p i (m t) -> p m t i", t=PACK),
                 scalar1=-1.0,
-                scalar2=None,
+                scalar2=0.0,
                 op0=ALU.mult,
+                op1=ALU.add,
             )
 
         def quantise_wa(a, b):
@@ -194,36 +199,37 @@ def tile_list_pen_biomass_cues_kernel(
 
         exp_b = {(b, 0): placed([P, PACK, HALF], F32, "exp_b%d0" % b, FIRST_EXP + 8 * b) for b in range(2)}
         exp_b[0, 1] = placed([P, PACK, HALF], F32, "exp_b01", TABLE[0])
-        exp_b[1, 1] = placed([P, PACK, HALF], F32, "exp_b11", LAST_EXP)
         gate = {(0, 0): placed([P, PACK, HALF], F32, "gate00", FIRST_GATE), (1, 0): placed([P, PACK, HALF], F32, "gate10", TABLE[1])}
         b_bank = {}
 
-        b_order = [(0, t, 0) for t in range(PACK)]
-        for t in range(PACK):
-            b_order.extend([(1, t, 0), (1, t, 1)])
-        b_order.extend([(0, t, 1) for t in range(PACK)])
-        for n, (b, t, half) in enumerate(b_order):
-            b_bank[b, t, half] = in_bank([P, HALF], "bank_b%d%d%d" % (b, t, half), LOW_BANKS + n % 4)
-            wb_passes(b_bank[b, t, half], b, t, half, True)
-            nc.scalar.activation(exp_b[b, half][:, t, :], b_bank[b, t, half][:], ACT.Exp)
-            if half == 0:
-                nc.scalar.copy(gate[b, half][:, t, :], b_bank[b, t, half][:])
+        def exponentials(b, half, first_bank):
+            for t in range(PACK):
+                b_bank[b, t, half] = in_bank([P, HALF], "bank_b%d%d%d" % (b, t, half), first_bank + t)
+                wb_passes(b_bank[b, t, half], b, t, half, True)
+                nc.scalar.activation(exp_b[b, half][:, t, :], b_bank[b, t, half][:], ACT.Exp)
+                if half == 0:
+                    nc.scalar.copy(gate[b, half][:, t, :], b_bank[b, t, half][:])
 
-        def difference(b, half, first_bank):
+
+        def difference(b, half, first_bank, into):
             for t in range(PACK):
                 bank = in_bank([P, HALF], "bank_a%d%d%d" % (b, t, half), first_bank + t)
                 wa_passes(bank, b, t, half, True)
-                nc.vector.tensor_tensor(gate[b, half][:, t, :], bank[:], gate[b, half][:, t, :], ALU.add)
+                nc.vector.tensor_tensor(into[:, t, :], bank[:], gate[b, half][:, t, :], ALU.add)
+            gate[b, half] = into
 
+        exponentials(0, 0, HIGH_BANKS)
+        exponentials(1, 0, LOW_BANKS)
         round_wa(0, 0)
         round_wa(1, 0)
         quantise_wa(0, 0)
         quantise_wa(1, 0)
         round_wa(0, 1)
-        round_wa(1, 1)
         quantise_wa(0, 1)
+        difference(0, 0, HIGH_BANKS, placed([P, PACK, HALF], F32, "difference00", WA[0, 1]))
+        exponentials(0, 1, LOW_BANKS)
+        round_wa(1, 1)
         quantise_wa(1, 1)
-        difference(0, 0, HIGH_BANKS)
 
         wc_raw = placed([P, 2, N], I32, "wc_raw", WA[0, 0])
         wgo_sb = placed([P, S], F32, "wgo_sb", WA[0, 0] + 4)
@@ -238,7 +244,7 @@ def tile_list_pen_biomass_cues_kernel(
             )
         nc.sync.dma_start(wgo_sb[:], wgo)
 
-        difference(1, 0, HIGH_BANKS)
+        difference(1, 0, HIGH_BANKS, gate[1, 0])
 
         wc_codes = held([P, 2, N], I32, "wc_codes")
         wc_plane = held([P, N], U8, "wc_plane")
@@ -258,7 +264,7 @@ def tile_list_pen_biomass_cues_kernel(
 
         def products(first, count, b):
             name = "h_rows%d_%d" % (first, b)
-            if (first, b) == (HALF, 0):
+            if (first, b) == (HALF, 1):
                 h_rows[first, b] = placed([P, PACK, count], BF16, name, LAST_ROWS)
             else:
                 h_rows[first, b] = held([P, PACK, count], BF16, name)
@@ -339,9 +345,6 @@ def tile_list_pen_biomass_cues_kernel(
         for b in range(2):
             first_sigmoids(0, b, 1)
             products(0, CHUNK, b)
-        gate[0, 1] = placed([P, PACK, HALF], F32, "gate01", WA[0, 1])
-        for t in range(PACK):
-            nc.scalar.copy(gate[0, 1][:, t, :], b_bank[0, t, 1][:])
         for b in range(2):
             interleave(0, CHUNK, b, nc.vector.tensor_copy)
         for b in range(2):
@@ -352,32 +355,37 @@ def tile_list_pen_biomass_cues_kernel(
             products(CHUNK, CHUNK, b)
             cells[2 + b] = placed([P, T2], F32, "cells%d" % (2 + b), FIRST_EXP + 8 * b)
             nc.gpsimd.memset(cells[2 + b][:].bitcast(I32), 0)
+        gate[0, 1] = placed([P, PACK, HALF], F32, "gate01", TABLE[1])
+        for t in range(PACK):
+            nc.scalar.copy(gate[0, 1][:, t, :], b_bank[0, t, 1][:])
         first_y = [evacuate(banks[k], held([P, 2, CHUNK], F32, "first_y%d" % k)) for k in range(2)]
-        difference(0, 1, LOW_BANKS)
+        difference(0, 1, LOW_BANKS, gate[0, 1])
         for t in range(2, PACK):
             summed(t, HIGH_BANKS + t - 2)
+        sigmoid[HALF, 1] = placed([P, PACK, HALF], F32, "sigmoid_sum", WA[0, 1])
+        for t in range(PACK):
+            nc.scalar.activation(sigmoid[HALF, 1][:, t, :], sum_bank[t][:], ACT.Sigmoid, scale=-1.0)
         for b in range(2):
             interleave(CHUNK, CHUNK, b, nc.scalar.copy)
         for i in range(PACK):
             put(i, first_y[i // 2][:, i % 2, :], 0, CHUNK)
         for b in range(2):
             quantise_h(CHUNK, CHUNK, b)
+        sigmoid[HALF, 0] = placed([P, PACK, HALF], F32, "sigmoid_last", FIRST_GATE)
+        nc.scalar.activation(sigmoid[HALF, 0][:], gate[0, 1][:], ACT.Sigmoid, scale=-1.0)
+        products(HALF, HALF, 0)
+
+        exp_b[1, 1] = placed([P, PACK, HALF], F32, "exp_b11", TABLE[1])
+        exponentials(1, 1, LOW_BANKS)
         banks = mix_chunk(CHUNK, LOW_BANKS)
+        products(HALF, HALF, 1)
 
-        sigmoid[HALF, 1] = placed([P, PACK, HALF], F32, "sigmoid_sum", FIRST_GATE)
-        for t in range(PACK):
-            nc.scalar.activation(sigmoid[HALF, 1][:, t, :], sum_bank[t][:], ACT.Sigmoid, scale=-1.0)
-        sigmoid[HALF, 0] = gate[0, 1]
-        nc.scalar.activation(gate[0, 1][:], gate[0, 1][:], ACT.Sigmoid, scale=-1.0)
-        for b in (1, 0):
-            products(HALF, HALF, b)
-
-        second_y = evacuate(banks[0], placed([P, 2, CHUNK], F32, "second_y0", LAST_EXP))
-        for b in (1, 0):
+        second_y = evacuate(banks[0], held([P, 2, CHUNK], F32, "second_y0"))
+        for b in range(2):
             interleave(HALF, HALF, b, nc.scalar.copy)
         for u in range(2):
             put(u, second_y[:, u, :], CHUNK, CHUNK)
-        for b in (1, 0):
+        for b in range(2):
             quantise_h(HALF, HALF, b)
         second_y = evacuate(banks[1], placed([P, 2, CHUNK], F32, "second_y1", LAST_ROWS))
         for u in range(2):
@@ -386,6 +394,6 @@ def tile_list_pen_biomass_cues_kernel(
         out_rows = out.rearrange("(p i) t -> i p t", i=PACK)
         for i in range(PACK):
             bank = in_bank([P, HALF], "bank_last%d" % i, HIGH_BANKS + i)
-            mix(HALF, i, bank[:], (0, 1))
+            mix(HALF, i, bank[:], (1, 0))
             put(i, evacuate(bank, held([P, HALF], F32, "last_y%d" % i))[:], HALF, HALF)
             nc.sync.dma_start(out_rows[i], cells[i][:])

@@ -24,13 +24,15 @@ CHUNK = 256
 LIST = 16
 BANK = 2048
 KIB = 1024
+ON_GPSIMD = 80
 
 TABLE = (0, 8)
 WA = {(0, 0): 16, (1, 0): 26, (0, 1): 34, (1, 1): 42}
 LATE_WORDS = 50
 FIRST_SIGMOIDS = 54
-FIRST_GATE, LAST_ROWS, FIRST_EXP, LAST_GROUPED = 70, 78, 82, 98
-HIGH_BANKS, LOW_BANKS = 0, 4
+FIRST_GATE, LAST_ROWS, FIRST_EXP, LAST_GROUPED = 70, 78, 84, 100
+THIRD_CELLS, FIRST_Y = 104, 112
+TURNING, HOLDING, CROSSED = (0, 1, 2, 3), (4, 5, 6, 7), (2, 3, 0, 1)
 
 
 def tile_list_pen_biomass_cues_kernel(
@@ -121,8 +123,8 @@ def tile_list_pen_biomass_cues_kernel(
             entries = offs_sb[:, HALF * half // LIST : HALF * (half + 1) // LIST]
             nc.vector.tensor_copy(picked[a, half][:], tab_win[a][:].bitcast(U32).indirect(entries))
 
-        wb_codes = [placed([P, 2, 2 * PASS], U8, "wb_codes0", FIRST_SIGMOIDS + 3), held([P, 2, 2 * PASS], U8, "wb_codes1")]
-        wb_plane = [placed([P, 2, PASS], U8, "wb_plane0", FIRST_SIGMOIDS + 11.5), held([P, 2, PASS], U8, "wb_plane1")]
+        wb_codes = [held([P, 2, 2 * PASS], U8, "wb_codes%d" % b) for b in range(2)]
+        wb_plane = [held([P, 2, PASS], U8, "wb_plane%d" % b) for b in range(2)]
 
         def deal_wb(b):
             nc.scalar.copy(
@@ -179,14 +181,16 @@ def tile_list_pen_biomass_cues_kernel(
                 wa_grouped[a, b] = held([P, PACK, P, PACK], BF16, name)
             else:
                 wa_grouped[a, b] = placed([P, PACK, P, PACK], BF16, name, LAST_GROUPED)
-            (nc.gpsimd if (a, b) == (1, 1) else nc.vector).tensor_scalar(
-                out=wa_grouped[a, b][:].rearrange("p t m i -> p m t i"),
-                in0=wa_raw[a, b][:].rearrange("p i (m t) -> p m t i", t=PACK),
-                scalar1=-1.0,
-                scalar2=0.0,
-                op0=ALU.mult,
-                op1=ALU.add,
-            )
+            shares = ((nc.gpsimd, 0, ON_GPSIMD), (nc.vector, ON_GPSIMD, P)) if (a, b) == (1, 1) else ((nc.vector, 0, P),)
+            for engine, first, last in shares:
+                engine.tensor_scalar(
+                    out=wa_grouped[a, b][:].rearrange("p t m i -> p m t i")[:, first:last],
+                    in0=wa_raw[a, b][:].rearrange("p i (m t) -> p m t i", t=PACK)[:, first:last],
+                    scalar1=-1.0,
+                    scalar2=0.0,
+                    op0=ALU.mult,
+                    op1=ALU.add,
+                )
 
         def quantise_wa(a, b):
             wa_codes[a, b] = held([P, HALF], U32, "wa_codes%d%d" % (a, b))
@@ -198,36 +202,38 @@ def tile_list_pen_biomass_cues_kernel(
             )
 
         exp_b = {(b, 0): placed([P, PACK, HALF], F32, "exp_b%d0" % b, FIRST_EXP + 8 * b) for b in range(2)}
-        exp_b[0, 1] = placed([P, PACK, HALF], F32, "exp_b01", TABLE[0])
         gate = {(0, 0): placed([P, PACK, HALF], F32, "gate00", FIRST_GATE), (1, 0): placed([P, PACK, HALF], F32, "gate10", TABLE[1])}
         b_bank = {}
 
-        def exponentials(b, half, first_bank):
-            for t in range(PACK):
-                b_bank[b, t, half] = in_bank([P, HALF], "bank_b%d%d%d" % (b, t, half), first_bank + t)
-                wb_passes(b_bank[b, t, half], b, t, half, True)
-                nc.scalar.activation(exp_b[b, half][:, t, :], b_bank[b, t, half][:], ACT.Exp)
-                if half == 0:
-                    nc.scalar.copy(gate[b, half][:, t, :], b_bank[b, t, half][:])
+        def b_sum(b, t, half, bank):
+            b_bank[b, t, half] = in_bank([P, HALF], "bank_b%d%d%d" % (b, t, half), bank)
+            wb_passes(b_bank[b, t, half], b, t, half, True)
 
+        def exponential(b, t, half):
+            nc.scalar.activation(exp_b[b, half][:, t, :], b_bank[b, t, half][:], ACT.Exp)
 
-        def difference(b, half, first_bank, into):
+        def first_phase(b, banks):
             for t in range(PACK):
-                bank = in_bank([P, HALF], "bank_a%d%d%d" % (b, t, half), first_bank + t)
+                b_sum(b, t, 0, banks[t])
+                exponential(b, t, 0)
+                nc.scalar.copy(gate[b, 0][:, t, :], b_bank[b, t, 0][:])
+
+        def difference(b, half, banks, into):
+            for t in range(PACK):
+                bank = in_bank([P, HALF], "bank_a%d%d%d" % (b, t, half), banks[t])
                 wa_passes(bank, b, t, half, True)
                 nc.vector.tensor_tensor(into[:, t, :], bank[:], gate[b, half][:, t, :], ALU.add)
             gate[b, half] = into
 
-        exponentials(0, 0, HIGH_BANKS)
-        exponentials(1, 0, LOW_BANKS)
+        first_phase(0, TURNING)
+        first_phase(1, HOLDING)
         round_wa(0, 0)
         round_wa(1, 0)
         quantise_wa(0, 0)
         quantise_wa(1, 0)
         round_wa(0, 1)
         quantise_wa(0, 1)
-        difference(0, 0, HIGH_BANKS, placed([P, PACK, HALF], F32, "difference00", WA[0, 1]))
-        exponentials(0, 1, LOW_BANKS)
+        difference(0, 0, TURNING, placed([P, PACK, HALF], F32, "difference00", WA[0, 1]))
         round_wa(1, 1)
         quantise_wa(1, 1)
 
@@ -244,7 +250,18 @@ def tile_list_pen_biomass_cues_kernel(
             )
         nc.sync.dma_start(wgo_sb[:], wgo)
 
-        difference(1, 0, HIGH_BANKS, gate[1, 0])
+        difference(1, 0, HOLDING, gate[1, 0])
+        sum_bank = {}
+
+        def summed(t):
+            sum_bank[t] = in_bank([P, HALF], "bank_sum%d" % t, TURNING[t])
+            wb_passes(sum_bank[t], 1, t, 1, False)
+            wa_passes(sum_bank[t], 1, t, 1, False)
+
+        for t in range(2):
+            summed(t)
+        for t in range(PACK):
+            b_sum(0, t, 1, HOLDING[t])
 
         wc_codes = held([P, 2, N], I32, "wc_codes")
         wc_plane = held([P, N], U8, "wc_plane")
@@ -279,14 +296,37 @@ def tile_list_pen_biomass_cues_kernel(
                 )
 
         def interleave(first, count, b, copy):
-            h_grouped[first, b] = held([P, count, PACK], BF16, "h_grouped%d_%d" % (first, b))
+            name = "h_grouped%d_%d" % (first, b)
+            if (first, b) == (0, 1):
+                h_grouped[first, b] = placed([P, count, PACK], BF16, name, THIRD_CELLS)
+            else:
+                h_grouped[first, b] = held([P, count, PACK], BF16, name)
             copy(
                 h_grouped[first, b][:].rearrange("p (j e) t -> p j t e", e=4),
                 h_rows[first, b][:].rearrange("p t (j e) -> p j t e", e=4),
             )
 
+        def interleave_second(b):
+            h_grouped[CHUNK, b] = placed([P, CHUNK, PACK], BF16, "h_grouped_second%d" % b, FIRST_SIGMOIDS + 12 + 2 * b)
+            nc.gpsimd.tensor_scalar(
+                out=h_grouped[CHUNK, b][:],
+                in0=h_rows[CHUNK, b][:].rearrange("p t j -> p j t"),
+                scalar1=1.0,
+                scalar2=0.0,
+                op0=ALU.mult,
+                op1=ALU.add,
+            )
+
+        def clear_late(i, kib):
+            cells[i] = placed([P, T2], F32, "cells%d" % i, kib)
+            nc.gpsimd.memset(cells[i][:].bitcast(I32), 0)
+
         def quantise_h(first, count, b):
-            codes = held([P, count], U32, "h_codes%d_%d" % (first, b))
+            name = "h_codes%d_%d" % (first, b)
+            if first == CHUNK:
+                codes = placed([P, count], U32, name, FIRST_Y + b)
+            else:
+                codes = held([P, count], U32, name)
             plane = held([P, count], U8, "h_plane%d_%d" % (first, b))
             nc.vector.quantize_mx(
                 out=codes[:].bitcast(FP8X4), scales=plane[:], in_=h_grouped[first, b][:].rearrange("p j t -> p (j t)")
@@ -333,51 +373,56 @@ def tile_list_pen_biomass_cues_kernel(
                     scale=-1.0,
                 )
 
-        sum_bank = {}
-
-        def summed(t, bank):
-            sum_bank[t] = in_bank([P, HALF], "bank_sum%d" % t, bank)
-            wb_passes(sum_bank[t], 1, t, 1, False)
-            wa_passes(sum_bank[t], 1, t, 1, False)
-
-        for t in range(2):
-            summed(t, HIGH_BANKS + 2 + t)
         for b in range(2):
             first_sigmoids(0, b, 1)
             products(0, CHUNK, b)
+        sigmoid[HALF, 1] = placed([P, PACK, HALF], F32, "sigmoid_sum", WA[1, 1])
+
+        def summed_sigmoid(t):
+            nc.scalar.activation(sigmoid[HALF, 1][:, t, :], sum_bank[t][:], ACT.Sigmoid, scale=-1.0)
+
+        for t in range(2):
+            summed_sigmoid(t)
         for b in range(2):
             interleave(0, CHUNK, b, nc.vector.tensor_copy)
         for b in range(2):
             quantise_h(0, CHUNK, b)
-        banks = mix_chunk(0, HIGH_BANKS)
+        clear_late(2, THIRD_CELLS)
         for b in range(2):
             first_sigmoids(1, b, PACK)
             products(CHUNK, CHUNK, b)
-            cells[2 + b] = placed([P, T2], F32, "cells%d" % (2 + b), FIRST_EXP + 8 * b)
-            nc.gpsimd.memset(cells[2 + b][:].bitcast(I32), 0)
+        interleave_second(1)
+        clear_late(3, FIRST_EXP + 8)
         gate[0, 1] = placed([P, PACK, HALF], F32, "gate01", TABLE[1])
-        for t in range(PACK):
-            nc.scalar.copy(gate[0, 1][:, t, :], b_bank[0, t, 1][:])
-        first_y = [evacuate(banks[k], held([P, 2, CHUNK], F32, "first_y%d" % k)) for k in range(2)]
-        difference(0, 1, LOW_BANKS, gate[0, 1])
+        banks = mix_chunk(0, TURNING[0])
+        first_y = []
+        for k in range(2):
+            for t in (2 * k, 2 * k + 1):
+                nc.scalar.copy(gate[0, 1][:, t, :], b_bank[0, t, 1][:])
+            if k == 0:
+                first_y = [evacuate(banks[n], placed([P, 2, CHUNK], F32, "first_y%d" % n, FIRST_Y + 2 * n)) for n in range(2)]
+        difference(0, 1, CROSSED, gate[0, 1])
         for t in range(2, PACK):
-            summed(t, HIGH_BANKS + t - 2)
-        sigmoid[HALF, 1] = placed([P, PACK, HALF], F32, "sigmoid_sum", WA[0, 1])
-        for t in range(PACK):
-            nc.scalar.activation(sigmoid[HALF, 1][:, t, :], sum_bank[t][:], ACT.Sigmoid, scale=-1.0)
-        for b in range(2):
-            interleave(CHUNK, CHUNK, b, nc.scalar.copy)
+            summed(t)
+        interleave(CHUNK, CHUNK, 0, nc.scalar.copy)
         for i in range(PACK):
             put(i, first_y[i // 2][:, i % 2, :], 0, CHUNK)
         for b in range(2):
             quantise_h(CHUNK, CHUNK, b)
         sigmoid[HALF, 0] = placed([P, PACK, HALF], F32, "sigmoid_last", FIRST_GATE)
         nc.scalar.activation(sigmoid[HALF, 0][:], gate[0, 1][:], ACT.Sigmoid, scale=-1.0)
-        products(HALF, HALF, 0)
+        for t in range(2, PACK):
+            summed_sigmoid(t)
 
-        exp_b[1, 1] = placed([P, PACK, HALF], F32, "exp_b11", TABLE[1])
-        exponentials(1, 1, LOW_BANKS)
-        banks = mix_chunk(CHUNK, LOW_BANKS)
+        exp_b[0, 1] = placed([P, PACK, HALF], F32, "exp_b01", TABLE[1] - 4)
+        exp_b[1, 1] = placed([P, PACK, HALF], F32, "exp_b11", TABLE[1] + 4)
+        for t in range(PACK):
+            exponential(0, t, 1)
+        products(HALF, HALF, 0)
+        for t in range(PACK):
+            b_sum(1, t, 1, TURNING[t])
+            exponential(1, t, 1)
+        banks = mix_chunk(CHUNK, HOLDING[0])
         products(HALF, HALF, 1)
 
         second_y = evacuate(banks[0], held([P, 2, CHUNK], F32, "second_y0"))
@@ -393,7 +438,7 @@ def tile_list_pen_biomass_cues_kernel(
 
         out_rows = out.rearrange("(p i) t -> i p t", i=PACK)
         for i in range(PACK):
-            bank = in_bank([P, HALF], "bank_last%d" % i, HIGH_BANKS + i)
+            bank = in_bank([P, HALF], "bank_last%d" % i, (HOLDING[2:] + TURNING)[i])
             mix(HALF, i, bank[:], (1, 0))
             put(i, evacuate(bank, held([P, HALF], F32, "last_y%d" % i))[:], HALF, HALF)
             nc.sync.dma_start(out_rows[i], cells[i][:])

@@ -151,27 +151,27 @@ def tile_list_pen_biomass_cues_kernel(
                 rhs=picked[a, half][:].bitcast(FP8X4), rhs_scale=tab_plane[:, a, HALF * half : HALF * (half + 1)]
             )
 
-        def wb_passes(bank, b, t, half, stop):
+        def wb_passes(bank, b, t, half, start):
             for a in range(2):
                 nc.tensor.matmul_mx(
                     out=bank[:],
                     lhsT=wb_codes[b][:, a, 2 * P * t : 2 * P * (t + 1)].bitcast(FP4X4),
                     lhsT_scale=wb_plane[b][:, a, P * t : P * (t + 1)],
-                    start=(a == 0),
-                    stop=(stop and a == 1),
+                    start=(start and a == 0),
+                    stop=(a == 1),
                     **table_operand(a, half),
                 )
 
         wa_grouped, wa_codes, wa_plane = {}, {}, {}
 
-        def wa_passes(bank, b, t, half, start):
-            for a in range(2):
+        def wa_passes(bank, b, t, half, order, stop):
+            for a in order:
                 nc.tensor.matmul_mx(
                     out=bank[:],
                     lhsT=wa_codes[a, b][:, P * t : P * (t + 1)].bitcast(FP8X4),
                     lhsT_scale=wa_plane[a, b][:, P * t : P * (t + 1)],
-                    start=(start and a == 0),
-                    stop=(a == 1),
+                    start=(a == order[0]),
+                    stop=(stop and a == order[1]),
                     **table_operand(a, half),
                 )
 
@@ -181,11 +181,13 @@ def tile_list_pen_biomass_cues_kernel(
                 wa_grouped[a, b] = held([P, PACK, P, PACK], BF16, name)
             else:
                 wa_grouped[a, b] = placed([P, PACK, P, PACK], BF16, name, LAST_GROUPED)
-            shares = ((nc.gpsimd, 0, ON_GPSIMD), (nc.vector, ON_GPSIMD, P)) if (a, b) == (1, 1) else ((nc.vector, 0, P),)
-            for engine, first, last in shares:
+            shares = [(nc.vector, "p m i t", 0, P)]
+            if (a, b) == (1, 1):
+                shares = [(nc.gpsimd, "p m t i", 0, ON_GPSIMD), (nc.vector, "p m i t", ON_GPSIMD, P)]
+            for engine, walk, first, last in shares:
                 engine.tensor_scalar(
-                    out=wa_grouped[a, b][:].rearrange("p t m i -> p m t i")[:, first:last],
-                    in0=wa_raw[a, b][:].rearrange("p i (m t) -> p m t i", t=PACK)[:, first:last],
+                    out=wa_grouped[a, b][:].rearrange("p t m i -> " + walk)[:, first:last],
+                    in0=wa_raw[a, b][:].rearrange("p i (m t) -> " + walk, t=PACK)[:, first:last],
                     scalar1=-1.0,
                     scalar2=0.0,
                     op0=ALU.mult,
@@ -221,7 +223,7 @@ def tile_list_pen_biomass_cues_kernel(
         def difference(b, half, banks, into):
             for t in range(PACK):
                 bank = in_bank([P, HALF], "bank_a%d%d%d" % (b, t, half), banks[t])
-                wa_passes(bank, b, t, half, True)
+                wa_passes(bank, b, t, half, (0, 1), True)
                 nc.vector.tensor_tensor(into[:, t, :], bank[:], gate[b, half][:, t, :], ALU.add)
             gate[b, half] = into
 
@@ -255,8 +257,8 @@ def tile_list_pen_biomass_cues_kernel(
 
         def summed(t):
             sum_bank[t] = in_bank([P, HALF], "bank_sum%d" % t, TURNING[t])
+            wa_passes(sum_bank[t], 1, t, 1, (1, 0), False)
             wb_passes(sum_bank[t], 1, t, 1, False)
-            wa_passes(sum_bank[t], 1, t, 1, False)
 
         for t in range(2):
             summed(t)

@@ -20,19 +20,16 @@ P = 128
 PACK = 4
 PASS = P * PACK
 HALF = 512
-CHUNK = 256
 LIST = 16
 BANK = 2048
 KIB = 1024
-ON_GPSIMD = 80
 
 TABLE = (0, 8)
 WA = {(0, 0): 16, (1, 0): 26, (0, 1): 34, (1, 1): 42}
 LATE_WORDS = 50
-FIRST_SIGMOIDS = 54
-FIRST_GATE, LAST_ROWS, FIRST_EXP, LAST_GROUPED = 70, 78, 84, 100
-THIRD_CELLS, FIRST_Y = 104, 112
-TURNING, HOLDING, CROSSED = (0, 1, 2, 3), (4, 5, 6, 7), (2, 3, 0, 1)
+LATE_SIGMOIDS, LATE_EXP, FIRST_GATE, FIRST_EXP, THIRD_CELLS, GAINED, STAIR = 54, 62.5, 70, 84, 100, 108, 77
+TURNING, HOLDING, SUMMING = (0, 1, 2, 3), (4, 5, 6, 7), (5, 6, 7, 3)
+CHUNKS = ((0, 128), (128, 128), (256, 256), (512, 256), (768, 256))
 
 
 def tile_list_pen_biomass_cues_kernel(
@@ -180,19 +177,15 @@ def tile_list_pen_biomass_cues_kernel(
             if b == 0:
                 wa_grouped[a, b] = held([P, PACK, P, PACK], BF16, name)
             else:
-                wa_grouped[a, b] = placed([P, PACK, P, PACK], BF16, name, LAST_GROUPED)
-            shares = [(nc.vector, "p m i t", 0, P)]
-            if (a, b) == (1, 1):
-                shares = [(nc.gpsimd, "p m t i", 0, ON_GPSIMD), (nc.vector, "p m i t", ON_GPSIMD, P)]
-            for engine, walk, first, last in shares:
-                engine.tensor_scalar(
-                    out=wa_grouped[a, b][:].rearrange("p t m i -> " + walk)[:, first:last],
-                    in0=wa_raw[a, b][:].rearrange("p i (m t) -> " + walk, t=PACK)[:, first:last],
-                    scalar1=-1.0,
-                    scalar2=0.0,
-                    op0=ALU.mult,
-                    op1=ALU.add,
-                )
+                wa_grouped[a, b] = placed([P, PACK, P, PACK], BF16, name, (THIRD_CELLS, FIRST_GATE + 4)[a])
+            nc.vector.tensor_scalar(
+                out=wa_grouped[a, b][:].rearrange("p t m i -> p m i t"),
+                in0=wa_raw[a, b][:].rearrange("p i (m t) -> p m i t", t=PACK),
+                scalar1=-1.0,
+                scalar2=0.0,
+                op0=ALU.mult,
+                op1=ALU.add,
+            )
 
         def quantise_wa(a, b):
             wa_codes[a, b] = held([P, HALF], U32, "wa_codes%d%d" % (a, b))
@@ -203,28 +196,32 @@ def tile_list_pen_biomass_cues_kernel(
                 in_=wa_grouped[a, b][:].rearrange("p t m i -> p (t m i)"),
             )
 
+        def clear_late(i, kib):
+            cells[i] = placed([P, T2], F32, "cells%d" % i, kib)
+            nc.gpsimd.memset(cells[i][:].bitcast(I32), 0)
+
         exp_b = {(b, 0): placed([P, PACK, HALF], F32, "exp_b%d0" % b, FIRST_EXP + 8 * b) for b in range(2)}
-        gate = {(0, 0): placed([P, PACK, HALF], F32, "gate00", FIRST_GATE), (1, 0): placed([P, PACK, HALF], F32, "gate10", TABLE[1])}
-        b_bank = {}
+        b_copy = {
+            (0, 0): placed([P, PACK, HALF], F32, "b_copy00", FIRST_GATE),
+            (1, 0): placed([P, PACK, HALF], F32, "b_copy10", TABLE[1]),
+        }
+        b_bank, gate = {}, {}
 
         def b_sum(b, t, half, bank):
             b_bank[b, t, half] = in_bank([P, HALF], "bank_b%d%d%d" % (b, t, half), bank)
             wb_passes(b_bank[b, t, half], b, t, half, True)
 
-        def exponential(b, t, half):
-            nc.scalar.activation(exp_b[b, half][:, t, :], b_bank[b, t, half][:], ACT.Exp)
-
         def first_phase(b, banks):
             for t in range(PACK):
                 b_sum(b, t, 0, banks[t])
-                exponential(b, t, 0)
-                nc.scalar.copy(gate[b, 0][:, t, :], b_bank[b, t, 0][:])
+                nc.scalar.activation(exp_b[b, 0][:, t, :], b_bank[b, t, 0][:], ACT.Exp)
+                nc.scalar.copy(b_copy[b, 0][:, t, :], b_bank[b, t, 0][:])
 
-        def difference(b, half, banks, into):
-            for t in range(PACK):
+        def difference(b, half, banks, into, steps=range(PACK)):
+            for t in steps:
                 bank = in_bank([P, HALF], "bank_a%d%d%d" % (b, t, half), banks[t])
                 wa_passes(bank, b, t, half, (0, 1), True)
-                nc.vector.tensor_tensor(into[:, t, :], bank[:], gate[b, half][:, t, :], ALU.add)
+                nc.vector.tensor_tensor(into[:, t, :], bank[:], b_copy[b, half][:, t, :], ALU.add)
             gate[b, half] = into
 
         first_phase(0, TURNING)
@@ -235,12 +232,13 @@ def tile_list_pen_biomass_cues_kernel(
         quantise_wa(1, 0)
         round_wa(0, 1)
         quantise_wa(0, 1)
+        clear_late(2, THIRD_CELLS)
         difference(0, 0, TURNING, placed([P, PACK, HALF], F32, "difference00", WA[0, 1]))
         round_wa(1, 1)
         quantise_wa(1, 1)
 
         wc_raw = placed([P, 2, N], I32, "wc_raw", WA[0, 0])
-        wgo_sb = placed([P, S], F32, "wgo_sb", WA[0, 0] + 4)
+        wgo_sb = placed([P, S], F32, "wgo_sb", WA[1, 0] + 2)
         wc_rows = placed([P, N], U8, "wc_rows", WA[1, 0])
         gain_sb = placed([P, 2, PACK], F32, "gain_sb", WA[1, 0] + 1)
         nc.vector.memset(wc_rows[:].bitcast(I32), 0)
@@ -252,195 +250,193 @@ def tile_list_pen_biomass_cues_kernel(
             )
         nc.sync.dma_start(wgo_sb[:], wgo)
 
-        difference(1, 0, HOLDING, gate[1, 0])
-        sum_bank = {}
-
-        def summed(t):
-            sum_bank[t] = in_bank([P, HALF], "bank_sum%d" % t, TURNING[t])
-            wa_passes(sum_bank[t], 1, t, 1, (1, 0), False)
-            wb_passes(sum_bank[t], 1, t, 1, False)
-
-        for t in range(2):
-            summed(t)
+        difference(1, 0, HOLDING, b_copy[1, 0])
+        b_copy[0, 1] = placed([P, PACK, HALF], F32, "b_copy01", TABLE[0])
         for t in range(PACK):
-            b_sum(0, t, 1, HOLDING[t])
+            b_sum(0, t, 1, TURNING[t])
+            nc.scalar.copy(b_copy[0, 1][:, t, :], b_bank[0, t, 1][:])
 
         wc_codes = held([P, 2, N], I32, "wc_codes")
         wc_plane = held([P, N], U8, "wc_plane")
         nc.vector.tensor_copy(
-            wc_codes[:].rearrange("p b (t m) -> p b m t", t=PACK),
-            wc_raw[:].rearrange("p b (m t) -> p b m t", t=PACK),
-        )
-        nc.vector.tensor_copy(
             wc_plane[:].rearrange("p (t m) -> p m t", t=PACK),
             wc_rows[:].rearrange("p (m t) -> p m t", t=PACK),
         )
+        nc.vector.tensor_copy(
+            wc_codes[:].rearrange("p b (t m) -> p b m t", t=PACK),
+            wc_raw[:].rearrange("p b (m t) -> p b m t", t=PACK),
+        )
+        clear_late(3, WA[0, 0])
 
-        sigmoid, h_rows, h_grouped, h_operand = {}, {}, {}, {}
+        h_grouped, h_operand, y_bank = {}, {}, {}
 
-        def within_half(first, count):
+        def columns(c):
+            first, count = CHUNKS[c]
             return slice(first % HALF, first % HALF + count)
 
-        def products(first, count, b):
-            name = "h_rows%d_%d" % (first, b)
-            if (first, b) == (HALF, 1):
-                h_rows[first, b] = placed([P, PACK, count], BF16, name, LAST_ROWS)
-            else:
-                h_rows[first, b] = held([P, PACK, count], BF16, name)
+        def sigmoid(out, in_):
+            nc.scalar.activation(out, in_, ACT.Sigmoid, scale=-1.0)
+
+        def grouped(c):
+            h_grouped[c] = placed([P, 2, CHUNKS[c][1], PACK], BF16, "h_grouped%d" % c, STAIR + (-9, 0, 1.5, 5, 8)[c])
+
+        def product(c, b, gained, gates):
+            nc.gpsimd.tensor_tensor(
+                h_grouped[c][:, b, :, :], gained.rearrange("p t j -> p j t"), gates.rearrange("p t j -> p j t"), ALU.mult
+            )
+
+        def quantise_h(c):
+            count = CHUNKS[c][1]
+            codes = held([P, 2, count], U32, "h_codes%d" % c)
+            plane = held([P, 2, count], U8, "h_plane%d" % c)
+            nc.vector.quantize_mx(
+                out=codes[:].rearrange("p b j -> p (b j)").bitcast(FP8X4),
+                scales=plane[:].rearrange("p b j -> p (b j)"),
+                in_=h_grouped[c][:].rearrange("p b j t -> p (b j t)"),
+            )
+            h_operand[c] = (codes, plane)
+
+        def mix(c, banks):
+            count = CHUNKS[c][1]
+            per_bank = PACK // len(banks)
+            tiles = [in_bank([P, per_bank, count], "bank_y%d_%d" % (c, k), k) for k in banks]
+            for i in range(PACK):
+                y_bank[c, i] = tiles[i // per_bank]
+                for b in range(2):
+                    nc.tensor.matmul_mx(
+                        out=tiles[i // per_bank][:, i % per_bank, :],
+                        lhsT=wc_codes[:, b, P * i : P * (i + 1)].bitcast(FP8X4),
+                        lhsT_scale=wc_plane[4 * b : P, P * i : P * (i + 1)],
+                        rhs=h_operand[c][0][:, b, :].bitcast(FP8X4),
+                        rhs_scale=h_operand[c][1][:, b, :],
+                        start=(b == 0),
+                        stop=(b == 1),
+                    )
+
+        def entries(first, count):
+            return offs2_sb[:, first // LIST : (first + count) // LIST]
+
+        def weigh_and_put(c, low, high, kib=None):
+            first, count = CHUNKS[c]
+            name = "weighted%d_%d" % (c, low)
+            shape = [P, high - low, count]
+            weighted = held(shape, F32, name) if kib is None else placed(shape, F32, name, kib)
+            within = low % y_bank[c, low].shape[1]
+            nc.vector.tensor_tensor(
+                weighted[:],
+                y_bank[c, low][:, within : within + high - low, :],
+                wgo_sb[:, first : first + count].unsqueeze(1).to_broadcast(shape),
+                ALU.mult,
+            )
+            for i in range(low, high):
+                nc.vector.tensor_copy(cells[i][:].indirect(entries(first, count)), weighted[:, i - low, :])
+
+        first_count = CHUNKS[0][1]
+        sigmoid(gate[0, 0][:, :, :first_count], gate[0, 0][:, :, :first_count])
+        for t in range(0, PACK, 2):
+            sigmoid(gate[1, 0][:, t : t + 2, :first_count], gate[1, 0][:, t : t + 2, :first_count])
+        for b in range(2):
+            sigmoid(gate[b, 0][:, :, columns(1)], gate[b, 0][:, :, columns(1)])
+        grouped(0)
+        for b in range(2):
+            rows = placed([P, PACK, first_count], BF16, "h_rows%d" % b, GAINED + 5 + b)
             for t in range(PACK):
                 nc.vector.scalar_tensor_tensor(
-                    out=h_rows[first, b][:, t, :],
-                    in0=exp_b[b, first // HALF][:, t, within_half(first, count)],
+                    out=rows[:, t, :],
+                    in0=exp_b[b, 0][:, t, :first_count],
                     scalar=gain_sb[:, b, t : t + 1],
-                    in1=sigmoid[first, b][:, t, :],
+                    in1=gate[b, 0][:, t, :first_count],
                     op0=ALU.mult,
                     op1=ALU.mult,
                 )
-
-        def interleave(first, count, b, copy):
-            name = "h_grouped%d_%d" % (first, b)
-            if (first, b) == (0, 1):
-                h_grouped[first, b] = placed([P, count, PACK], BF16, name, THIRD_CELLS)
-            else:
-                h_grouped[first, b] = held([P, count, PACK], BF16, name)
-            copy(
-                h_grouped[first, b][:].rearrange("p (j e) t -> p j t e", e=4),
-                h_rows[first, b][:].rearrange("p t (j e) -> p j t e", e=4),
+            nc.vector.tensor_copy(
+                h_grouped[0][:, b, :, :].rearrange("p (j e) t -> p j t e", e=4),
+                rows[:].rearrange("p t (j e) -> p j t e", e=4),
             )
+        quantise_h(0)
+        mix(0, (4,))
 
-        def interleave_second(b):
-            h_grouped[CHUNK, b] = placed([P, CHUNK, PACK], BF16, "h_grouped_second%d" % b, FIRST_SIGMOIDS + 12 + 2 * b)
-            nc.gpsimd.tensor_scalar(
-                out=h_grouped[CHUNK, b][:],
-                in0=h_rows[CHUNK, b][:].rearrange("p t j -> p j t"),
-                scalar1=1.0,
-                scalar2=0.0,
-                op0=ALU.mult,
-                op1=ALU.add,
-            )
-
-        def clear_late(i, kib):
-            cells[i] = placed([P, T2], F32, "cells%d" % i, kib)
-            nc.gpsimd.memset(cells[i][:].bitcast(I32), 0)
-
-        def quantise_h(first, count, b):
-            name = "h_codes%d_%d" % (first, b)
-            if first == CHUNK:
-                codes = placed([P, count], U32, name, FIRST_Y + b)
-            else:
-                codes = held([P, count], U32, name)
-            plane = held([P, count], U8, "h_plane%d_%d" % (first, b))
-            nc.vector.quantize_mx(
-                out=codes[:].bitcast(FP8X4), scales=plane[:], in_=h_grouped[first, b][:].rearrange("p j t -> p (j t)")
-            )
-            h_operand[first, b] = (codes, plane)
-
-        def mix(first, i, view, order):
-            for b in order:
-                nc.tensor.matmul_mx(
-                    out=view,
-                    lhsT=wc_codes[:, b, P * i : P * (i + 1)].bitcast(FP8X4),
-                    lhsT_scale=wc_plane[4 * b : P, P * i : P * (i + 1)],
-                    rhs=h_operand[first, b][0][:].bitcast(FP8X4),
-                    rhs_scale=h_operand[first, b][1][:],
-                    start=(b == order[0]),
-                    stop=(b == order[1]),
+        gained = {}
+        for b in range(2):
+            gained[b] = placed([P, PACK, first_count], F32, "gained%d" % b, GAINED + 4 + 2 * b)
+            for t in range(PACK):
+                nc.vector.tensor_scalar(
+                    out=gained[b][:, t, :],
+                    in0=exp_b[b, 0][:, t, columns(1)],
+                    scalar1=gain_sb[:, b, t : t + 1],
+                    scalar2=None,
+                    op0=ALU.mult,
                 )
 
-        def mix_chunk(first, first_bank):
-            banks = [in_bank([P, 2, CHUNK], "bank_y%d_%d" % (first, k), first_bank + k) for k in range(2)]
-            for i in range(PACK):
-                mix(first, i, banks[i // 2][:, i % 2, :], (1, 0))
-            return banks
-
-        def put(i, values, first, count):
-            nc.vector.tensor_tensor(
-                cells[i][:].indirect(offs2_sb[:, first // LIST : (first + count) // LIST]),
-                values,
-                wgo_sb[:, first : first + count],
-                ALU.mult,
-            )
-
-        def evacuate(bank, tile):
-            nc.scalar.copy(tile[:], bank[:])
-            return tile
-
-        def first_sigmoids(c, b, steps):
-            sigmoid[CHUNK * c, b] = placed([P, PACK, CHUNK], F32, "sigmoid%d%d" % (c, b), FIRST_SIGMOIDS + 8 * c + 4 * b)
-            for t in range(0, PACK, steps):
-                nc.scalar.activation(
-                    sigmoid[CHUNK * c, b][:, t : t + steps, :],
-                    gate[b, 0][:, t : t + steps, CHUNK * c : CHUNK * (c + 1)],
-                    ACT.Sigmoid,
-                    scale=-1.0,
-                )
-
+        late_difference = placed([P, PACK, HALF], F32, "difference01", FIRST_GATE - 2)
+        difference(0, 1, TURNING, late_difference, range(PACK - 1))
         for b in range(2):
-            first_sigmoids(0, b, 1)
-            products(0, CHUNK, b)
-        sigmoid[HALF, 1] = placed([P, PACK, HALF], F32, "sigmoid_sum", WA[1, 1])
+            sigmoid(gate[b, 0][:, :, columns(2)], gate[b, 0][:, :, columns(2)])
+            for t in range(PACK):
+                row = exp_b[b, 0][:, t, columns(2)]
+                nc.scalar.activation(row, row, ACT.Copy, scale=gain_sb[:, b, t : t + 1])
 
-        def summed_sigmoid(t):
-            nc.scalar.activation(sigmoid[HALF, 1][:, t, :], sum_bank[t][:], ACT.Sigmoid, scale=-1.0)
+        grouped(1)
+        for b in range(2):
+            product(1, b, gained[b][:], gate[b, 0][:, :, columns(1)])
+        weigh_and_put(0, 0, 1)
+        quantise_h(1)
+        mix(1, (0,))
+        weigh_and_put(0, 1, 4, STAIR)
+        grouped(2)
+        for b in range(2):
+            product(2, b, exp_b[b, 0][:, :, columns(2)], gate[b, 0][:, :, columns(2)])
 
-        for t in range(2):
-            summed_sigmoid(t)
-        for b in range(2):
-            interleave(0, CHUNK, b, nc.vector.tensor_copy)
-        for b in range(2):
-            quantise_h(0, CHUNK, b)
-        clear_late(2, THIRD_CELLS)
-        for b in range(2):
-            first_sigmoids(1, b, PACK)
-            products(CHUNK, CHUNK, b)
-        interleave_second(1)
-        clear_late(3, FIRST_EXP + 8)
-        gate[0, 1] = placed([P, PACK, HALF], F32, "gate01", TABLE[1])
-        banks = mix_chunk(0, TURNING[0])
-        first_y = []
-        for k in range(2):
-            for t in (2 * k, 2 * k + 1):
-                nc.scalar.copy(gate[0, 1][:, t, :], b_bank[0, t, 1][:])
-            if k == 0:
-                first_y = [evacuate(banks[n], placed([P, 2, CHUNK], F32, "first_y%d" % n, FIRST_Y + 2 * n)) for n in range(2)]
-        difference(0, 1, CROSSED, gate[0, 1])
-        for t in range(2, PACK):
-            summed(t)
-        interleave(CHUNK, CHUNK, 0, nc.scalar.copy)
-        for i in range(PACK):
-            put(i, first_y[i // 2][:, i % 2, :], 0, CHUNK)
-        for b in range(2):
-            quantise_h(CHUNK, CHUNK, b)
-        sigmoid[HALF, 0] = placed([P, PACK, HALF], F32, "sigmoid_last", FIRST_GATE)
-        nc.scalar.activation(sigmoid[HALF, 0][:], gate[0, 1][:], ACT.Sigmoid, scale=-1.0)
-        for t in range(2, PACK):
-            summed_sigmoid(t)
-
-        exp_b[0, 1] = placed([P, PACK, HALF], F32, "exp_b01", TABLE[1] - 4)
-        exp_b[1, 1] = placed([P, PACK, HALF], F32, "exp_b11", TABLE[1] + 4)
+        late_gate = {b: placed([P, PACK, HALF], F32, "late_gate%d" % b, (LATE_SIGMOIDS, WA[1, 1])[b]) for b in range(2)}
         for t in range(PACK):
-            exponential(0, t, 1)
-        products(HALF, HALF, 0)
-        for t in range(PACK):
-            b_sum(1, t, 1, TURNING[t])
-            exponential(1, t, 1)
-        banks = mix_chunk(CHUNK, HOLDING[0])
-        products(HALF, HALF, 1)
+            bank = in_bank([P, HALF], "bank_sum%d" % t, SUMMING[t])
+            wa_passes(bank, 1, t, 1, (1, 0), False)
+            wb_passes(bank, 1, t, 1, False)
+            sigmoid(late_gate[1][:, t, :], bank[:])
+        difference(0, 1, TURNING, late_difference, (PACK - 1,))
+        for t in range(0, PACK, 2):
+            sigmoid(late_gate[0][:, t : t + 2, :], gate[0, 1][:, t : t + 2, :])
 
-        second_y = evacuate(banks[0], held([P, 2, CHUNK], F32, "second_y0"))
-        for b in range(2):
-            interleave(HALF, HALF, b, nc.scalar.copy)
-        for u in range(2):
-            put(u, second_y[:, u, :], CHUNK, CHUNK)
-        for b in range(2):
-            quantise_h(HALF, HALF, b)
-        second_y = evacuate(banks[1], placed([P, 2, CHUNK], F32, "second_y1", LAST_ROWS))
-        for u in range(2):
-            put(2 + u, second_y[:, u, :], CHUNK, CHUNK)
+        weigh_and_put(1, 0, 3)
+        quantise_h(2)
+        mix(2, (1, 2))
+        weigh_and_put(1, 3, 4, STAIR + 2)
+
+        for t in range(PACK):
+            b_sum(1, t, 1, SUMMING[t])
+        exp_b[0, 1] = placed([P, PACK, HALF], F32, "exp_b01", LATE_EXP + 8)
+        exp_b[1, 1] = placed([P, PACK, HALF], F32, "exp_b11", LATE_EXP)
+
+        def late_products(c):
+            grouped(c)
+            for b in range(2):
+                if b == 0:
+                    nc.scalar.activation(exp_b[0, 1][:, :, columns(c)], b_copy[0, 1][:, :, columns(c)], ACT.Exp)
+                for t in range(PACK):
+                    row = exp_b[b, 1][:, t, columns(c)]
+                    if b == 1:
+                        nc.scalar.activation(row, b_bank[1, t, 1][:, columns(c)], ACT.Exp)
+                    nc.scalar.activation(row, row, ACT.Copy, scale=gain_sb[:, b, t : t + 1])
+                product(c, b, exp_b[b, 1][:, :, columns(c)], late_gate[b][:, :, columns(c)])
+
+        late_products(3)
+        weigh_and_put(2, 0, 2)
+        weigh_and_put(2, 2, 3)
+        quantise_h(3)
+        mix(3, (4, 0))
+        weigh_and_put(2, 3, 4, STAIR + 6)
+        late_products(4)
+        weigh_and_put(3, 0, 2)
+        quantise_h(4)
+        mix(4, (1, 2))
+        weigh_and_put(3, 2, 3, STAIR + 9)
 
         out_rows = out.rearrange("(p i) t -> i p t", i=PACK)
         for i in range(PACK):
-            bank = in_bank([P, HALF], "bank_last%d" % i, (HOLDING[2:] + TURNING)[i])
-            mix(HALF, i, bank[:], (1, 0))
-            put(i, evacuate(bank, held([P, HALF], F32, "last_y%d" % i))[:], HALF, HALF)
+            first = CHUNKS[3 if i == PACK - 1 else 4][0]
+            rows = held([P, S - first], F32, "last_y%d" % i)
+            if i == PACK - 1:
+                nc.scalar.copy(rows[:, : CHUNKS[3][1]], y_bank[3, i][:, 1, :])
+            nc.scalar.copy(rows[:, CHUNKS[4][0] - first :], y_bank[4, i][:, i % 2, :])
+            nc.vector.tensor_tensor(cells[i][:].indirect(entries(first, S - first)), rows[:], wgo_sb[:, first:], ALU.mult)
             nc.sync.dma_start(out_rows[i], cells[i][:])

@@ -282,7 +282,10 @@ def tile_list_pen_biomass_cues_kernel(
 
         def product(c, b, gained, gates):
             nc.gpsimd.tensor_tensor(
-                h_grouped[c][:, b, :, :], gained.rearrange("p t j -> p j t"), gates.rearrange("p t j -> p j t"), ALU.mult
+                h_grouped[c][:, b, :, :].rearrange("p (j e) t -> p j t e", e=4),
+                gained.rearrange("p t (j e) -> p j t e", e=4),
+                gates.rearrange("p t (j e) -> p j t e", e=4),
+                ALU.mult,
             )
 
         def quantise_h(c):

@@ -27,7 +27,8 @@ KIB = 1024
 TABLE = (0, 8)
 WA = {(0, 0): 16, (1, 0): 26, (0, 1): 34, (1, 1): 42}
 LATE_WORDS = 50
-LATE_SIGMOIDS, LATE_EXP, FIRST_GATE, FIRST_EXP, THIRD_CELLS, GAINED, STAIR = 54, 62.5, 70, 84, 100, 108, 77
+LATE_EXP, FIRST_GATE, FIRST_EXP, THIRD_CELLS, GAINED, STAIR = 62, 70, 84, 100, 124, 77
+GATES = (108, 112, 116, 42, 54)
 TURNING, HOLDING, SUMMING = (0, 1, 2, 3), (4, 5, 6, 7), (5, 6, 7, 3)
 CHUNKS = ((0, 128), (128, 128), (256, 256), (512, 256), (768, 256))
 
@@ -280,13 +281,15 @@ def tile_list_pen_biomass_cues_kernel(
         def grouped(c):
             h_grouped[c] = placed([P, 2, CHUNKS[c][1], PACK], BF16, "h_grouped%d" % c, STAIR + (-9, 0, 1.5, 5, 8)[c])
 
-        def product(c, b, gained, gates):
-            nc.gpsimd.tensor_tensor(
-                h_grouped[c][:, b, :, :].rearrange("p (j e) t -> p j t e", e=4),
-                gained.rearrange("p t (j e) -> p j t e", e=4),
-                gates.rearrange("p t (j e) -> p j t e", e=4),
-                ALU.mult,
-            )
+        def products(c):
+            grouped(c)
+            for b in range(2):
+                nc.gpsimd.tensor_tensor(
+                    h_grouped[c][:, b, :, :].rearrange("p (j e) t -> p j t e", e=2),
+                    gained[c][:, b, :, :].rearrange("p t (j e) -> p j t e", e=2),
+                    gates[c][:, b, :, :].rearrange("p t (j e) -> p j t e", e=2),
+                    ALU.mult,
+                )
 
         def quantise_h(c):
             count = CHUNKS[c][1]
@@ -335,20 +338,22 @@ def tile_list_pen_biomass_cues_kernel(
                 nc.vector.tensor_copy(cells[i][:].indirect(entries(first, count)), weighted[:, i - low, :])
 
         first_count = CHUNKS[0][1]
-        sigmoid(gate[0, 0][:, :, :first_count], gate[0, 0][:, :, :first_count])
+        gates = {c: placed([P, 2, PACK, CHUNKS[c][1]], F32, "gates%d" % c, GATES[c]) for c in range(5)}
+        gained = {}
+        sigmoid(gates[0][:, 0, :, :], gate[0, 0][:, :, columns(0)])
         for t in range(0, PACK, 2):
-            sigmoid(gate[1, 0][:, t : t + 2, :first_count], gate[1, 0][:, t : t + 2, :first_count])
+            sigmoid(gates[0][:, 1, t : t + 2, :], gate[1, 0][:, t : t + 2, columns(0)])
         for b in range(2):
-            sigmoid(gate[b, 0][:, :, columns(1)], gate[b, 0][:, :, columns(1)])
+            sigmoid(gates[1][:, b, :, :], gate[b, 0][:, :, columns(1)])
         grouped(0)
         for b in range(2):
-            rows = placed([P, PACK, first_count], BF16, "h_rows%d" % b, GAINED + 5 + b)
+            rows = placed([P, PACK, first_count], BF16, "h_rows%d" % b, GAINED + 9 + b)
             for t in range(PACK):
                 nc.vector.scalar_tensor_tensor(
                     out=rows[:, t, :],
-                    in0=exp_b[b, 0][:, t, :first_count],
+                    in0=exp_b[b, 0][:, t, columns(0)],
                     scalar=gain_sb[:, b, t : t + 1],
-                    in1=gate[b, 0][:, t, :first_count],
+                    in1=gates[0][:, b, t, :],
                     op0=ALU.mult,
                     op1=ALU.mult,
                 )
@@ -359,12 +364,11 @@ def tile_list_pen_biomass_cues_kernel(
         quantise_h(0)
         mix(0, (4,))
 
-        gained = {}
+        gained[1] = placed([P, 2, PACK, first_count], F32, "gained1", GAINED + 8)
         for b in range(2):
-            gained[b] = placed([P, PACK, first_count], F32, "gained%d" % b, GAINED + 4 + 2 * b)
             for t in range(PACK):
                 nc.vector.tensor_scalar(
-                    out=gained[b][:, t, :],
+                    out=gained[1][:, b, t, :],
                     in0=exp_b[b, 0][:, t, columns(1)],
                     scalar1=gain_sb[:, b, t : t + 1],
                     scalar2=None,
@@ -373,32 +377,32 @@ def tile_list_pen_biomass_cues_kernel(
 
         late_difference = placed([P, PACK, HALF], F32, "difference01", FIRST_GATE - 2)
         difference(0, 1, TURNING, late_difference, range(PACK - 1))
+        gained[2] = placed([P, 2, PACK, CHUNKS[2][1]], F32, "gained2", GAINED)
         for b in range(2):
-            sigmoid(gate[b, 0][:, :, columns(2)], gate[b, 0][:, :, columns(2)])
+            sigmoid(gates[2][:, b, :, :], gate[b, 0][:, :, columns(2)])
             for t in range(PACK):
-                row = exp_b[b, 0][:, t, columns(2)]
-                nc.scalar.activation(row, row, ACT.Copy, scale=gain_sb[:, b, t : t + 1])
+                nc.scalar.activation(
+                    gained[2][:, b, t, :], exp_b[b, 0][:, t, columns(2)], ACT.Copy, scale=gain_sb[:, b, t : t + 1]
+                )
 
-        grouped(1)
-        for b in range(2):
-            product(1, b, gained[b][:], gate[b, 0][:, :, columns(1)])
+        products(1)
         weigh_and_put(0, 0, 1)
         quantise_h(1)
         mix(1, (0,))
         weigh_and_put(0, 1, 4, STAIR)
-        grouped(2)
-        for b in range(2):
-            product(2, b, exp_b[b, 0][:, :, columns(2)], gate[b, 0][:, :, columns(2)])
+        products(2)
 
-        late_gate = {b: placed([P, PACK, HALF], F32, "late_gate%d" % b, (LATE_SIGMOIDS, WA[1, 1])[b]) for b in range(2)}
+        for c in (3, 4):
+            sigmoid(gates[c][:, 0, : PACK - 1, :], late_difference[:, : PACK - 1, columns(c)])
         for t in range(PACK):
             bank = in_bank([P, HALF], "bank_sum%d" % t, SUMMING[t])
             wa_passes(bank, 1, t, 1, (1, 0), False)
             wb_passes(bank, 1, t, 1, False)
-            sigmoid(late_gate[1][:, t, :], bank[:])
+            for c in (3, 4):
+                sigmoid(gates[c][:, 1, t, :], bank[:, columns(c)])
         difference(0, 1, TURNING, late_difference, (PACK - 1,))
-        for t in range(0, PACK, 2):
-            sigmoid(late_gate[0][:, t : t + 2, :], gate[0, 1][:, t : t + 2, :])
+        for c in (3, 4):
+            sigmoid(gates[c][:, 0, PACK - 1, :], late_difference[:, PACK - 1, columns(c)])
 
         weigh_and_put(1, 0, 3)
         quantise_h(2)
@@ -407,20 +411,18 @@ def tile_list_pen_biomass_cues_kernel(
 
         for t in range(PACK):
             b_sum(1, t, 1, SUMMING[t])
-        exp_b[0, 1] = placed([P, PACK, HALF], F32, "exp_b01", LATE_EXP + 8)
-        exp_b[1, 1] = placed([P, PACK, HALF], F32, "exp_b11", LATE_EXP)
 
         def late_products(c):
-            grouped(c)
+            gained[c] = placed([P, 2, PACK, CHUNKS[c][1]], F32, "gained%d" % c, LATE_EXP + 8 * (c - 3))
             for b in range(2):
                 if b == 0:
-                    nc.scalar.activation(exp_b[0, 1][:, :, columns(c)], b_copy[0, 1][:, :, columns(c)], ACT.Exp)
+                    nc.scalar.activation(gained[c][:, 0, :, :], b_copy[0, 1][:, :, columns(c)], ACT.Exp)
                 for t in range(PACK):
-                    row = exp_b[b, 1][:, t, columns(c)]
+                    row = gained[c][:, b, t, :]
                     if b == 1:
                         nc.scalar.activation(row, b_bank[1, t, 1][:, columns(c)], ACT.Exp)
                     nc.scalar.activation(row, row, ACT.Copy, scale=gain_sb[:, b, t : t + 1])
-                product(c, b, exp_b[b, 1][:, :, columns(c)], late_gate[b][:, :, columns(c)])
+            products(c)
 
         late_products(3)
         weigh_and_put(2, 0, 2)

@@ -20,17 +20,19 @@ P = 128
 PACK = 4
 PASS = P * PACK
 HALF = 512
+CHUNK = 256
 LIST = 16
 BANK = 2048
 KIB = 1024
+ON_GPSIMD = 80
 
 TABLE = (0, 8)
-WA = {(0, 0): 16, (1, 0): 26, (0, 1): 34, (1, 1): 42}
+WA = {(0, 0): 16, (1, 0): 26, (0, 1): 34, (1, 1): 116}
 LATE_WORDS = 50
-LATE_EXP, FIRST_GATE, FIRST_EXP, THIRD_CELLS, GAINED, STAIR = 62, 70, 84, 100, 124, 77
-GATES = (108, 112, 116, 42, 54)
-TURNING, HOLDING, SUMMING = (0, 1, 2, 3), (4, 5, 6, 7), (5, 6, 7, 3)
-CHUNKS = ((0, 128), (128, 128), (256, 256), (512, 256), (768, 256))
+LATE_EXP, FIRST_GATE, STAIR, FIRST_EXP, LAST_GROUPED, FIRST_ROWS = 61, 70, 75, 84, 100, 140
+GATES = (104, 132, 116, 144)
+TURNING, HOLDING, SUMMING = (0, 1, 2, 3), (4, 5, 6, 7), (0, 1, 2, 3)
+LATE = (4, 5, 6, 7)
 
 
 def tile_list_pen_biomass_cues_kernel(
@@ -61,7 +63,7 @@ def tile_list_pen_biomass_cues_kernel(
         for j in range(4):
             nc.sync.dma_start(tab_rows[j:P:4, :].bitcast(I32), tab_scales.rearrange("a q t -> q a t").bitcast(I32))
 
-        wb_rows = placed([P, 2, H], U8, "wb_rows", WA[1, 1])
+        wb_rows = placed([P, 2, H], U8, "wb_rows", WA[1, 1] + 7)
         tab_plane = held([P, 2, S], U8, "tab_plane")
         nc.gpsimd.memset(wb_rows[:].rearrange("p a c -> p (a c)").bitcast(I32), 0)
 
@@ -94,11 +96,17 @@ def tile_list_pen_biomass_cues_kernel(
         load_wb(0, WA[0, 1] - 1)
         load_table(0)
 
-        nc.vector.memset(tab_plane[:].rearrange("p a s -> p (a s)").bitcast(I32), 0)
-        cells = {}
-        for i in range(2):
-            cells[i] = held([P, T2], F32, "cells%d" % i)
-            nc.vector.memset(cells[i][:].bitcast(I32), 0)
+        def clear_alone(words):
+            middle = words.shape[1] // 2 - 1
+            nc.vector.memset(words[:, :middle], 0)
+            nc.vector.memset(words[:, middle:], 0)
+
+        clear_alone(tab_plane[:].rearrange("p a s -> p (a s)").bitcast(I32))
+        cells = {i: held([P, T2], F32, "cells%d" % i) for i in (0, 2)}
+        cells[3] = placed([P, T2], F32, "cells3", 42)
+        clear_alone(cells[0][:].bitcast(I32))
+        for i in (2, 3):
+            nc.gpsimd.memset(cells[i][:].bitcast(I32), 0)
 
         picked_rows = placed([P, S], U8, "picked_rows", LATE_WORDS + 1.5)
         nc.vector.tensor_copy(picked_rows[:], tab_rows[:].indirect(offs_sb[:]))
@@ -138,6 +146,8 @@ def tile_list_pen_biomass_cues_kernel(
         deal_wb(0)
         gather_words(0, 0)
         deal_wb(1)
+        cells[1] = placed([P, T2], F32, "cells1", WA[1, 1] + 8)
+        nc.gpsimd.memset(cells[1][:].bitcast(I32), 0)
         gather_words(1, 1)
         gather_words(0, 1)
         load_wa(1, 0)
@@ -178,15 +188,19 @@ def tile_list_pen_biomass_cues_kernel(
             if b == 0:
                 wa_grouped[a, b] = held([P, PACK, P, PACK], BF16, name)
             else:
-                wa_grouped[a, b] = placed([P, PACK, P, PACK], BF16, name, (THIRD_CELLS, FIRST_GATE + 4)[a])
-            nc.vector.tensor_scalar(
-                out=wa_grouped[a, b][:].rearrange("p t m i -> p m i t"),
-                in0=wa_raw[a, b][:].rearrange("p i (m t) -> p m i t", t=PACK),
-                scalar1=-1.0,
-                scalar2=0.0,
-                op0=ALU.mult,
-                op1=ALU.add,
-            )
+                wa_grouped[a, b] = placed([P, PACK, P, PACK], BF16, name, LAST_GROUPED)
+            shares = [(nc.vector, "p m i t", 0, P)]
+            if (a, b) == (1, 1):
+                shares = [(nc.gpsimd, "p m t i", 0, ON_GPSIMD), (nc.vector, "p m i t", ON_GPSIMD, P)]
+            for engine, walk, first, last in shares:
+                engine.tensor_scalar(
+                    out=wa_grouped[a, b][:].rearrange("p t m i -> " + walk)[:, first:last],
+                    in0=wa_raw[a, b][:].rearrange("p i (m t) -> " + walk, t=PACK)[:, first:last],
+                    scalar1=-1.0,
+                    scalar2=0.0,
+                    op0=ALU.mult,
+                    op1=ALU.add,
+                )
 
         def quantise_wa(a, b):
             wa_codes[a, b] = held([P, HALF], U32, "wa_codes%d%d" % (a, b))
@@ -196,10 +210,6 @@ def tile_list_pen_biomass_cues_kernel(
                 scales=wa_plane[a, b][:],
                 in_=wa_grouped[a, b][:].rearrange("p t m i -> p (t m i)"),
             )
-
-        def clear_late(i, kib):
-            cells[i] = placed([P, T2], F32, "cells%d" % i, kib)
-            nc.gpsimd.memset(cells[i][:].bitcast(I32), 0)
 
         exp_b = {(b, 0): placed([P, PACK, HALF], F32, "exp_b%d0" % b, FIRST_EXP + 8 * b) for b in range(2)}
         b_copy = {
@@ -218,8 +228,8 @@ def tile_list_pen_biomass_cues_kernel(
                 nc.scalar.activation(exp_b[b, 0][:, t, :], b_bank[b, t, 0][:], ACT.Exp)
                 nc.scalar.copy(b_copy[b, 0][:, t, :], b_bank[b, t, 0][:])
 
-        def difference(b, half, banks, into, steps=range(PACK)):
-            for t in steps:
+        def difference(b, half, banks, into):
+            for t in range(PACK):
                 bank = in_bank([P, HALF], "bank_a%d%d%d" % (b, t, half), banks[t])
                 wa_passes(bank, b, t, half, (0, 1), True)
                 nc.vector.tensor_tensor(into[:, t, :], bank[:], b_copy[b, half][:, t, :], ALU.add)
@@ -233,13 +243,12 @@ def tile_list_pen_biomass_cues_kernel(
         quantise_wa(1, 0)
         round_wa(0, 1)
         quantise_wa(0, 1)
-        clear_late(2, THIRD_CELLS)
         difference(0, 0, TURNING, placed([P, PACK, HALF], F32, "difference00", WA[0, 1]))
         round_wa(1, 1)
         quantise_wa(1, 1)
 
         wc_raw = placed([P, 2, N], I32, "wc_raw", WA[0, 0])
-        wgo_sb = placed([P, S], F32, "wgo_sb", WA[1, 0] + 2)
+        wgo_sb = placed([P, S], F32, "wgo_sb", WA[0, 0] + 4)
         wc_rows = placed([P, N], U8, "wc_rows", WA[1, 0])
         gain_sb = placed([P, 2, PACK], F32, "gain_sb", WA[1, 0] + 1)
         nc.vector.memset(wc_rows[:].bitcast(I32), 0)
@@ -254,8 +263,7 @@ def tile_list_pen_biomass_cues_kernel(
         difference(1, 0, HOLDING, b_copy[1, 0])
         b_copy[0, 1] = placed([P, PACK, HALF], F32, "b_copy01", TABLE[0])
         for t in range(PACK):
-            b_sum(0, t, 1, TURNING[t])
-            nc.scalar.copy(b_copy[0, 1][:, t, :], b_bank[0, t, 1][:])
+            b_sum(0, t, 1, LATE[t])
 
         wc_codes = held([P, 2, N], I32, "wc_codes")
         wc_plane = held([P, N], U8, "wc_plane")
@@ -267,50 +275,50 @@ def tile_list_pen_biomass_cues_kernel(
             wc_codes[:].rearrange("p b (t m) -> p b m t", t=PACK),
             wc_raw[:].rearrange("p b (m t) -> p b m t", t=PACK),
         )
-        clear_late(3, WA[0, 0])
 
-        h_grouped, h_operand, y_bank = {}, {}, {}
+        h_grouped, h_operand, y_bank, gained = {}, {}, {}, {}
+        gates = {c: placed([P, 2, PACK, CHUNK], F32, "gates%d" % c, GATES[c]) for c in range(2)}
+        late_gates = [placed([P, PACK, HALF], F32, "late_gates%d" % b, GATES[2 + b]) for b in range(2)]
 
         def columns(c):
-            first, count = CHUNKS[c]
-            return slice(first % HALF, first % HALF + count)
+            return slice(CHUNK * (c % 2), CHUNK * (c % 2 + 1))
 
         def sigmoid(out, in_):
             nc.scalar.activation(out, in_, ACT.Sigmoid, scale=-1.0)
 
-        def grouped(c):
-            h_grouped[c] = placed([P, 2, CHUNKS[c][1], PACK], BF16, "h_grouped%d" % c, STAIR + (-9, 0, 1.5, 5, 8)[c])
+        def scaled(out, in_, b, t):
+            nc.scalar.activation(out, in_, ACT.Copy, scale=gain_sb[:, b, t : t + 1])
 
-        def products(c):
-            grouped(c)
-            for b in range(2):
-                nc.gpsimd.tensor_tensor(
-                    h_grouped[c][:, b, :, :].rearrange("p (j e) t -> p j t e", e=2),
-                    gained[c][:, b, :, :].rearrange("p t (j e) -> p j t e", e=2),
-                    gates[c][:, b, :, :].rearrange("p t (j e) -> p j t e", e=2),
-                    ALU.mult,
-                )
+        def grouped(c):
+            h_grouped[c] = placed([P, 2, CHUNK, PACK], BF16, "h_grouped%d" % c, STAIR + 3 * c)
+
+        def product(c, b, rows, skip=0, count=CHUNK):
+            gate_rows = gates[c][:, b, :, :] if c < 2 else late_gates[b][:, :, columns(c)]
+            nc.gpsimd.tensor_tensor(
+                h_grouped[c][:, b, skip : skip + count, :].rearrange("p (j e) t -> p j t e", e=4),
+                rows.rearrange("p t (j e) -> p j t e", e=4),
+                gate_rows[:, :, skip : skip + count].rearrange("p t (j e) -> p j t e", e=4),
+                ALU.mult,
+            )
 
         def quantise_h(c):
-            count = CHUNKS[c][1]
-            codes = held([P, 2, count], U32, "h_codes%d" % c)
-            plane = held([P, 2, count], U8, "h_plane%d" % c)
-            nc.vector.quantize_mx(
-                out=codes[:].rearrange("p b j -> p (b j)").bitcast(FP8X4),
-                scales=plane[:].rearrange("p b j -> p (b j)"),
-                in_=h_grouped[c][:].rearrange("p b j t -> p (b j t)"),
-            )
+            codes = held([P, 2, CHUNK], U32, "h_codes%d" % c)
+            plane = held([P, 2, CHUNK], U8, "h_plane%d" % c)
+            for part in (slice(0, 1), slice(1, 2)) if c == 0 else (slice(0, 2),):
+                nc.vector.quantize_mx(
+                    out=codes[:, part, :].rearrange("p b j -> p (b j)").bitcast(FP8X4),
+                    scales=plane[:, part, :].rearrange("p b j -> p (b j)"),
+                    in_=h_grouped[c][:, part, :, :].rearrange("p b j t -> p (b j t)"),
+                )
             h_operand[c] = (codes, plane)
 
         def mix(c, banks):
-            count = CHUNKS[c][1]
-            per_bank = PACK // len(banks)
-            tiles = [in_bank([P, per_bank, count], "bank_y%d_%d" % (c, k), k) for k in banks]
+            tiles = [in_bank([P, 2, CHUNK], "bank_y%d_%d" % (c, k), k) for k in banks]
             for i in range(PACK):
-                y_bank[c, i] = tiles[i // per_bank]
+                y_bank[c, i] = tiles[i // 2]
                 for b in range(2):
                     nc.tensor.matmul_mx(
-                        out=tiles[i // per_bank][:, i % per_bank, :],
+                        out=tiles[i // 2][:, i % 2, :],
                         lhsT=wc_codes[:, b, P * i : P * (i + 1)].bitcast(FP8X4),
                         lhsT_scale=wc_plane[4 * b : P, P * i : P * (i + 1)],
                         rhs=h_operand[c][0][:, b, :].bitcast(FP8X4),
@@ -322,126 +330,119 @@ def tile_list_pen_biomass_cues_kernel(
         def entries(first, count):
             return offs2_sb[:, first // LIST : (first + count) // LIST]
 
-        def weigh_and_put(c, low, high, kib=None):
-            first, count = CHUNKS[c]
-            name = "weighted%d_%d" % (c, low)
+        def weigh_and_put(c, low, high, kib=None, skip=0, count=CHUNK):
+            name = "weighted%d_%d_%d" % (c, low, skip)
             shape = [P, high - low, count]
+            first = CHUNK * c + skip
             weighted = held(shape, F32, name) if kib is None else placed(shape, F32, name, kib)
-            within = low % y_bank[c, low].shape[1]
             nc.vector.tensor_tensor(
                 weighted[:],
-                y_bank[c, low][:, within : within + high - low, :],
+                y_bank[c, low][:, low % 2 : low % 2 + high - low, skip : skip + count],
                 wgo_sb[:, first : first + count].unsqueeze(1).to_broadcast(shape),
                 ALU.mult,
             )
             for i in range(low, high):
                 nc.vector.tensor_copy(cells[i][:].indirect(entries(first, count)), weighted[:, i - low, :])
 
-        first_count = CHUNKS[0][1]
-        gates = {c: placed([P, 2, PACK, CHUNKS[c][1]], F32, "gates%d" % c, GATES[c]) for c in range(5)}
-        gained = {}
+        early = placed([P, PACK, CHUNK], F32, "gained1_0", LAST_GROUPED)
+        for t in range(PACK):
+            nc.gpsimd.tensor_scalar(
+                out=early[:, t, :],
+                in0=exp_b[0, 0][:, t, columns(1)],
+                scalar1=gain_sb[:, 0, t : t + 1],
+                scalar2=0.0,
+                op0=ALU.mult,
+                op1=ALU.add,
+            )
+        gained[1, 0] = early[:]
+
         sigmoid(gates[0][:, 0, :, :], gate[0, 0][:, :, columns(0)])
-        for t in range(0, PACK, 2):
-            sigmoid(gates[0][:, 1, t : t + 2, :], gate[1, 0][:, t : t + 2, columns(0)])
+        for t in range(PACK):
+            sigmoid(gates[0][:, 1, t, :], gate[1, 0][:, t, columns(0)])
+        for t in range(PACK):
+            nc.scalar.copy(b_copy[0, 1][:, t, :], b_bank[0, t, 1][:])
         for b in range(2):
             sigmoid(gates[1][:, b, :, :], gate[b, 0][:, :, columns(1)])
+        second = placed([P, PACK, CHUNK], F32, "gained1_1", GATES[0] + 8)
+        for t in range(PACK):
+            scaled(second[:, t, :], exp_b[1, 0][:, t, columns(1)], 1, t)
+        gained[1, 1] = second[:]
+
         grouped(0)
+        rows = [placed([P, PACK, CHUNK], BF16, "h_rows%d" % b, FIRST_ROWS + 2 * b) for b in range(2)]
         for b in range(2):
-            rows = placed([P, PACK, first_count], BF16, "h_rows%d" % b, GAINED + 9 + b)
             for t in range(PACK):
                 nc.vector.scalar_tensor_tensor(
-                    out=rows[:, t, :],
+                    out=rows[b][:, t, :],
                     in0=exp_b[b, 0][:, t, columns(0)],
                     scalar=gain_sb[:, b, t : t + 1],
                     in1=gates[0][:, b, t, :],
                     op0=ALU.mult,
                     op1=ALU.mult,
                 )
+        for b in range(2):
             nc.vector.tensor_copy(
                 h_grouped[0][:, b, :, :].rearrange("p (j e) t -> p j t e", e=4),
-                rows[:].rearrange("p t (j e) -> p j t e", e=4),
+                rows[b][:].rearrange("p t (j e) -> p j t e", e=4),
             )
         quantise_h(0)
-        mix(0, (4,))
-
-        gained[1] = placed([P, 2, PACK, first_count], F32, "gained1", GAINED + 8)
+        difference(0, 1, LATE, placed([P, PACK, HALF], F32, "difference01", FIRST_GATE - 2))
+        mix(0, LATE[:2])
+        grouped(1)
         for b in range(2):
-            for t in range(PACK):
-                nc.vector.tensor_scalar(
-                    out=gained[1][:, b, t, :],
-                    in0=exp_b[b, 0][:, t, columns(1)],
-                    scalar1=gain_sb[:, b, t : t + 1],
-                    scalar2=None,
-                    op0=ALU.mult,
-                )
+            product(1, b, gained[1, b])
 
-        late_difference = placed([P, PACK, HALF], F32, "difference01", FIRST_GATE - 2)
-        difference(0, 1, TURNING, late_difference, range(PACK - 1))
-        gained[2] = placed([P, 2, PACK, CHUNKS[2][1]], F32, "gained2", GAINED)
-        for b in range(2):
-            sigmoid(gates[2][:, b, :, :], gate[b, 0][:, :, columns(2)])
-            for t in range(PACK):
-                nc.scalar.activation(
-                    gained[2][:, b, t, :], exp_b[b, 0][:, t, columns(2)], ACT.Copy, scale=gain_sb[:, b, t : t + 1]
-                )
-
-        products(1)
-        weigh_and_put(0, 0, 1)
-        quantise_h(1)
-        mix(1, (0,))
-        weigh_and_put(0, 1, 4, STAIR)
-        products(2)
-
-        for c in (3, 4):
-            sigmoid(gates[c][:, 0, : PACK - 1, :], late_difference[:, : PACK - 1, columns(c)])
         for t in range(PACK):
             bank = in_bank([P, HALF], "bank_sum%d" % t, SUMMING[t])
             wa_passes(bank, 1, t, 1, (1, 0), False)
             wb_passes(bank, 1, t, 1, False)
-            for c in (3, 4):
-                sigmoid(gates[c][:, 1, t, :], bank[:, columns(c)])
-        difference(0, 1, TURNING, late_difference, (PACK - 1,))
-        for c in (3, 4):
-            sigmoid(gates[c][:, 0, PACK - 1, :], late_difference[:, PACK - 1, columns(c)])
-
-        weigh_and_put(1, 0, 3)
-        quantise_h(2)
-        mix(2, (1, 2))
-        weigh_and_put(1, 3, 4, STAIR + 2)
-
+            sigmoid(late_gates[1][:, t, :], bank[:])
+        for t in range(0, PACK, 2):
+            sigmoid(late_gates[0][:, t : t + 2, :], gate[0, 1][:, t : t + 2, :])
         for t in range(PACK):
             b_sum(1, t, 1, SUMMING[t])
 
-        def late_products(c):
-            gained[c] = placed([P, 2, PACK, CHUNKS[c][1]], F32, "gained%d" % c, LATE_EXP + 8 * (c - 3))
-            for b in range(2):
-                if b == 0:
-                    nc.scalar.activation(gained[c][:, 0, :, :], b_copy[0, 1][:, :, columns(c)], ACT.Exp)
-                for t in range(PACK):
-                    row = gained[c][:, b, t, :]
-                    if b == 1:
-                        nc.scalar.activation(row, b_bank[1, t, 1][:, columns(c)], ACT.Exp)
-                    nc.scalar.activation(row, row, ACT.Copy, scale=gain_sb[:, b, t : t + 1])
-            products(c)
+        def late_product(c, b, rows, skip=0, count=CHUNK):
+            first = CHUNK * (c % 2) + skip
+            if b == 0:
+                nc.scalar.activation(rows, b_copy[0, 1][:, :, first : first + count], ACT.Exp)
+            for t in range(PACK):
+                if b == 1:
+                    nc.scalar.activation(rows[:, t, :], b_bank[1, t, 1][:, first : first + count], ACT.Exp)
+                scaled(rows[:, t, :], rows[:, t, :], b, t)
+            product(c, b, rows, skip, count)
 
-        late_products(3)
-        weigh_and_put(2, 0, 2)
-        weigh_and_put(2, 2, 3)
-        quantise_h(3)
-        mix(3, (4, 0))
-        weigh_and_put(2, 3, 4, STAIR + 6)
-        late_products(4)
-        weigh_and_put(3, 0, 2)
-        quantise_h(4)
-        mix(4, (1, 2))
-        weigh_and_put(3, 2, 3, STAIR + 9)
+        def late_products(c):
+            grouped(c)
+            if c == 2:
+                for k in range(2):
+                    rows = placed([P, PACK, CHUNK // 2], F32, "gained2_0%d" % k, LATE_EXP + 10 - 2 * k)
+                    late_product(c, 0, rows[:], k * CHUNK // 2, CHUNK // 2)
+                late_product(c, 1, placed([P, PACK, CHUNK], F32, "gained2_1", LATE_EXP + 12)[:])
+            else:
+                rows = placed([P, 2, PACK, CHUNK], F32, "gained3", LATE_EXP + 0.5)
+                for b in range(2):
+                    late_product(c, b, rows[:, b, :, :])
+
+        for c in range(3):
+            weigh_and_put(c, 0, 2)
+            if c < 2:
+                weigh_and_put(c, 2, 3, count=CHUNK // (c + 1))
+            quantise_h(c + 1)
+            mix(c + 1, (LATE[2:], LATE[:2])[c % 2])
+            if c == 1:
+                weigh_and_put(c, 2, 3, STAIR + 3 * c + 5, CHUNK // 2, CHUNK // 2)
+            held_back = 3 if c < 2 else 2
+            weigh_and_put(c, held_back, held_back + 1, STAIR + 3 * c + 4)
+            if c < 2:
+                late_products(c + 2)
 
         out_rows = out.rearrange("(p i) t -> i p t", i=PACK)
         for i in range(PACK):
-            first = CHUNKS[3 if i == PACK - 1 else 4][0]
+            first = CHUNK * (2 if i == PACK - 1 else 3)
             rows = held([P, S - first], F32, "last_y%d" % i)
             if i == PACK - 1:
-                nc.scalar.copy(rows[:, : CHUNKS[3][1]], y_bank[3, i][:, 1, :])
-            nc.scalar.copy(rows[:, CHUNKS[4][0] - first :], y_bank[4, i][:, i % 2, :])
+                nc.scalar.copy(rows[:, :CHUNK], y_bank[2, i][:, 1, :])
+            nc.scalar.copy(rows[:, S - CHUNK - first :], y_bank[3, i][:, i % 2, :])
             nc.vector.tensor_tensor(cells[i][:].indirect(entries(first, S - first)), rows[:], wgo_sb[:, first:], ALU.mult)
             nc.sync.dma_start(out_rows[i], cells[i][:])

@@ -295,9 +295,9 @@ def tile_list_pen_biomass_cues_kernel(
         def product(c, b, rows, skip=0, count=CHUNK):
             gate_rows = gates[c][:, b, :, :] if c < 2 else late_gates[b][:, :, columns(c)]
             nc.gpsimd.tensor_tensor(
-                h_grouped[c][:, b, skip : skip + count, :].rearrange("p (j e) t -> p j t e", e=4),
-                rows.rearrange("p t (j e) -> p j t e", e=4),
-                gate_rows[:, :, skip : skip + count].rearrange("p t (j e) -> p j t e", e=4),
+                h_grouped[c][:, b, skip : skip + count, :].rearrange("p (j e) t -> p j t e", e=2),
+                rows.rearrange("p t (j e) -> p j t e", e=2),
+                gate_rows[:, :, skip : skip + count].rearrange("p t (j e) -> p j t e", e=2),
                 ALU.mult,
             )
 
@@ -313,12 +313,13 @@ def tile_list_pen_biomass_cues_kernel(
             h_operand[c] = (codes, plane)
 
         def mix(c, banks):
-            tiles = [in_bank([P, 2, CHUNK], "bank_y%d_%d" % (c, k), k) for k in banks]
+            shared = PACK // len(banks)
+            tiles = [in_bank([P, shared, CHUNK], "bank_y%d_%d" % (c, k), k) for k in banks]
             for i in range(PACK):
-                y_bank[c, i] = tiles[i // 2]
+                y_bank[c, i] = tiles[i // shared]
                 for b in range(2):
                     nc.tensor.matmul_mx(
-                        out=tiles[i // 2][:, i % 2, :],
+                        out=tiles[i // shared][:, i % shared, :],
                         lhsT=wc_codes[:, b, P * i : P * (i + 1)].bitcast(FP8X4),
                         lhsT_scale=wc_plane[4 * b : P, P * i : P * (i + 1)],
                         rhs=h_operand[c][0][:, b, :].bitcast(FP8X4),
@@ -330,19 +331,18 @@ def tile_list_pen_biomass_cues_kernel(
         def entries(first, count):
             return offs2_sb[:, first // LIST : (first + count) // LIST]
 
-        def weigh_and_put(c, low, high, kib=None, skip=0, count=CHUNK):
-            name = "weighted%d_%d_%d" % (c, low, skip)
-            shape = [P, high - low, count]
-            first = CHUNK * c + skip
-            weighted = held(shape, F32, name) if kib is None else placed(shape, F32, name, kib)
-            nc.vector.tensor_tensor(
-                weighted[:],
-                y_bank[c, low][:, low % 2 : low % 2 + high - low, skip : skip + count],
-                wgo_sb[:, first : first + count].unsqueeze(1).to_broadcast(shape),
-                ALU.mult,
-            )
-            for i in range(low, high):
-                nc.vector.tensor_copy(cells[i][:].indirect(entries(first, count)), weighted[:, i - low, :])
+        def weigh_and_put(c, pieces):
+            weighted = []
+            for i, skip, count, kib in pieces:
+                name = "weighted%d_%d_%d" % (c, i, skip)
+                values = held([P, count], F32, name) if kib is None else placed([P, count], F32, name, kib)
+                first = CHUNK * c + skip
+                nc.vector.tensor_tensor(
+                    values[:], y_bank[c, i][:, i % 2, skip : skip + count], wgo_sb[:, first : first + count], ALU.mult
+                )
+                weighted.append((i, first, count, values))
+            for i, first, count, values in weighted:
+                nc.vector.tensor_copy(cells[i][:].indirect(entries(first, count)), values[:])
 
         early = placed([P, PACK, CHUNK], F32, "gained1_0", LAST_GROUPED)
         for t in range(PACK):
@@ -424,16 +424,14 @@ def tile_list_pen_biomass_cues_kernel(
                 for b in range(2):
                     late_product(c, b, rows[:, b, :, :])
 
+        part = CHUNK // 2
+        ahead = ([(2, 0, CHUNK, None)], [(2, 0, part, None)], [])
+        behind = ([(3, 0, part), (3, part, part)], [(2, part, part), (3, 0, CHUNK)], [(2, 0, part), (2, part, part)])
         for c in range(3):
-            weigh_and_put(c, 0, 2)
-            if c < 2:
-                weigh_and_put(c, 2, 3, count=CHUNK // (c + 1))
+            weigh_and_put(c, [(i, 0, CHUNK, None) for i in range(2)] + ahead[c])
             quantise_h(c + 1)
-            mix(c + 1, (LATE[2:], LATE[:2])[c % 2])
-            if c == 1:
-                weigh_and_put(c, 2, 3, STAIR + 3 * c + 5, CHUNK // 2, CHUNK // 2)
-            held_back = 3 if c < 2 else 2
-            weigh_and_put(c, held_back, held_back + 1, STAIR + 3 * c + 4)
+            mix(c + 1, (LATE[2:], LATE[:2], SUMMING)[c])
+            weigh_and_put(c, [piece + (STAIR + 3 * c + 4 + k / 2,) for k, piece in enumerate(behind[c])])
             if c < 2:
                 late_products(c + 2)
 
@@ -443,6 +441,6 @@ def tile_list_pen_biomass_cues_kernel(
             rows = held([P, S - first], F32, "last_y%d" % i)
             if i == PACK - 1:
                 nc.scalar.copy(rows[:, :CHUNK], y_bank[2, i][:, 1, :])
-            nc.scalar.copy(rows[:, S - CHUNK - first :], y_bank[3, i][:, i % 2, :])
+            nc.scalar.copy(rows[:, S - CHUNK - first :], y_bank[3, i][:, 0, :])
             nc.vector.tensor_tensor(cells[i][:].indirect(entries(first, S - first)), rows[:], wgo_sb[:, first:], ALU.mult)
             nc.sync.dma_start(out_rows[i], cells[i][:])

@@ -29,7 +29,8 @@ ON_GPSIMD = 80
 TABLE = (0, 8)
 WA = {(0, 0): 16, (1, 0): 26, (0, 1): 34, (1, 1): 116}
 LATE_WORDS = 50
-LATE_EXP, FIRST_GATE, STAIR, FIRST_EXP, LAST_GROUPED, FIRST_ROWS = 61, 70, 75, 84, 100, 140
+LATE_EXP, FIRST_GATE, STAIR, FIRST_EXP, LAST_GROUPED, FIRST_ROWS = 57.5, 70, 74.5, 84, 100, 140
+GROUPED = ((73, 78), (76.5, 79), (74.5, 84), (83, 85))
 GATES = (104, 132, 116, 144)
 TURNING, HOLDING, SUMMING = (0, 1, 2, 3), (4, 5, 6, 7), (0, 1, 2, 3)
 LATE = (4, 5, 6, 7)
@@ -290,25 +291,28 @@ def tile_list_pen_biomass_cues_kernel(
             nc.scalar.activation(out, in_, ACT.Copy, scale=gain_sb[:, b, t : t + 1])
 
         def grouped(c):
-            h_grouped[c] = placed([P, 2, CHUNK, PACK], BF16, "h_grouped%d" % c, STAIR + 3 * c)
+            for b in range(2):
+                h_grouped[c, b] = placed([P, CHUNK, PACK], BF16, "h_grouped%d_%d" % (c, b), GROUPED[c][b])
 
         def product(c, b, rows, skip=0, count=CHUNK):
             gate_rows = gates[c][:, b, :, :] if c < 2 else late_gates[b][:, :, columns(c)]
             nc.gpsimd.tensor_tensor(
-                h_grouped[c][:, b, skip : skip + count, :].rearrange("p (j e) t -> p j t e", e=2),
+                h_grouped[c, b][:, skip : skip + count, :].rearrange("p (j e) t -> p j t e", e=2),
                 rows.rearrange("p t (j e) -> p j t e", e=2),
                 gate_rows[:, :, skip : skip + count].rearrange("p t (j e) -> p j t e", e=2),
                 ALU.mult,
             )
 
         def quantise_h(c):
-            codes = held([P, 2, CHUNK], U32, "h_codes%d" % c)
+            name = "h_codes%d_0" % c
+            lower = placed([P, CHUNK], U32, name, (GATES[0] + 8, LATE_EXP + 9.75, LATE_EXP)[c - 1]) if c else held([P, CHUNK], U32, name)
+            codes = (lower, held([P, CHUNK], U32, "h_codes%d_1" % c))
             plane = held([P, 2, CHUNK], U8, "h_plane%d" % c)
-            for part in (slice(0, 1), slice(1, 2)) if c == 0 else (slice(0, 2),):
+            for b in range(2):
                 nc.vector.quantize_mx(
-                    out=codes[:, part, :].rearrange("p b j -> p (b j)").bitcast(FP8X4),
-                    scales=plane[:, part, :].rearrange("p b j -> p (b j)"),
-                    in_=h_grouped[c][:, part, :, :].rearrange("p b j t -> p (b j t)"),
+                    out=codes[b][:].bitcast(FP8X4),
+                    scales=plane[:, b, :],
+                    in_=h_grouped[c, b][:].rearrange("p j t -> p (j t)"),
                 )
             h_operand[c] = (codes, plane)
 
@@ -322,7 +326,7 @@ def tile_list_pen_biomass_cues_kernel(
                         out=tiles[i // shared][:, i % shared, :],
                         lhsT=wc_codes[:, b, P * i : P * (i + 1)].bitcast(FP8X4),
                         lhsT_scale=wc_plane[4 * b : P, P * i : P * (i + 1)],
-                        rhs=h_operand[c][0][:, b, :].bitcast(FP8X4),
+                        rhs=h_operand[c][0][b][:].bitcast(FP8X4),
                         rhs_scale=h_operand[c][1][:, b, :],
                         start=(b == 0),
                         stop=(b == 1),
@@ -382,11 +386,11 @@ def tile_list_pen_biomass_cues_kernel(
                 )
         for b in range(2):
             nc.vector.tensor_copy(
-                h_grouped[0][:, b, :, :].rearrange("p (j e) t -> p j t e", e=4),
+                h_grouped[0, b][:].rearrange("p (j e) t -> p j t e", e=4),
                 rows[b][:].rearrange("p t (j e) -> p j t e", e=4),
             )
         quantise_h(0)
-        difference(0, 1, LATE, placed([P, PACK, HALF], F32, "difference01", FIRST_GATE - 2))
+        difference(0, 1, LATE, placed([P, PACK, HALF], F32, "difference01", FIRST_GATE - 3))
         mix(0, LATE[:2])
         grouped(1)
         for b in range(2):
@@ -412,28 +416,49 @@ def tile_list_pen_biomass_cues_kernel(
                 scaled(rows[:, t, :], rows[:, t, :], b, t)
             product(c, b, rows, skip, count)
 
-        def late_products(c):
-            grouped(c)
-            if c == 2:
-                for k in range(2):
-                    rows = placed([P, PACK, CHUNK // 2], F32, "gained2_0%d" % k, LATE_EXP + 10 - 2 * k)
-                    late_product(c, 0, rows[:], k * CHUNK // 2, CHUNK // 2)
-                late_product(c, 1, placed([P, PACK, CHUNK], F32, "gained2_1", LATE_EXP + 12)[:])
-            else:
-                rows = placed([P, 2, PACK, CHUNK], F32, "gained3", LATE_EXP + 0.5)
-                for b in range(2):
-                    late_product(c, b, rows[:, b, :, :])
-
         part = CHUNK // 2
-        ahead = ([(2, 0, CHUNK, None)], [(2, 0, part, None)], [])
-        behind = ([(3, 0, part), (3, part, part)], [(2, part, part), (3, 0, CHUNK)], [(2, 0, part), (2, part, part)])
-        for c in range(3):
-            weigh_and_put(c, [(i, 0, CHUNK, None) for i in range(2)] + ahead[c])
-            quantise_h(c + 1)
-            mix(c + 1, (LATE[2:], LATE[:2], SUMMING)[c])
-            weigh_and_put(c, [piece + (STAIR + 3 * c + 4 + k / 2,) for k, piece in enumerate(behind[c])])
-            if c < 2:
-                late_products(c + 2)
+        weigh_and_put(0, [(i, 0, CHUNK, None) for i in range(3)])
+        quantise_h(1)
+        mix(1, LATE[2:])
+        plain = [placed([P, 2, part], F32, "plain2_%d" % k, STAIR - 1.5 + k) for k in range(2)]
+        for k in range(2):
+            nc.scalar.activation(plain[k][:], b_copy[0, 1][:, 2 * k : 2 * k + 2, :part], ACT.Exp)
+        rows = placed([P, PACK, part], BF16, "h_rows2", STAIR + 2.5)
+        for t in range(PACK):
+            nc.vector.scalar_tensor_tensor(
+                out=rows[:, t, :],
+                in0=plain[t // 2][:, t % 2, :],
+                scalar=gain_sb[:, 0, t : t + 1],
+                in1=late_gates[0][:, t, :part],
+                op0=ALU.mult,
+                op1=ALU.mult,
+            )
+        weigh_and_put(0, [(3, part * k, part, STAIR - 1.25 + k / 2) for k in range(2)])
+        grouped(2)
+        late_product(2, 0, placed([P, PACK, part], F32, "gained2_0", LATE_EXP + 7.75)[:], part, part)
+        late_product(2, 1, placed([P, PACK, CHUNK], F32, "gained2_1", LATE_EXP + 9.75)[:])
+        nc.scalar.copy(
+            h_grouped[2, 0][:, :part, :].rearrange("p (j e) t -> p j t e", e=4),
+            rows[:].rearrange("p t (j e) -> p j t e", e=4),
+        )
+
+        pair = placed([P, 2, CHUNK], F32, "weighted1", STAIR - 3.25)
+        for i in range(2):
+            nc.vector.tensor_tensor(pair[:, i, :], y_bank[1, i][:, i, :], wgo_sb[:, CHUNK : 2 * CHUNK], ALU.mult)
+        for i in range(2):
+            nc.vector.tensor_copy(cells[i][:].indirect(entries(CHUNK, CHUNK)), pair[:, i, :])
+        quantise_h(2)
+        mix(2, LATE[:2])
+        weigh_and_put(1, [(i, 0, CHUNK, STAIR - 2 + i) for i in (2, 3)])
+        grouped(3)
+        last = placed([P, 2, PACK, CHUNK], F32, "gained3", LATE_EXP)
+        for b in range(2):
+            late_product(3, b, last[:, b, :, :])
+
+        weigh_and_put(2, [(i, 0, CHUNK, None) for i in range(2)])
+        quantise_h(3)
+        mix(3, SUMMING)
+        weigh_and_put(2, [(2, part * k, part, GROUPED[3][0] + k / 2) for k in range(2)])
 
         out_rows = out.rearrange("(p i) t -> i p t", i=PACK)
         for i in range(PACK):

from contextlib import ExitStack

import concourse.mybir as mybir

K, T, S, H, N, T2 = 1024, 2048, 1024, 1024, 512, 2048
FLOPS = 2 * (2 * K * H * S + H * N * S)

F32 = mybir.dt.float32
BF16 = mybir.dt.bfloat16
I32 = mybir.dt.int32
U32 = mybir.dt.uint32
U16 = mybir.dt.uint16
U8 = mybir.dt.uint8
FP8X4 = mybir.dt.float8_e4m3fn_x4
FP4X4 = mybir.dt.float4_e2m1fn_x4
ALU = mybir.AluOpType
ACT = mybir.ActivationFunctionType

P = 128
PACK = 4
PASS = P * PACK
HALF = 512
CHUNK = 256
LIST = 16
BANK = 2048
KIB = 1024
ON_GPSIMD = 80

TABLE = (0, 8)
WA = {(0, 0): 16, (1, 0): 26, (0, 1): 34, (1, 1): 116}
LATE_WORDS = 50
LATE_EXP, FIRST_GATE, STAIR, FIRST_EXP, LAST_GROUPED, FIRST_ROWS = 57.5, 70, 74.5, 84, 100, 140
GROUPED = ((73, 78), (76.5, 79), (74.5, 84), (83, 85))
GATES = (104, 132, 116, 144)
TURNING, HOLDING, SUMMING = (0, 1, 2, 3), (4, 5, 6, 7), (0, 1, 2, 3)
LATE = (4, 5, 6, 7)


def tile_list_pen_biomass_cues_kernel(
    tc, tab_words, tab_scales, offs, wa, wb_words, wb_scales, gain, wc_words, wc_scales, offs2, wgo, out
):
    nc = tc.nc
    with ExitStack() as ctx:
        lists = ctx.enter_context(tc.tile_pool(name="lists", bufs=1))
        keep = ctx.enter_context(tc.tile_pool(name="keep", bufs=1))
        reused = ctx.enter_context(tc.tile_pool(name="reused", bufs=1))
        psum = ctx.enter_context(tc.psum_pool(name="psum", bufs=1))

        def held(shape, dtype, name):
            return keep.tile(shape, dtype, name=name, align_bytes=64)

        def placed(shape, dtype, name, kib):
            return reused.tile(shape, dtype, name=name, align_bytes=64, offset=int(KIB * kib))

        def in_bank(shape, name, bank):
            return psum.tile(shape, F32, name=name, offset=BANK * bank)

        offs_sb = lists.tile([P, S // LIST], U16, name="offs_sb")
        offs2_sb = lists.tile([P, S // LIST], U16, name="offs2_sb")
        nc.sync.dma_start(offs_sb[:], offs)
        nc.sync.dma_start(offs2_sb[:], offs2)

        tab_rows = placed([P, T], U8, "tab_rows", WA[0, 0] + 7)
        for j in range(4):
            nc.sync.dma_start(tab_rows[j:P:4, :].bitcast(I32), tab_scales.rearrange("a q t -> q a t").bitcast(I32))

        wb_rows = placed([P, 2, H], U8, "wb_rows", WA[1, 1] + 7)
        tab_plane = held([P, 2, S], U8, "tab_plane")
        nc.gpsimd.memset(wb_rows[:].rearrange("p a c -> p (a c)").bitcast(I32), 0)

        tab_win, wb_raw, wa_raw = {}, {}, {}

        def load_table(a):
            tab_win[a] = placed([P, T], I32, "tab_win%d" % a, TABLE[a])
            nc.sync.dma_start(tab_win[a][:], tab_words[a].rearrange("p t i -> p (t i)").bitcast(I32))

        def load_wb(b, kib):
            wb_raw[b] = placed([P, 2, 2 * PASS], U8, "wb_raw%d" % b, kib)
            nc.sync.dma_start(
                wb_raw[b][:].bitcast(I32),
                wb_words[:, :, 2 * PASS * b : 2 * PASS * (b + 1)].rearrange("a p c -> p a c").bitcast(I32),
            )

        def load_wa(a, b):
            wa_raw[a, b] = placed([P, PACK, HALF], F32, "wa_raw%d%d" % (a, b), WA[a, b])
            nc.sync.dma_start(
                wa_raw[a, b][:],
                wa[PASS * a : PASS * (a + 1), PASS * b : PASS * (b + 1)].rearrange("(p i) c -> p i c", i=PACK),
            )

        load_table(1)
        for d in range(4):
            nc.sync.dma_start(
                wb_rows[32 * d : 32 * d + 4, :, :].bitcast(I32),
                wb_scales[:, 4 * d : 4 * d + 4, :].rearrange("a q c -> q a c").bitcast(I32),
            )
        load_wb(0, WA[0, 1] - 1)
        load_table(0)

        def clear_alone(words):
            middle = words.shape[1] // 2 - 1
            nc.vector.memset(words[:, :middle], 0)
            nc.vector.memset(words[:, middle:], 0)

        clear_alone(tab_plane[:].rearrange("p a s -> p (a s)").bitcast(I32))
        cells = {i: held([P, T2], F32, "cells%d" % i) for i in (0, 2)}
        cells[3] = placed([P, T2], F32, "cells3", 42)
        clear_alone(cells[0][:].bitcast(I32))
        for i in (2, 3):
            nc.gpsimd.memset(cells[i][:].bitcast(I32), 0)

        picked_rows = placed([P, S], U8, "picked_rows", LATE_WORDS + 1.5)
        nc.vector.tensor_copy(picked_rows[:], tab_rows[:].indirect(offs_sb[:]))
        for d in range(4):
            nc.sync.dma_start(
                tab_plane[32 * d : 32 * d + 4, :, :].bitcast(I32),
                picked_rows[32 * d : 32 * (d + 1) : 4, :].bitcast(I32),
            )
        load_wb(1, WA[0, 0] + 8)
        load_wa(0, 0)

        picked = {}

        def gather_words(a, half):
            name = "picked%d%d" % (a, half)
            if half == 0:
                picked[a, half] = held([P, HALF], U32, name)
            else:
                picked[a, half] = placed([P, HALF], U32, name, LATE_WORDS + 2 * a)
            entries = offs_sb[:, HALF * half // LIST : HALF * (half + 1) // LIST]
            nc.vector.tensor_copy(picked[a, half][:], tab_win[a][:].bitcast(U32).indirect(entries))

        wb_codes = [held([P, 2, 2 * PASS], U8, "wb_codes%d" % b) for b in range(2)]
        wb_plane = [held([P, 2, PASS], U8, "wb_plane%d" % b) for b in range(2)]

        def deal_wb(b):
            nc.scalar.copy(
                wb_codes[b][:].bitcast(U16).rearrange("p a (t m) -> p a m t", t=PACK),
                wb_raw[b][:].bitcast(U16).rearrange("p a (m t) -> p a m t", t=PACK),
            )
            nc.vector.tensor_copy(
                wb_plane[b][:].rearrange("p a (t m) -> p a m t", t=PACK),
                wb_rows[:, :, PASS * b : PASS * (b + 1)].rearrange("p a (m t) -> p a m t", t=PACK),
            )

        gather_words(1, 0)
        deal_wb(0)
        gather_words(0, 0)
        deal_wb(1)
        cells[1] = placed([P, T2], F32, "cells1", WA[1, 1] + 8)
        nc.gpsimd.memset(cells[1][:].bitcast(I32), 0)
        gather_words(1, 1)
        gather_words(0, 1)
        load_wa(1, 0)
        load_wa(0, 1)
        load_wa(1, 1)

        def table_operand(a, half):
            return dict(
                rhs=picked[a, half][:].bitcast(FP8X4), rhs_scale=tab_plane[:, a, HALF * half : HALF * (half + 1)]
            )

        def wb_passes(bank, b, t, half, start):
            for a in range(2):
                nc.tensor.matmul_mx(
                    out=bank[:],
                    lhsT=wb_codes[b][:, a, 2 * P * t : 2 * P * (t + 1)].bitcast(FP4X4),
                    lhsT_scale=wb_plane[b][:, a, P * t : P * (t + 1)],
                    start=(start and a == 0),
                    stop=(a == 1),
                    **table_operand(a, half),
                )

        wa_grouped, wa_codes, wa_plane = {}, {}, {}

        def wa_passes(bank, b, t, half, order, stop):
            for a in order:
                nc.tensor.matmul_mx(
                    out=bank[:],
                    lhsT=wa_codes[a, b][:, P * t : P * (t + 1)].bitcast(FP8X4),
                    lhsT_scale=wa_plane[a, b][:, P * t : P * (t + 1)],
                    start=(a == order[0]),
                    stop=(stop and a == order[1]),
                    **table_operand(a, half),
                )

        def round_wa(a, b):
            name = "wa_grouped%d%d" % (a, b)
            if b == 0:
                wa_grouped[a, b] = held([P, PACK, P, PACK], BF16, name)
            else:
                wa_grouped[a, b] = placed([P, PACK, P, PACK], BF16, name, LAST_GROUPED)
            shares = [(nc.vector, "p m i t", 0, P)]
            if (a, b) == (1, 1):
                shares = [(nc.gpsimd, "p m t i", 0, ON_GPSIMD), (nc.vector, "p m i t", ON_GPSIMD, P)]
            for engine, walk, first, last in shares:
                engine.tensor_scalar(
                    out=wa_grouped[a, b][:].rearrange("p t m i -> " + walk)[:, first:last],
                    in0=wa_raw[a, b][:].rearrange("p i (m t) -> " + walk, t=PACK)[:, first:last],
                    scalar1=-1.0,
                    scalar2=0.0,
                    op0=ALU.mult,
                    op1=ALU.add,
                )

        def quantise_wa(a, b):
            wa_codes[a, b] = held([P, HALF], U32, "wa_codes%d%d" % (a, b))
            wa_plane[a, b] = held([P, HALF], U8, "wa_plane%d%d" % (a, b))
            nc.vector.quantize_mx(
                out=wa_codes[a, b][:].bitcast(FP8X4),
                scales=wa_plane[a, b][:],
                in_=wa_grouped[a, b][:].rearrange("p t m i -> p (t m i)"),
            )

        exp_b = {(b, 0): placed([P, PACK, HALF], F32, "exp_b%d0" % b, FIRST_EXP + 8 * b) for b in range(2)}
        b_copy = {
            (0, 0): placed([P, PACK, HALF], F32, "b_copy00", FIRST_GATE),
            (1, 0): placed([P, PACK, HALF], F32, "b_copy10", TABLE[1]),
        }
        b_bank, gate = {}, {}

        def b_sum(b, t, half, bank):
            b_bank[b, t, half] = in_bank([P, HALF], "bank_b%d%d%d" % (b, t, half), bank)
            wb_passes(b_bank[b, t, half], b, t, half, True)

        def first_phase(b, banks):
            for t in range(PACK):
                b_sum(b, t, 0, banks[t])
                nc.scalar.activation(exp_b[b, 0][:, t, :], b_bank[b, t, 0][:], ACT.Exp)
                nc.scalar.copy(b_copy[b, 0][:, t, :], b_bank[b, t, 0][:])

        def difference(b, half, banks, into):
            for t in range(PACK):
                bank = in_bank([P, HALF], "bank_a%d%d%d" % (b, t, half), banks[t])
                wa_passes(bank, b, t, half, (0, 1), True)
                nc.vector.tensor_tensor(into[:, t, :], bank[:], b_copy[b, half][:, t, :], ALU.add)
            gate[b, half] = into

        first_phase(0, TURNING)
        first_phase(1, HOLDING)
        round_wa(0, 0)
        round_wa(1, 0)
        quantise_wa(0, 0)
        quantise_wa(1, 0)
        round_wa(0, 1)
        quantise_wa(0, 1)
        difference(0, 0, TURNING, placed([P, PACK, HALF], F32, "difference00", WA[0, 1]))
        round_wa(1, 1)
        quantise_wa(1, 1)

        wc_raw = placed([P, 2, N], I32, "wc_raw", WA[0, 0])
        wgo_sb = placed([P, S], F32, "wgo_sb", WA[0, 0] + 4)
        wc_rows = placed([P, N], U8, "wc_rows", WA[1, 0])
        gain_sb = placed([P, 2, PACK], F32, "gain_sb", WA[1, 0] + 1)
        nc.vector.memset(wc_rows[:].bitcast(I32), 0)
        nc.sync.dma_start(wc_raw[:], wc_words.rearrange("a p c i -> p a (c i)").bitcast(I32))
        nc.sync.dma_start(gain_sb[:], gain.rearrange("(b p t) -> p b t", b=2, t=PACK))
        for d in range(4):
            nc.sync.dma_start(
                wc_rows[32 * d : 32 * d + 8, :].bitcast(I32), wc_scales[:, 4 * d : 4 * d + 4, :].bitcast(I32)
            )
        nc.sync.dma_start(wgo_sb[:], wgo)

        difference(1, 0, HOLDING, b_copy[1, 0])
        b_copy[0, 1] = placed([P, PACK, HALF], F32, "b_copy01", TABLE[0])
        for t in range(PACK):
            b_sum(0, t, 1, LATE[t])

        wc_codes = held([P, 2, N], I32, "wc_codes")
        wc_plane = held([P, N], U8, "wc_plane")
        nc.vector.tensor_copy(
            wc_plane[:].rearrange("p (t m) -> p m t", t=PACK),
            wc_rows[:].rearrange("p (m t) -> p m t", t=PACK),
        )
        nc.vector.tensor_copy(
            wc_codes[:].rearrange("p b (t m) -> p b m t", t=PACK),
            wc_raw[:].rearrange("p b (m t) -> p b m t", t=PACK),
        )

        h_grouped, h_operand, y_bank, gained = {}, {}, {}, {}
        gates = {c: placed([P, 2, PACK, CHUNK], F32, "gates%d" % c, GATES[c]) for c in range(2)}
        late_gates = [placed([P, PACK, HALF], F32, "late_gates%d" % b, GATES[2 + b]) for b in range(2)]

        def columns(c):
            return slice(CHUNK * (c % 2), CHUNK * (c % 2 + 1))

        def sigmoid(out, in_):
            nc.scalar.activation(out, in_, ACT.Sigmoid, scale=-1.0)

        def scaled(out, in_, b, t):
            nc.scalar.activation(out, in_, ACT.Copy, scale=gain_sb[:, b, t : t + 1])

        def grouped(c):
            for b in range(2):
                h_grouped[c, b] = placed([P, CHUNK, PACK], BF16, "h_grouped%d_%d" % (c, b), GROUPED[c][b])

        def product(c, b, rows, skip=0, count=CHUNK):
            gate_rows = gates[c][:, b, :, :] if c < 2 else late_gates[b][:, :, columns(c)]
            nc.gpsimd.tensor_tensor(
                h_grouped[c, b][:, skip : skip + count, :].rearrange("p (j e) t -> p j t e", e=2),
                rows.rearrange("p t (j e) -> p j t e", e=2),
                gate_rows[:, :, skip : skip + count].rearrange("p t (j e) -> p j t e", e=2),
                ALU.mult,
            )

        def quantise_h(c):
            name = "h_codes%d_0" % c
            lower = placed([P, CHUNK], U32, name, (GATES[0] + 8, LATE_EXP + 9.75, LATE_EXP)[c - 1]) if c else held([P, CHUNK], U32, name)
            codes = (lower, held([P, CHUNK], U32, "h_codes%d_1" % c))
            plane = held([P, 2, CHUNK], U8, "h_plane%d" % c)
            for b in range(2):
                nc.vector.quantize_mx(
                    out=codes[b][:].bitcast(FP8X4),
                    scales=plane[:, b, :],
                    in_=h_grouped[c, b][:].rearrange("p j t -> p (j t)"),
                )
            h_operand[c] = (codes, plane)

        def mix(c, banks):
            shared = PACK // len(banks)
            tiles = [in_bank([P, shared, CHUNK], "bank_y%d_%d" % (c, k), k) for k in banks]
            for i in range(PACK):
                y_bank[c, i] = tiles[i // shared]
                for b in range(2):
                    nc.tensor.matmul_mx(
                        out=tiles[i // shared][:, i % shared, :],
                        lhsT=wc_codes[:, b, P * i : P * (i + 1)].bitcast(FP8X4),
                        lhsT_scale=wc_plane[4 * b : P, P * i : P * (i + 1)],
                        rhs=h_operand[c][0][b][:].bitcast(FP8X4),
                        rhs_scale=h_operand[c][1][:, b, :],
                        start=(b == 0),
                        stop=(b == 1),
                    )

        def entries(first, count):
            return offs2_sb[:, first // LIST : (first + count) // LIST]

        def weigh_and_put(c, pieces):
            weighted = []
            for i, skip, count, kib in pieces:
                name = "weighted%d_%d_%d" % (c, i, skip)
                values = held([P, count], F32, name) if kib is None else placed([P, count], F32, name, kib)
                first = CHUNK * c + skip
                nc.vector.tensor_tensor(
                    values[:], y_bank[c, i][:, i % 2, skip : skip + count], wgo_sb[:, first : first + count], ALU.mult
                )
                weighted.append((i, first, count, values))
            for i, first, count, values in weighted:
                nc.vector.tensor_copy(cells[i][:].indirect(entries(first, count)), values[:])

        early = placed([P, PACK, CHUNK], F32, "gained1_0", LAST_GROUPED)
        for t in range(PACK):
            nc.gpsimd.tensor_scalar(
                out=early[:, t, :],
                in0=exp_b[0, 0][:, t, columns(1)],
                scalar1=gain_sb[:, 0, t : t + 1],
                scalar2=0.0,
                op0=ALU.mult,
                op1=ALU.add,
            )
        gained[1, 0] = early[:]

        sigmoid(gates[0][:, 0, :, :], gate[0, 0][:, :, columns(0)])
        for t in range(PACK):
            sigmoid(gates[0][:, 1, t, :], gate[1, 0][:, t, columns(0)])
        for t in range(PACK):
            nc.scalar.copy(b_copy[0, 1][:, t, :], b_bank[0, t, 1][:])
        for b in range(2):
            sigmoid(gates[1][:, b, :, :], gate[b, 0][:, :, columns(1)])
        second = placed([P, PACK, CHUNK], F32, "gained1_1", GATES[0] + 8)
        for t in range(PACK):
            scaled(second[:, t, :], exp_b[1, 0][:, t, columns(1)], 1, t)
        gained[1, 1] = second[:]

        grouped(0)
        rows = [placed([P, PACK, CHUNK], BF16, "h_rows%d" % b, FIRST_ROWS + 2 * b) for b in range(2)]
        for b in range(2):
            for t in range(PACK):
                nc.vector.scalar_tensor_tensor(
                    out=rows[b][:, t, :],
                    in0=exp_b[b, 0][:, t, columns(0)],
                    scalar=gain_sb[:, b, t : t + 1],
                    in1=gates[0][:, b, t, :],
                    op0=ALU.mult,
                    op1=ALU.mult,
                )
        for b in range(2):
            nc.vector.tensor_copy(
                h_grouped[0, b][:].rearrange("p (j e) t -> p j t e", e=4),
                rows[b][:].rearrange("p t (j e) -> p j t e", e=4),
            )
        quantise_h(0)
        difference(0, 1, LATE, placed([P, PACK, HALF], F32, "difference01", FIRST_GATE - 3))
        mix(0, LATE[:2])
        grouped(1)
        for b in range(2):
            product(1, b, gained[1, b])

        for t in range(PACK):
            bank = in_bank([P, HALF], "bank_sum%d" % t, SUMMING[t])
            wa_passes(bank, 1, t, 1, (1, 0), False)
            wb_passes(bank, 1, t, 1, False)
            sigmoid(late_gates[1][:, t, :], bank[:])
        for t in range(0, PACK, 2):
            sigmoid(late_gates[0][:, t : t + 2, :], gate[0, 1][:, t : t + 2, :])
        for t in range(PACK):
            b_sum(1, t, 1, SUMMING[t])

        def late_product(c, b, rows, skip=0, count=CHUNK):
            first = CHUNK * (c % 2) + skip
            if b == 0:
                nc.scalar.activation(rows, b_copy[0, 1][:, :, first : first + count], ACT.Exp)
            for t in range(PACK):
                if b == 1:
                    nc.scalar.activation(rows[:, t, :], b_bank[1, t, 1][:, first : first + count], ACT.Exp)
                scaled(rows[:, t, :], rows[:, t, :], b, t)
            product(c, b, rows, skip, count)

        part = CHUNK // 2
        weigh_and_put(0, [(i, 0, CHUNK, None) for i in range(3)])
        quantise_h(1)
        mix(1, LATE[2:])
        plain = [placed([P, 2, part], F32, "plain2_%d" % k, STAIR - 1.5 + k) for k in range(2)]
        for k in range(2):
            nc.scalar.activation(plain[k][:], b_copy[0, 1][:, 2 * k : 2 * k + 2, :part], ACT.Exp)
        rows = placed([P, PACK, part], BF16, "h_rows2", STAIR + 2.5)
        for t in range(PACK):
            nc.vector.scalar_tensor_tensor(
                out=rows[:, t, :],
                in0=plain[t // 2][:, t % 2, :],
                scalar=gain_sb[:, 0, t : t + 1],
                in1=late_gates[0][:, t, :part],
                op0=ALU.mult,
                op1=ALU.mult,
            )
        weigh_and_put(0, [(3, part * k, part, STAIR - 1.25 + k / 2) for k in range(2)])
        grouped(2)
        late_product(2, 0, placed([P, PACK, part], F32, "gained2_0", LATE_EXP + 7.75)[:], part, part)
        late_product(2, 1, placed([P, PACK, CHUNK], F32, "gained2_1", LATE_EXP + 9.75)[:])
        nc.scalar.copy(
            h_grouped[2, 0][:, :part, :].rearrange("p (j e) t -> p j t e", e=4),
            rows[:].rearrange("p t (j e) -> p j t e", e=4),
        )

        pair = placed([P, 2, CHUNK], F32, "weighted1", STAIR - 3.25)
        for i in range(2):
            nc.vector.tensor_tensor(pair[:, i, :], y_bank[1, i][:, i, :], wgo_sb[:, CHUNK : 2 * CHUNK], ALU.mult)
        for i in range(2):
            nc.vector.tensor_copy(cells[i][:].indirect(entries(CHUNK, CHUNK)), pair[:, i, :])
        quantise_h(2)
        mix(2, LATE[:2])
        weigh_and_put(1, [(i, 0, CHUNK, STAIR - 2 + i) for i in (2, 3)])
        grouped(3)
        last = placed([P, 2, PACK, CHUNK], F32, "gained3", LATE_EXP)
        for b in range(2):
            late_product(3, b, last[:, b, :, :])

        weigh_and_put(2, [(i, 0, CHUNK, None) for i in range(2)])
        quantise_h(3)
        mix(3, SUMMING)
        weigh_and_put(2, [(2, part * k, part, GROUPED[3][0] + k / 2) for k in range(2)])

        out_rows = out.rearrange("(p i) t -> i p t", i=PACK)
        for i in range(PACK):
            first = CHUNK * (2 if i == PACK - 1 else 3)
            rows = held([P, S - first], F32, "last_y%d" % i)
            if i == PACK - 1:
                nc.scalar.copy(rows[:, :CHUNK], y_bank[2, i][:, 1, :])
            nc.scalar.copy(rows[:, S - CHUNK - first :], y_bank[3, i][:, 0, :])
            nc.vector.tensor_tensor(cells[i][:].indirect(entries(first, S - first)), rows[:], wgo_sb[:, first:], ALU.mult)
            nc.sync.dma_start(out_rows[i], cells[i][:])
